import numpy as np
import ml_dtypes


def mxq(x, axis, fmt="e4m3"):
    dtype, down = {"e4m3": (ml_dtypes.float8_e4m3fn, 7), "e5m2": (ml_dtypes.float8_e5m2, 14)}[fmt]
    v = np.moveaxis(np.asarray(x, np.float32).astype(ml_dtypes.bfloat16).astype(np.float64), axis, -1)
    blocks = v.reshape(v.shape[:-1] + (-1, 32))
    amax = np.abs(blocks).max(-1, keepdims=True)
    byte = np.maximum(np.where(amax > 0, np.frexp(amax)[1] - 1 + 127, 0) - down, 1)
    scale = np.exp2(byte - 127.0)
    codes = (blocks / scale).astype(np.float32).astype(dtype).astype(np.float64)
    return np.moveaxis((codes * scale).reshape(v.shape), -1, axis)


WIDE = False


def mx_kscale(k):
    if not WIDE:
        return np.ones(k)
    levels = np.array([10, -10, 5, -5, 0])
    if k % 512:
        return np.exp2(np.random.permutation(np.resize(levels, k // 32))).repeat(32)
    a = np.empty((k // 512, 16))
    for p in range(k // 512):
        a[p, :8] = np.random.permutation(np.resize(levels, 8))
        for g in range(8):
            far = levels[np.abs(levels - a[p, g]) >= 10]
            a[p, g + 8] = far[np.random.randint(len(far))]
    return np.exp2(a.ravel()).repeat(32)


def f64(x):
    return np.asarray(x).astype(np.float64)


def striped(idx):
    return np.tile(idx.reshape(-1, 16).T, (8, 1)).astype(np.uint16)


def unstriped(offs):
    return offs[:16].T.reshape(-1).astype(np.int64)


E2M1 = np.array([0.0, 0.5, 1.0, 1.5, 2.0, 3.0, 4.0, 6.0, -0.0, -0.5, -1.0, -1.5, -2.0, -3.0, -4.0, -6.0])


def pack_weight(w, fmt):
    k, n = w.shape
    w = f64(np.asarray(w, np.float32).astype(ml_dtypes.bfloat16)).reshape(k // 32, 32, n)
    amax = np.abs(w).max(1)
    if fmt == "e4m3":
        byte = np.frexp(amax)[1] - 1 + 127 - 7
    else:
        mant, ex = np.frexp(amax / 6.0)
        byte = np.where(mant > 0.5, ex, ex - 1) + 127
    byte = np.clip(np.where(amax > 0, byte, 1), 1, 254)
    scaled = (w * np.exp2(127.0 - byte)[:, None, :]).reshape(k, n).astype(np.float32)
    by_word = np.ascontiguousarray(scaled.reshape(k // 512, 128, 4, n).transpose(0, 1, 3, 2))
    if fmt == "e4m3":
        words = by_word.astype(ml_dtypes.float8_e4m3fn).view(np.uint8)
    else:
        c = by_word.astype(ml_dtypes.float4_e2m1fn).view(np.uint8) & 0xF
        words = (c[..., 0::2] | (c[..., 1::2] << 4)).reshape(k // 512, 128, 2 * n)
    return np.ascontiguousarray(words), np.ascontiguousarray(byte.astype(np.uint8).reshape(k // 512, 16, n))


def unpack_weight(words, scales, fmt):
    g, _, n = scales.shape
    words = np.ascontiguousarray(words).reshape(g, 128, n, -1)
    if fmt == "e4m3":
        vals = words.view(ml_dtypes.float8_e4m3fn).astype(np.float64)
    else:
        nib = np.empty((g, 128, n, 4), np.uint8)
        nib[..., 0::2] = words & 0xF
        nib[..., 1::2] = words >> 4
        vals = E2M1[nib]
    vals = vals * np.repeat(np.exp2(scales.astype(np.float64) - 127.0), 8, axis=1)[..., None]
    return vals.transpose(0, 1, 3, 2).reshape(g * 512, n)


def gelu(v):
    return 0.5 * v * (1.0 + np.tanh(np.sqrt(2.0 / np.pi) * (v + 0.044715 * v**3)))


def bf(x):
    return np.asarray(x, np.float32).astype(ml_dtypes.bfloat16)


def planes(Y):
    n, m = Y.shape
    b = f64(bf(Y)).reshape(n // 32, 32, m)
    amax = np.abs(b).max(1)
    byte = np.clip(np.where(amax > 0, np.frexp(amax)[1] - 1 + 127 - 7, 1), 1, 254)
    codes = (b * np.exp2(127.0 - byte)[:, None, :]).reshape(n, m).astype(np.float32).astype(ml_dtypes.float8_e4m3fn).view(np.uint8)
    words = codes.reshape(n // 512, 128, 4, m).transpose(0, 1, 3, 2)
    return np.ascontiguousarray(words), np.ascontiguousarray(byte.astype(np.uint8).reshape(n // 512, 16, m))


K, H, N, T, S, T2, P = 512, 1024, 512, 4096, 1024, 2048, 512

def setup_inputs():
    n = np.random.standard_normal
    s = mx_kscale(K)[:, None]
    u = mx_kscale(H)[:, None]
    size = np.exp(0.8 * n(N))[None, :]
    tab_words, tab_scales = pack_weight(n((K, T)) * s, "e4m3")
    w2_words, w2_scales = pack_weight(n((K, H)) / np.sqrt(K) / s, "e2m1")
    w5_words, w5_scales = pack_weight(n((H, N)) / np.sqrt(H) / u, "e2m1")
    w6_words, w6_scales = pack_weight(n((H, N)) / np.sqrt(H) / u * size, "e4m3")
    return {
        "tab_words": tab_words, "tab_scales": tab_scales,
        "offs": striped(np.random.permutation(T)[:S]),
        "offs2": striped(np.random.permutation(T2)[:S]),
        "offs3": striped(np.random.permutation(T2)[:P]),
        "w1": (n((K, H)) / np.sqrt(K) / s * u.T).astype(np.float32),
        "w2_words": w2_words, "w2_scales": w2_scales,
        "w3": (n((K, H)) / np.sqrt(K) / s * u.T).astype(np.float32),
        "wgs": np.exp(0.3 * n((128, S))).astype(np.float32),
        "ctx": (n((H, P)) * u).astype(np.float32),
        "w4": (n((H, N)) / np.sqrt(H) / u * size).astype(np.float32),
        "w5_words": w5_words, "w5_scales": w5_scales,
        "w6_words": w6_words, "w6_scales": w6_scales,
    }

def reference(tab_words, tab_scales, offs, offs2, offs3, w1, w2_words, w2_scales, w3, wgs, ctx, w4, w5_words, w5_scales, w6_words, w6_scales):
    v = unpack_weight(tab_words, tab_scales, "e4m3")[:, unstriped(offs)]
    a = mxq(f64(w1), 0, "e4m3").T @ v
    b = unpack_weight(w2_words, w2_scales, "e2m1").T @ v
    d = mxq(f64(w3), 0, "e4m3").T @ v
    h = a * b + d
    page = np.zeros((H, T2))
    page[:, unstriped(offs2)] = np.tile(f64(wgs), (H // 128, 1)) * h
    x = page[:, unstriped(offs3)]
    z = mxq(x + f64(ctx), 0, "e4m3")
    base = mxq(f64(w4), 0, "e4m3").T @ z
    gate = unpack_weight(w5_words, w5_scales, "e2m1").T @ z
    more = unpack_weight(w6_words, w6_scales, "e4m3").T @ z
    y = base + more / (1.0 + np.exp(-gate))
    words, scales = planes(y)
    return y, words, scales

@@ -1,0 +1,327 @@
+from contextlib import ExitStack
+
+import concourse.mybir as mybir
+from concourse.masks import make_identity
+
+K, H, N, T, S, T2, M = 512, 1024, 512, 4096, 1024, 2048, 512
+FLOPS = 2 * (3 * K * H * S + 3 * H * N * M)
+
+F32 = mybir.dt.float32
+BF16 = mybir.dt.bfloat16
+I32 = mybir.dt.int32
+U32 = mybir.dt.uint32
+U16 = mybir.dt.uint16
+U8 = mybir.dt.uint8
+E4M3 = mybir.dt.float8_e4m3fn_x4
+E2M1 = mybir.dt.float4_e2m1fn_x4
+MULT = mybir.AluOpType.mult
+ADD = mybir.AluOpType.add
+SIGMOID = mybir.ActivationFunctionType.Sigmoid
+
+P = 128
+BANK = 512
+PAGES = H // P
+HALF = S // 2
+STEPS = 2 * PAGES
+KIB = 1024
+
+
+def tile_list_resumed_session_features_kernel(
+    tc, tab_words, tab_scales, offs, offs2, offs3, w1, w2_words, w2_scales, w3, wgs, ctx, w4,
+    w5_words, w5_scales, w6_words, w6_scales, out_0, out_1, out_2,
+):
+    nc = tc.nc
+    with ExitStack() as stack:
+        lists = stack.enter_context(tc.tile_pool(name="lists", bufs=1))
+        keep = stack.enter_context(tc.tile_pool(name="keep", bufs=1))
+        shared = stack.enter_context(tc.tile_pool(name="shared", bufs=1))
+        ring = stack.enter_context(tc.tile_pool(name="ring", bufs=2))
+        psum = stack.enter_context(tc.psum_pool(name="psum", bufs=1))
+
+        def bank(index, name):
+            return psum.tile([P, BANK], F32, name=name, tag="bank%d" % index)
+
+        def load_scale_rows(queue, plane, rows):
+            for q in range(4):
+                queue.dma_start(
+                    out=plane[32 * q : 32 * q + 4].bitcast(I32),
+                    in_=rows[:, 4 * q : 4 * q + 4, :].rearrange("a q n -> q a n").bitcast(I32),
+                )
+
+        def interleave(engine_copy, grouped, raw):
+            engine_copy(
+                out=grouped.rearrange("p (c i) t -> p c t i", i=4),
+                in_=raw.rearrange("p t (c i) -> p c t i", i=4),
+            )
+
+        list1 = lists.tile([P, S // 16], U16, name="list1")
+        list2 = lists.tile([P, S // 16], U16, name="list2")
+        list3 = lists.tile([P, M // 16], U16, name="list3")
+        nc.sync.dma_start(list1[:], offs)
+        nc.sync.dma_start(list2[:], offs2)
+        nc.sync.dma_start(list3[:], offs3)
+
+        table = shared.tile([P, T], I32, name="table", offset=0)
+        nc.sync.dma_start(out=table[:], in_=tab_words[0].rearrange("p t i -> p (t i)").bitcast(I32))
+        table_plane = shared.tile([P, T], U8, name="table_plane", offset=16 * KIB)
+        nc.vector.memset(table_plane[:].bitcast(I32), 0)
+        load_scale_rows(nc.scalar, table_plane[:].rearrange("p (a n) -> p a n", a=1), tab_scales)
+
+        w2_plane = keep.tile([P, 1, H], U8, name="w2_plane", align_bytes=64)
+        nc.gpsimd.memset(w2_plane[:].bitcast(I32), 0)
+        load_scale_rows(nc.gpsimd, w2_plane, w2_scales)
+        identity = keep.tile([P, P], F32, name="identity")
+        make_identity(nc, identity[:])
+
+        w1_rows = w1.rearrange("(p t) r -> p t r", t=4)
+        w3_rows = w3.rearrange("(p t) r -> p t r", t=4)
+        up_codes = {}
+        up_planes = {}
+
+        def prepare_up(c):
+            cols = slice(c * P, (c + 1) * P)
+            grouped = ring.tile([P, 2, P, 4], BF16, name="up_grouped", align_bytes=64)
+            for i, rows in enumerate((w1_rows, w3_rows)):
+                raw = ring.tile([P, 4, P], F32, name="up_raw%d" % i, bufs=1)
+                nc.sync.dma_start(out=raw[:], in_=rows[:, :, cols])
+                interleave(nc.scalar.copy, grouped[:, i], raw[:])
+            up_codes[c] = ring.tile([P, 2 * P], U32, name="up_codes", align_bytes=64)
+            up_planes[c] = ring.tile([P, 2 * P], U8, name="up_plane", align_bytes=64)
+            nc.vector.quantize_mx(
+                out=up_codes[c][:].bitcast(E4M3),
+                scales=up_planes[c][:],
+                in_=grouped[:].rearrange("p w r t -> p (w r t)"),
+            )
+
+        prepare_up(0)
+        w2_codes = keep.tile([P, 2 * H], U8, name="w2_codes", align_bytes=64)
+        nc.sync.dma_start(out=w2_codes[:].bitcast(I32), in_=w2_words[0].bitcast(I32))
+
+        warm = keep.tile([P, 1], F32, name="warm")
+        nc.scalar.activation(warm[:], identity[:, 0:1], SIGMOID)
+
+        pages = [keep.tile([P, T2], F32, name="page%d" % i) for i in range(2)]
+        for page in pages:
+            nc.vector.memset(page[:], 0.0)
+
+        v_codes = [keep.tile([P, HALF], U32, name="v_codes%d" % h, align_bytes=64) for h in range(2)]
+        v_planes = [keep.tile([P, HALF], U8, name="v_plane%d" % h, align_bytes=64) for h in range(2)]
+        half_cols = [slice(h * HALF // 16, (h + 1) * HALF // 16) for h in range(2)]
+        for h in range(2):
+            nc.vector.tensor_copy(v_planes[h][:], table_plane[:].indirect(list1[:, half_cols[h]]))
+        for h in range(2):
+            nc.vector.tensor_copy(v_codes[h][:], table[:].bitcast(U32).indirect(list1[:, half_cols[h]]))
+
+        weights = shared.tile([P, S], F32, name="weights", offset=16 * KIB)
+        nc.sync.dma_start(out=weights[:], in_=wgs)
+
+        products = {}
+        addends = {}
+        states = {}
+
+        def blocks(ap):
+            return [ap[:, i * P : (i + 1) * P] for i in range(4)]
+
+        def front(s):
+            c, h = divmod(s, 2)
+            a_bank = bank(s % 2, "a_bank")
+            b_bank = bank(2, "b_bank")
+            d_bank = bank(3, "d_bank")
+            moving = (
+                (b_bank, w2_codes[:, 2 * P * c : 2 * P * (c + 1)].bitcast(E2M1), w2_plane[:, 0, P * c : P * (c + 1)]),
+                (a_bank, up_codes[c][:, 0:P].bitcast(E4M3), up_planes[c][:, 0:P]),
+                (d_bank, up_codes[c][:, P : 2 * P].bitcast(E4M3), up_planes[c][:, P : 2 * P]),
+            )
+            for acc, codes, plane in moving:
+                for out, v_block, v_scale in zip(blocks(acc), blocks(v_codes[h]), blocks(v_planes[h])):
+                    nc.tensor.matmul_mx(
+                        out=out, lhsT=v_block.bitcast(E4M3), lhsT_scale=v_scale,
+                        rhs=codes, rhs_scale=plane, start=True, stop=True,
+                    )
+            b_vals = ring.tile([P, BANK], F32, name="b_vals")
+            nc.scalar.copy(out=b_vals[:], in_=b_bank[:])
+            addends[s] = ring.tile([P, BANK], F32, name="d_vals", bufs=3)
+            nc.scalar.copy(out=addends[s][:], in_=d_bank[:])
+            products[s] = ring.tile([P, BANK], F32, name="ab_vals", bufs=3)
+            nc.vector.tensor_tensor(products[s][:], a_bank[:], b_vals[:], MULT)
+
+        def add_transposed(acc_blocks, first, second):
+            n = len(acc_blocks)
+            for i in range(n):
+                nc.tensor.matmul(acc_blocks[i], lhsT=first[i], rhs=identity[:], is_transpose=True, start=(i == 0), stop=False)
+            for i in range(n):
+                nc.tensor.matmul(acc_blocks[i], lhsT=second[i], rhs=identity[:], is_transpose=True, start=False, stop=(i == n - 1))
+
+        def back(s):
+            h_bank = bank(4 + s % 2, "h_bank")
+            add_transposed(blocks(h_bank), blocks(addends[s]), blocks(products[s]))
+            states[s] = ring.tile([P, BANK], F32, name="h_vals", bufs=3)
+            nc.scalar.copy(out=states[s][:], in_=h_bank[:])
+
+        def scatter(s):
+            c, h = divmod(s, 2)
+            nc.vector.tensor_tensor(
+                pages[c % 2][:].indirect(list2[:, half_cols[h]]),
+                states[s][:], weights[:, h * HALF : (h + 1) * HALF], MULT,
+            )
+
+        z_rows = {(g, mh): keep.tile([P, 2, 2, P, 2], BF16, name="z_rows%d%d" % (g, mh)) for g in range(2) for mh in range(2)}
+        z_codes = {}
+        z_planes = {}
+        ctx_rows = ctx.rearrange("(c p) m -> c p m", p=P)
+
+        def round_z(c, mh, z_blocks):
+            g, cc = divmod(c, 4)
+            nc.scalar.copy(
+                out=z_rows[g, mh][:, :, :, 32 * cc : 32 * (cc + 1), :],
+                in_=z_blocks.rearrange("m (b p u e) -> m b u p e", b=2, u=2, e=2),
+            )
+
+        def fetch(c):
+            context = shared.tile([P, M], F32, name="context%d" % c, offset=8 * KIB + 2 * KIB * (c % 2))
+            nc.sync.dma_start(out=context[:], in_=ctx_rows[c])
+            page = pages[c % 2]
+            if c < PAGES - 1:
+                picked = ring.tile([P, M], F32, name="picked")
+                nc.vector.tensor_copy(picked[:], page[:].indirect(list3[:]))
+                z_bank = bank(6, "z_bank")
+                add_transposed(blocks(z_bank), blocks(context), blocks(picked))
+                for mh in range(2):
+                    round_z(c, mh, z_bank[:, 256 * mh : 256 * (mh + 1)])
+            else:
+                for mh in range(2):
+                    picked = ring.tile([P, M // 2], F32, name="picked")
+                    nc.vector.tensor_copy(picked[:], page[:].indirect(list3[:, 16 * mh : 16 * (mh + 1)]))
+                    z_bank = bank(6 + mh, "z_bank")
+                    add_transposed(blocks(z_bank)[:2], blocks(context)[2 * mh : 2 * mh + 2], [picked[:, 0:P], picked[:, P : 2 * P]])
+                    round_z(c, mh, z_bank[:, 0:256])
+                    quantize_z(1, mh, 6 + mh, nc.vector.tensor_copy)
+
+        def quantize_z(g, mh, bank_index, engine_copy):
+            words = z_rows[g, mh][:].rearrange("m b u p e -> m (b u p e)").bitcast(F32)
+            w_bank = bank(bank_index, "w_bank")
+            for out, block in zip(blocks(w_bank), blocks(words)):
+                nc.tensor.transpose(out, block, identity[:])
+            grouped = ring.tile([P, 2 * P * 4], BF16, name="z_grouped", align_bytes=64)
+            engine_copy(
+                out=grouped[:].bitcast(F32).rearrange("p (b m u) -> p b m u", b=2, u=2),
+                in_=w_bank[:].rearrange("p (b u m) -> p b m u", b=2, u=2),
+            )
+            z_codes[g, mh] = keep.tile([P, 2 * P], U32, name="z_codes%d%d" % (g, mh), align_bytes=64)
+            z_planes[g, mh] = keep.tile([P, 2 * P], U8, name="z_plane%d%d" % (g, mh), align_bytes=64)
+            nc.vector.quantize_mx(out=z_codes[g, mh][:].bitcast(E4M3), scales=z_planes[g, mh][:], in_=grouped[:])
+
+        w4_rows = w4.rearrange("(g p t) n -> g p t n", p=P, t=4)
+        w4_codes = {}
+        w4_planes = {}
+
+        def prepare_w4(g):
+            raw = shared.tile([P, 4, N], F32, name="w4_raw%d" % g, offset=0)
+            nc.sync.dma_start(out=raw[:], in_=w4_rows[g])
+            grouped = ring.tile([P, N, 4], BF16, name="w4_grouped", align_bytes=64, bufs=1)
+            for i in range(4):
+                cols = slice(i * P, (i + 1) * P)
+                interleave(nc.scalar.copy, grouped[:, cols], raw[:, :, cols])
+            w4_codes[g] = keep.tile([P, N], U32, name="w4_codes%d" % g, align_bytes=64)
+            w4_planes[g] = keep.tile([P, N], U8, name="w4_plane%d" % g, align_bytes=64)
+            nc.vector.quantize_mx(
+                out=w4_codes[g][:].bitcast(E4M3), scales=w4_planes[g][:],
+                in_=grouped[:].rearrange("p n t -> p (n t)"),
+            )
+
+        packed = {}
+
+        def load_packed():
+            packed["w6"] = shared.tile([P, 2, N], U32, name="w6_codes", offset=0, align_bytes=64)
+            nc.sync.dma_start(out=packed["w6"][:].bitcast(I32), in_=w6_words.rearrange("g p n t -> p g (n t)").bitcast(I32))
+            packed["w5"] = shared.tile([P, 2, 2 * N], U8, name="w5_codes", offset=4 * KIB, align_bytes=64)
+            nc.sync.dma_start(out=packed["w5"][:].bitcast(I32), in_=w5_words.rearrange("g p n -> p g n").bitcast(I32))
+            for name, rows, at in (("s5", w5_scales, 6), ("s6", w6_scales, 7)):
+                packed[name] = shared.tile([P, 2, N], U8, name="plane_" + name, offset=at * KIB, align_bytes=64)
+                nc.vector.memset(packed[name][:].bitcast(I32), 0)
+                load_scale_rows(nc.sync, packed[name], rows)
+
+        front(0)
+        front(1)
+        back(0)
+        for s in range(STEPS):
+            c, h = divmod(s, 2)
+            if h == 0 and c + 1 < PAGES:
+                prepare_up(c + 1)
+            if s + 2 < STEPS:
+                front(s + 2)
+            if s + 1 < STEPS:
+                back(s + 1)
+            scatter(s)
+            if s == 3 or s == 5:
+                prepare_w4((s - 3) // 2)
+            if s == 7:
+                load_packed()
+            if h == 1:
+                fetch(c)
+            if s == 7:
+                for mh in range(2):
+                    quantize_z(0, mh, 7, nc.scalar.copy)
+
+        y_codes = keep.tile([P, M], U32, name="y_codes", align_bytes=64)
+        y_plane = keep.tile([P, M], U8, name="y_plane", align_bytes=64)
+        out_rows = out_0.rearrange("(p t) m -> p t m", t=4)
+        out_words = out_1[0].rearrange("p m t -> p (m t)").bitcast(I32)
+
+        def dealt(ap):
+            return ap.rearrange("m (p t) -> m t p", t=4)
+
+        def by_slot(ap):
+            return ap.rearrange("m (t p) -> m t p", t=4)
+
+        sums = {}
+
+        def multiply(q):
+            mh, b = divmod(q, 2)
+            cols = slice(b * P, (b + 1) * P)
+            sums[q] = [bank(3 * (q % 2) + i, "y_sum") for i in range(3)]
+            for g in range(2):
+                moving = (
+                    (packed["w5"][:, g, :].bitcast(E2M1), packed["s5"][:, g, :]),
+                    (packed["w6"][:, g, :].bitcast(E4M3), packed["s6"][:, g, :]),
+                    (w4_codes[g][:].bitcast(E4M3), w4_planes[g][:]),
+                )
+                for acc, (codes, plane) in zip(sums[q], moving):
+                    nc.tensor.matmul_mx(
+                        out=acc[:], lhsT=z_codes[g, mh][:, cols].bitcast(E4M3), lhsT_scale=z_planes[g, mh][:, cols],
+                        rhs=codes, rhs_scale=plane, start=(g == 0), stop=(g == 1),
+                    )
+
+        def finish(q):
+            gate, more, base = sums[q]
+            cols = slice(q * P, (q + 1) * P)
+            opened = ring.tile([P, N], F32, name="opened")
+            nc.scalar.activation(by_slot(opened[:]), dealt(gate[:]), SIGMOID)
+            gated = ring.tile([P, N], F32, name="gated")
+            nc.vector.tensor_tensor(by_slot(gated[:]), dealt(more[:]), by_slot(opened[:]), MULT)
+            y_rows = ring.tile([P, N], F32, name="y_rows")
+            nc.vector.tensor_tensor(by_slot(y_rows[:]), dealt(base[:]), by_slot(gated[:]), ADD)
+            y_bank = bank(6 + q % 2, "y_bank")
+            for out, block in zip(blocks(y_bank), blocks(y_rows)):
+                nc.tensor.transpose(out, block, identity[:])
+            y_vals = ring.tile([P, 4, P], F32, name="y_vals")
+            nc.scalar.copy(out=y_vals[:].rearrange("p t m -> p (t m)"), in_=y_bank[:])
+            nc.sync.dma_start(out=out_rows[:, :, cols], in_=y_vals[:])
+            y_grouped = ring.tile([P, P, 4], BF16, name="y_grouped", align_bytes=64)
+            interleave(nc.vector.tensor_copy, y_grouped[:], y_vals[:])
+            nc.vector.quantize_mx(
+                out=y_codes[:, cols].bitcast(E4M3), scales=y_plane[:, cols],
+                in_=y_grouped[:].rearrange("p m t -> p (m t)"),
+            )
+            nc.sync.dma_start(out=out_words[:, cols], in_=y_codes[:, cols].bitcast(I32))
+
+        multiply(0)
+        for q in range(4):
+            if q + 1 < 4:
+                multiply(q + 1)
+            finish(q)
+        for q in range(4):
+            nc.scalar.dma_start(
+                out=out_2[0, 4 * q : 4 * q + 4, :].bitcast(I32),
+                in_=y_plane[32 * q : 32 * q + 4, :].bitcast(I32),
+            )

@@ -61,8 +61,6 @@ def tile_list_resumed_session_features_kernel(
         nc.sync.dma_start(list2[:], offs2)
         nc.sync.dma_start(list3[:], offs3)
 
-        table = shared.tile([P, T], I32, name="table", offset=0)
-        nc.sync.dma_start(out=table[:], in_=tab_words[0].rearrange("p t i -> p (t i)").bitcast(I32))
         table_plane = shared.tile([P, T], U8, name="table_plane", offset=16 * KIB)
         nc.vector.memset(table_plane[:].bitcast(I32), 0)
         load_scale_rows(nc.scalar, table_plane[:].rearrange("p (a n) -> p a n", a=1), tab_scales)
@@ -85,8 +83,8 @@ def tile_list_resumed_session_features_kernel(
                 raw = ring.tile([P, 4, P], F32, name="up_raw%d" % i, bufs=1)
                 nc.sync.dma_start(out=raw[:], in_=rows[:, :, cols])
                 interleave(nc.scalar.copy, grouped[:, i], raw[:])
-            up_codes[c] = ring.tile([P, 2 * P], U32, name="up_codes", align_bytes=64)
-            up_planes[c] = ring.tile([P, 2 * P], U8, name="up_plane", align_bytes=64)
+            up_codes[c] = ring.tile([P, 2 * P], U32, name="up_codes", align_bytes=64, bufs=3)
+            up_planes[c] = ring.tile([P, 2 * P], U8, name="up_plane", align_bytes=64, bufs=3)
             nc.vector.quantize_mx(
                 out=up_codes[c][:].bitcast(E4M3),
                 scales=up_planes[c][:],
@@ -96,6 +94,10 @@ def tile_list_resumed_session_features_kernel(
         prepare_up(0)
         w2_codes = keep.tile([P, 2 * H], U8, name="w2_codes", align_bytes=64)
         nc.sync.dma_start(out=w2_codes[:].bitcast(I32), in_=w2_words[0].bitcast(I32))
+        table = shared.tile([P, T], I32, name="table", offset=0)
+        nc.sync.dma_start(out=table[:], in_=tab_words[0].rearrange("p t i -> p (t i)").bitcast(I32))
+        weights = keep.tile([P, S], F32, name="weights")
+        nc.sync.dma_start(out=weights[:], in_=wgs)
 
         warm = keep.tile([P, 1], F32, name="warm")
         nc.scalar.activation(warm[:], identity[:, 0:1], SIGMOID)
@@ -104,7 +106,7 @@ def tile_list_resumed_session_features_kernel(
         for page in pages:
             nc.vector.memset(page[:], 0.0)
 
-        v_codes = [keep.tile([P, HALF], U32, name="v_codes%d" % h, align_bytes=64) for h in range(2)]
+        v_codes = [shared.tile([P, HALF], U32, name="v_codes%d" % h, align_bytes=64, offset=(16 + 2 * h) * KIB) for h in range(2)]
         v_planes = [keep.tile([P, HALF], U8, name="v_plane%d" % h, align_bytes=64) for h in range(2)]
         half_cols = [slice(h * HALF // 16, (h + 1) * HALF // 16) for h in range(2)]
         for h in range(2):
@@ -112,8 +114,6 @@ def tile_list_resumed_session_features_kernel(
         for h in range(2):
             nc.vector.tensor_copy(v_codes[h][:], table[:].bitcast(U32).indirect(list1[:, half_cols[h]]))
 
-        weights = shared.tile([P, S], F32, name="weights", offset=16 * KIB)
-        nc.sync.dma_start(out=weights[:], in_=wgs)
 
         products = {}
         addends = {}
@@ -124,9 +124,7 @@ def tile_list_resumed_session_features_kernel(
 
         def front(s):
             c, h = divmod(s, 2)
-            a_bank = bank(s % 2, "a_bank")
-            b_bank = bank(2, "b_bank")
-            d_bank = bank(3, "d_bank")
+            b_bank, a_bank, d_bank = [bank(i, "up_sum") for i in range(3)]
             moving = (
                 (b_bank, w2_codes[:, 2 * P * c : 2 * P * (c + 1)].bitcast(E2M1), w2_plane[:, 0, P * c : P * (c + 1)]),
                 (a_bank, up_codes[c][:, 0:P].bitcast(E4M3), up_planes[c][:, 0:P]),
@@ -140,10 +138,15 @@ def tile_list_resumed_session_features_kernel(
                     )
             b_vals = ring.tile([P, BANK], F32, name="b_vals")
             nc.scalar.copy(out=b_vals[:], in_=b_bank[:])
+            products[s] = ring.tile([P, BANK], F32, name="ab_vals", bufs=3)
+            if s == 0:
+                nc.vector.tensor_tensor(products[s][:], a_bank[:], b_vals[:], MULT)
+            else:
+                a_vals = ring.tile([P, BANK], F32, name="a_vals")
+                nc.scalar.copy(out=a_vals[:], in_=a_bank[:])
+                nc.gpsimd.tensor_tensor(products[s][:], a_vals[:], b_vals[:], MULT)
             addends[s] = ring.tile([P, BANK], F32, name="d_vals", bufs=3)
             nc.scalar.copy(out=addends[s][:], in_=d_bank[:])
-            products[s] = ring.tile([P, BANK], F32, name="ab_vals", bufs=3)
-            nc.vector.tensor_tensor(products[s][:], a_bank[:], b_vals[:], MULT)
 
         def add_transposed(acc_blocks, first, second):
             n = len(acc_blocks)
@@ -153,17 +156,20 @@ def tile_list_resumed_session_features_kernel(
                 nc.tensor.matmul(acc_blocks[i], lhsT=second[i], rhs=identity[:], is_transpose=True, start=False, stop=(i == n - 1))
 
         def back(s):
-            h_bank = bank(4 + s % 2, "h_bank")
+            cols = slice((s % 2) * HALF, (s % 2 + 1) * HALF)
+            h_bank = bank(3 + s % 2, "h_bank")
             add_transposed(blocks(h_bank), blocks(addends[s]), blocks(products[s]))
-            states[s] = ring.tile([P, BANK], F32, name="h_vals", bufs=3)
-            nc.scalar.copy(out=states[s][:], in_=h_bank[:])
+            states[s] = ring.tile([P, BANK], F32, name="weighted", bufs=3)
+            if s == 0:
+                nc.vector.tensor_tensor(states[s][:], h_bank[:], weights[:, cols], MULT)
+            else:
+                h_vals = ring.tile([P, BANK], F32, name="h_vals")
+                nc.scalar.copy(out=h_vals[:], in_=h_bank[:])
+                nc.gpsimd.tensor_tensor(states[s][:], h_vals[:], weights[:, cols], MULT)
 
         def scatter(s):
             c, h = divmod(s, 2)
-            nc.vector.tensor_tensor(
-                pages[c % 2][:].indirect(list2[:, half_cols[h]]),
-                states[s][:], weights[:, h * HALF : (h + 1) * HALF], MULT,
-            )
+            nc.vector.tensor_copy(pages[c % 2][:].indirect(list2[:, half_cols[h]]), states[s][:])
 
         z_rows = {(g, mh): keep.tile([P, 2, 2, P, 2], BF16, name="z_rows%d%d" % (g, mh)) for g in range(2) for mh in range(2)}
         z_codes = {}
@@ -244,14 +250,15 @@ def tile_list_resumed_session_features_kernel(
         front(0)
         front(1)
         back(0)
+        prepare_up(1)
         for s in range(STEPS):
             c, h = divmod(s, 2)
-            if h == 0 and c + 1 < PAGES:
-                prepare_up(c + 1)
             if s + 2 < STEPS:
                 front(s + 2)
             if s + 1 < STEPS:
                 back(s + 1)
+            if h == 0 and c + 2 < PAGES:
+                prepare_up(c + 2)
             scatter(s)
             if s == 3 or s == 5:
                 prepare_w4((s - 3) // 2)

@@ -19,11 +19,29 @@ ADD = mybir.AluOpType.add
 SIGMOID = mybir.ActivationFunctionType.Sigmoid
 
 P = 128
+PACK = 4
+QUADRANT = 32
+STRIPE = 16
 BANK = 512
+BANK_BLOCKS = BANK // P
 PAGES = H // P
+PASSES = H // (P * PACK)
+PASS_PAGES = PAGES // PASSES
 HALF = S // 2
-STEPS = 2 * PAGES
+QUARTERS = M // P
+SCALAR_ROUNDS = 2
+
+STEPS = [(0, 0, 2), (0, 2, 2), (0, 4, 4)] + [(c, first, 4) for c in range(1, PAGES) for first in (0, 4)]
+LAST_STEP = len(STEPS) - 1
+
+B_BANK, D_BANK, A_BANKS, H_BANKS = 0, 2, (1, 5), (3, 4)
+SPARE_BANKS = (6, 7)
+
 KIB = 1024
+TABLE_AT = 0
+PLANE_AT = 16 * KIB
+FACTORS_AT = 20 * KIB
+LAST_STATES_AT = 32 * KIB
 
 
 def tile_list_resumed_session_features_kernel(
@@ -41,27 +59,40 @@ def tile_list_resumed_session_features_kernel(
         def bank(index, name):
             return psum.tile([P, BANK], F32, name=name, tag="bank%d" % index)
 
+        def blocks(ap):
+            return [ap[:, i * P : (i + 1) * P] for i in range(ap.shape[1] // P)]
+
+        def entries(list_tile, start, count):
+            return list_tile[:, start // STRIPE : (start + count) // STRIPE]
+
         def load_scale_rows(queue, plane, rows):
-            for q in range(4):
+            for quad in range(P // QUADRANT):
                 queue.dma_start(
-                    out=plane[32 * q : 32 * q + 4].bitcast(I32),
-                    in_=rows[:, 4 * q : 4 * q + 4, :].rearrange("a q n -> q a n").bitcast(I32),
+                    out=plane[QUADRANT * quad : QUADRANT * quad + 4].bitcast(I32),
+                    in_=rows[:, 4 * quad : 4 * quad + 4, :].rearrange("a q n -> q a n").bitcast(I32),
                 )
 
-        def interleave(engine_copy, grouped, raw):
+        def interleave(engine_copy, grouped, planar):
             engine_copy(
                 out=grouped.rearrange("p (c i) t -> p c t i", i=4),
-                in_=raw.rearrange("p t (c i) -> p c t i", i=4),
+                in_=planar.rearrange("p t (c i) -> p c t i", i=4),
             )
 
-        list1 = lists.tile([P, S // 16], U16, name="list1")
-        list2 = lists.tile([P, S // 16], U16, name="list2")
-        list3 = lists.tile([P, M // 16], U16, name="list3")
+        def add_transposed(sum_blocks, early, late):
+            n = len(sum_blocks)
+            for i in range(n):
+                nc.tensor.matmul(sum_blocks[i], lhsT=early[i], rhs=identity[:], is_transpose=True, start=(i == 0), stop=False)
+            for i in range(n):
+                nc.tensor.matmul(sum_blocks[i], lhsT=late[i], rhs=identity[:], is_transpose=True, start=False, stop=(i == n - 1))
+
+        list1 = lists.tile([P, S // STRIPE], U16, name="list1")
+        list2 = lists.tile([P, S // STRIPE], U16, name="list2")
+        list3 = lists.tile([P, M // STRIPE], U16, name="list3")
         nc.sync.dma_start(list1[:], offs)
         nc.sync.dma_start(list2[:], offs2)
         nc.sync.dma_start(list3[:], offs3)
 
-        table_plane = shared.tile([P, T], U8, name="table_plane", offset=16 * KIB)
+        table_plane = shared.tile([P, T], U8, name="table_plane", offset=PLANE_AT)
         nc.vector.memset(table_plane[:].bitcast(I32), 0)
         load_scale_rows(nc.scalar, table_plane[:].rearrange("p (a n) -> p a n", a=1), tab_scales)
 
@@ -71,251 +102,261 @@ def tile_list_resumed_session_features_kernel(
         identity = keep.tile([P, P], F32, name="identity")
         make_identity(nc, identity[:])
 
-        w1_rows = w1.rearrange("(p t) r -> p t r", t=4)
-        w3_rows = w3.rearrange("(p t) r -> p t r", t=4)
-        up_codes = {}
-        up_planes = {}
+        w1_rows = w1.rearrange("(p t) r -> p t r", t=PACK)
+        w3_rows = w3.rearrange("(p t) r -> p t r", t=PACK)
+        w13_codes = {}
+        w13_planes = {}
 
-        def prepare_up(c):
+        def round_block(grouped, rows):
+            raw = ring.tile([P, PACK, P], F32, name="raw", bufs=4)
+            nc.sync.dma_start(out=raw[:], in_=rows)
+            interleave(nc.scalar.copy, grouped, raw[:])
+
+        def prepare_page(c):
             cols = slice(c * P, (c + 1) * P)
-            grouped = ring.tile([P, 2, P, 4], BF16, name="up_grouped", align_bytes=64)
+            if c == 0:
+                grouped = shared.tile([P, 2, P, PACK], BF16, name="first_grouped", align_bytes=64, offset=FACTORS_AT)
+            else:
+                grouped = ring.tile([P, 2, P, PACK], BF16, name="w13_grouped", align_bytes=64)
             for i, rows in enumerate((w1_rows, w3_rows)):
-                raw = ring.tile([P, 4, P], F32, name="up_raw%d" % i, bufs=1)
-                nc.sync.dma_start(out=raw[:], in_=rows[:, :, cols])
-                interleave(nc.scalar.copy, grouped[:, i], raw[:])
-            up_codes[c] = ring.tile([P, 2 * P], U32, name="up_codes", align_bytes=64, bufs=3)
-            up_planes[c] = ring.tile([P, 2 * P], U8, name="up_plane", align_bytes=64, bufs=3)
+                round_block(grouped[:, i], rows[:, :, cols])
+            w13_codes[c] = ring.tile([P, 2 * P], U32, name="w13_codes", align_bytes=64, bufs=3)
+            w13_planes[c] = ring.tile([P, 2 * P], U8, name="w13_plane", align_bytes=64, bufs=3)
             nc.vector.quantize_mx(
-                out=up_codes[c][:].bitcast(E4M3),
-                scales=up_planes[c][:],
+                out=w13_codes[c][:].bitcast(E4M3),
+                scales=w13_planes[c][:],
                 in_=grouped[:].rearrange("p w r t -> p (w r t)"),
             )
 
-        prepare_up(0)
+        prepare_page(0)
         w2_codes = keep.tile([P, 2 * H], U8, name="w2_codes", align_bytes=64)
         nc.sync.dma_start(out=w2_codes[:].bitcast(I32), in_=w2_words[0].bitcast(I32))
-        table = shared.tile([P, T], I32, name="table", offset=0)
+        table = shared.tile([P, T], I32, name="table", offset=TABLE_AT)
         nc.sync.dma_start(out=table[:], in_=tab_words[0].rearrange("p t i -> p (t i)").bitcast(I32))
-        weights = keep.tile([P, S], F32, name="weights")
-        nc.sync.dma_start(out=weights[:], in_=wgs)
-
-        warm = keep.tile([P, 1], F32, name="warm")
-        nc.scalar.activation(warm[:], identity[:, 0:1], SIGMOID)
+        factors = shared.tile([P, S], F32, name="factors", offset=FACTORS_AT)
+        nc.sync.dma_start(out=factors[:], in_=wgs)
 
         pages = [keep.tile([P, T2], F32, name="page%d" % i) for i in range(2)]
         for page in pages:
             nc.vector.memset(page[:], 0.0)
 
-        v_codes = [shared.tile([P, HALF], U32, name="v_codes%d" % h, align_bytes=64, offset=(16 + 2 * h) * KIB) for h in range(2)]
+        v_codes = [
+            shared.tile([P, HALF], U32, name="v_codes%d" % h, align_bytes=64, offset=PLANE_AT + 4 * HALF * h)
+            for h in range(2)
+        ]
         v_planes = [keep.tile([P, HALF], U8, name="v_plane%d" % h, align_bytes=64) for h in range(2)]
-        half_cols = [slice(h * HALF // 16, (h + 1) * HALF // 16) for h in range(2)]
         for h in range(2):
-            nc.vector.tensor_copy(v_planes[h][:], table_plane[:].indirect(list1[:, half_cols[h]]))
+            nc.vector.tensor_copy(v_planes[h][:], table_plane[:].indirect(entries(list1, h * HALF, HALF)))
         for h in range(2):
-            nc.vector.tensor_copy(v_codes[h][:], table[:].bitcast(U32).indirect(list1[:, half_cols[h]]))
-
+            nc.vector.tensor_copy(v_codes[h][:], table[:].bitcast(U32).indirect(entries(list1, h * HALF, HALF)))
 
         products = {}
         addends = {}
         states = {}
 
-        def blocks(ap):
-            return [ap[:, i * P : (i + 1) * P] for i in range(4)]
-
-        def front(s):
-            c, h = divmod(s, 2)
-            b_bank, a_bank, d_bank = [bank(i, "up_sum") for i in range(3)]
+        def make_terms(s):
+            c, first, count = STEPS[s]
+            h, at = divmod(first, BANK_BLOCKS)
+            width = count * P
+            b_bank, a_bank, d_bank = [bank(i, "terms") for i in (B_BANK, A_BANKS[s % 2], D_BANK)]
             moving = (
                 (b_bank, w2_codes[:, 2 * P * c : 2 * P * (c + 1)].bitcast(E2M1), w2_plane[:, 0, P * c : P * (c + 1)]),
-                (a_bank, up_codes[c][:, 0:P].bitcast(E4M3), up_planes[c][:, 0:P]),
-                (d_bank, up_codes[c][:, P : 2 * P].bitcast(E4M3), up_planes[c][:, P : 2 * P]),
+                (a_bank, w13_codes[c][:, 0:P].bitcast(E4M3), w13_planes[c][:, 0:P]),
+                (d_bank, w13_codes[c][:, P : 2 * P].bitcast(E4M3), w13_planes[c][:, P : 2 * P]),
             )
-            for acc, codes, plane in moving:
-                for out, v_block, v_scale in zip(blocks(acc), blocks(v_codes[h]), blocks(v_planes[h])):
+            v_blocks = blocks(v_codes[h])[at : at + count]
+            v_scales = blocks(v_planes[h])[at : at + count]
+            for term_bank, codes, plane in moving:
+                for term_block, v_block, v_scale in zip(blocks(term_bank), v_blocks, v_scales):
                     nc.tensor.matmul_mx(
-                        out=out, lhsT=v_block.bitcast(E4M3), lhsT_scale=v_scale,
+                        out=term_block, lhsT=v_block.bitcast(E4M3), lhsT_scale=v_scale,
                         rhs=codes, rhs_scale=plane, start=True, stop=True,
                     )
-            b_vals = ring.tile([P, BANK], F32, name="b_vals")
-            nc.scalar.copy(out=b_vals[:], in_=b_bank[:])
-            products[s] = ring.tile([P, BANK], F32, name="ab_vals", bufs=3)
-            if s == 0:
-                nc.vector.tensor_tensor(products[s][:], a_bank[:], b_vals[:], MULT)
-            else:
-                a_vals = ring.tile([P, BANK], F32, name="a_vals")
-                nc.scalar.copy(out=a_vals[:], in_=a_bank[:])
-                nc.gpsimd.tensor_tensor(products[s][:], a_vals[:], b_vals[:], MULT)
-            addends[s] = ring.tile([P, BANK], F32, name="d_vals", bufs=3)
-            nc.scalar.copy(out=addends[s][:], in_=d_bank[:])
+            b_vals = ring.tile([P, width], F32, name="b_vals", bufs=3)
+            nc.scalar.copy(out=b_vals[:], in_=b_bank[:, 0:width])
+            products[s] = ring.tile([P, width], F32, name="ab_vals", bufs=3)
+            nc.vector.tensor_tensor(products[s][:], a_bank[:, 0:width], b_vals[:], MULT)
+            addends[s] = ring.tile([P, width], F32, name="d_vals", bufs=3)
+            nc.scalar.copy(out=addends[s][:], in_=d_bank[:, 0:width])
 
-        def add_transposed(acc_blocks, first, second):
-            n = len(acc_blocks)
-            for i in range(n):
-                nc.tensor.matmul(acc_blocks[i], lhsT=first[i], rhs=identity[:], is_transpose=True, start=(i == 0), stop=False)
-            for i in range(n):
-                nc.tensor.matmul(acc_blocks[i], lhsT=second[i], rhs=identity[:], is_transpose=True, start=False, stop=(i == n - 1))
-
-        def back(s):
-            cols = slice((s % 2) * HALF, (s % 2 + 1) * HALF)
-            h_bank = bank(3 + s % 2, "h_bank")
-            add_transposed(blocks(h_bank), blocks(addends[s]), blocks(products[s]))
-            states[s] = ring.tile([P, BANK], F32, name="weighted", bufs=3)
-            if s == 0:
-                nc.vector.tensor_tensor(states[s][:], h_bank[:], weights[:, cols], MULT)
+        def make_states(s):
+            h_bank = bank(H_BANKS[s % 2], "h_bank")
+            count = STEPS[s][2]
+            add_transposed(blocks(h_bank)[:count], blocks(addends[s]), blocks(products[s]))
+            if s == LAST_STEP:
+                states[s] = shared.tile([P, count * P], F32, name="last_states", offset=LAST_STATES_AT)
             else:
-                h_vals = ring.tile([P, BANK], F32, name="h_vals")
-                nc.scalar.copy(out=h_vals[:], in_=h_bank[:])
-                nc.gpsimd.tensor_tensor(states[s][:], h_vals[:], weights[:, cols], MULT)
+                states[s] = ring.tile([P, count * P], F32, name="states", bufs=4)
+            nc.scalar.copy(out=states[s][:], in_=h_bank[:, 0 : count * P])
 
         def scatter(s):
-            c, h = divmod(s, 2)
-            nc.vector.tensor_copy(pages[c % 2][:].indirect(list2[:, half_cols[h]]), states[s][:])
+            c, first, count = STEPS[s]
+            nc.vector.tensor_tensor(
+                pages[c % 2][:].indirect(entries(list2, first * P, count * P)),
+                states[s][:], factors[:, first * P : (first + count) * P], MULT,
+            )
 
-        z_rows = {(g, mh): keep.tile([P, 2, 2, P, 2], BF16, name="z_rows%d%d" % (g, mh)) for g in range(2) for mh in range(2)}
+        z_rows = {
+            (g, mh): keep.tile([P, 2, 2, P, 2], BF16, name="z_rows%d%d" % (g, mh))
+            for g in range(PASSES) for mh in range(2)
+        }
         z_codes = {}
         z_planes = {}
         ctx_rows = ctx.rearrange("(c p) m -> c p m", p=P)
+        contexts = {}
+        picks = {}
 
         def round_z(c, mh, z_blocks):
-            g, cc = divmod(c, 4)
+            g, cc = divmod(c, PASS_PAGES)
+            words = P // PACK
             nc.scalar.copy(
-                out=z_rows[g, mh][:, :, :, 32 * cc : 32 * (cc + 1), :],
+                out=z_rows[g, mh][:, :, :, words * cc : words * (cc + 1), :],
                 in_=z_blocks.rearrange("m (b p u e) -> m b u p e", b=2, u=2, e=2),
             )
 
-        def fetch(c):
-            context = shared.tile([P, M], F32, name="context%d" % c, offset=8 * KIB + 2 * KIB * (c % 2))
-            nc.sync.dma_start(out=context[:], in_=ctx_rows[c])
-            page = pages[c % 2]
-            if c < PAGES - 1:
-                picked = ring.tile([P, M], F32, name="picked")
-                nc.vector.tensor_copy(picked[:], page[:].indirect(list3[:]))
-                z_bank = bank(6, "z_bank")
-                add_transposed(blocks(z_bank), blocks(context), blocks(picked))
-                for mh in range(2):
-                    round_z(c, mh, z_bank[:, 256 * mh : 256 * (mh + 1)])
-            else:
-                for mh in range(2):
-                    picked = ring.tile([P, M // 2], F32, name="picked")
-                    nc.vector.tensor_copy(picked[:], page[:].indirect(list3[:, 16 * mh : 16 * (mh + 1)]))
-                    z_bank = bank(6 + mh, "z_bank")
-                    add_transposed(blocks(z_bank)[:2], blocks(context)[2 * mh : 2 * mh + 2], [picked[:, 0:P], picked[:, P : 2 * P]])
-                    round_z(c, mh, z_bank[:, 0:256])
-                    quantize_z(1, mh, 6 + mh, nc.vector.tensor_copy)
+        def load_context(c):
+            contexts[c] = shared.tile([P, M], F32, name="context%d" % c, offset=TABLE_AT + 4 * M * c)
+            nc.sync.dma_start(out=contexts[c][:], in_=ctx_rows[c])
 
-        def quantize_z(g, mh, bank_index, engine_copy):
-            words = z_rows[g, mh][:].rearrange("m b u p e -> m (b u p e)").bitcast(F32)
-            w_bank = bank(bank_index, "w_bank")
-            for out, block in zip(blocks(w_bank), blocks(words)):
-                nc.tensor.transpose(out, block, identity[:])
-            grouped = ring.tile([P, 2 * P * 4], BF16, name="z_grouped", align_bytes=64)
-            engine_copy(
+        def pick(c, start, count):
+            picked = ring.tile([P, count], F32, name="picked", bufs=3)
+            nc.vector.tensor_copy(picked[:], pages[c % 2][:].indirect(entries(list3, start, count)))
+            return picked
+
+        def place(c, bank_index):
+            z_bank = bank(bank_index, "z_bank")
+            add_transposed(blocks(z_bank), blocks(contexts[c]), blocks(picks[c]))
+            for mh in range(2):
+                round_z(c, mh, z_bank[:, 2 * P * mh : 2 * P * (mh + 1)])
+
+        def quantize_z(g, mh, bank_index):
+            z_words = z_rows[g, mh][:].rearrange("m b u p e -> m (b u p e)").bitcast(F32)
+            word_bank = bank(bank_index, "word_bank")
+            for turned, block in zip(blocks(word_bank), blocks(z_words)):
+                nc.tensor.transpose(turned, block, identity[:])
+            grouped = ring.tile([P, 2 * P * PACK], BF16, name="z_grouped", align_bytes=64)
+            nc.scalar.copy(
                 out=grouped[:].bitcast(F32).rearrange("p (b m u) -> p b m u", b=2, u=2),
-                in_=w_bank[:].rearrange("p (b u m) -> p b m u", b=2, u=2),
+                in_=word_bank[:].rearrange("p (b u m) -> p b m u", b=2, u=2),
             )
             z_codes[g, mh] = keep.tile([P, 2 * P], U32, name="z_codes%d%d" % (g, mh), align_bytes=64)
             z_planes[g, mh] = keep.tile([P, 2 * P], U8, name="z_plane%d%d" % (g, mh), align_bytes=64)
             nc.vector.quantize_mx(out=z_codes[g, mh][:].bitcast(E4M3), scales=z_planes[g, mh][:], in_=grouped[:])
 
-        w4_rows = w4.rearrange("(g p t) n -> g p t n", p=P, t=4)
-        w4_codes = {}
-        w4_planes = {}
+        w4_rows = w4.rearrange("(g p t) n -> g p t n", p=P, t=PACK)
+        w4_grouped = {}
+        last_weights = {}
 
-        def prepare_w4(g):
-            raw = shared.tile([P, 4, N], F32, name="w4_raw%d" % g, offset=0)
-            nc.sync.dma_start(out=raw[:], in_=w4_rows[g])
-            grouped = ring.tile([P, N, 4], BF16, name="w4_grouped", align_bytes=64, bufs=1)
-            for i in range(4):
+        def round_w4(g, half):
+            if half == 0:
+                w4_grouped[g] = keep.tile([P, N, PACK], BF16, name="w4_grouped%d" % g, align_bytes=64)
+            for i in (2 * half, 2 * half + 1):
                 cols = slice(i * P, (i + 1) * P)
-                interleave(nc.scalar.copy, grouped[:, cols], raw[:, :, cols])
-            w4_codes[g] = keep.tile([P, N], U32, name="w4_codes%d" % g, align_bytes=64)
-            w4_planes[g] = keep.tile([P, N], U8, name="w4_plane%d" % g, align_bytes=64)
-            nc.vector.quantize_mx(
-                out=w4_codes[g][:].bitcast(E4M3), scales=w4_planes[g][:],
-                in_=grouped[:].rearrange("p n t -> p (n t)"),
-            )
+                round_block(w4_grouped[g][:, cols], w4_rows[g][:, :, cols])
 
-        packed = {}
+        def quantize_w4():
+            codes = shared.tile([P, PASSES, N], U32, name="w4_codes", align_bytes=64, offset=LAST_STATES_AT)
+            for g in range(PASSES):
+                plane = keep.tile([P, N], U8, name="w4_plane%d" % g, align_bytes=64)
+                nc.vector.quantize_mx(
+                    out=codes[:, g, :].bitcast(E4M3), scales=plane[:],
+                    in_=w4_grouped[g][:].rearrange("p n t -> p (n t)"),
+                )
+                last_weights["base", g] = (codes[:, g, :].bitcast(E4M3), plane[:])
 
-        def load_packed():
-            packed["w6"] = shared.tile([P, 2, N], U32, name="w6_codes", offset=0, align_bytes=64)
-            nc.sync.dma_start(out=packed["w6"][:].bitcast(I32), in_=w6_words.rearrange("g p n t -> p g (n t)").bitcast(I32))
-            packed["w5"] = shared.tile([P, 2, 2 * N], U8, name="w5_codes", offset=4 * KIB, align_bytes=64)
-            nc.sync.dma_start(out=packed["w5"][:].bitcast(I32), in_=w5_words.rearrange("g p n -> p g n").bitcast(I32))
-            for name, rows, at in (("s5", w5_scales, 6), ("s6", w6_scales, 7)):
-                packed[name] = shared.tile([P, 2, N], U8, name="plane_" + name, offset=at * KIB, align_bytes=64)
-                nc.vector.memset(packed[name][:].bitcast(I32), 0)
-                load_scale_rows(nc.sync, packed[name], rows)
+        def load_w5_w6():
+            w5_at = TABLE_AT + 4 * PASSES * N
+            planes_at = w5_at + 2 * PASSES * N
+            w6_codes = shared.tile([P, PASSES, N], U32, name="w6_codes", offset=TABLE_AT, align_bytes=64)
+            nc.sync.dma_start(out=w6_codes[:].bitcast(I32), in_=w6_words.rearrange("g p n t -> p g (n t)").bitcast(I32))
+            w5_codes = shared.tile([P, PASSES, 2 * N], U8, name="w5_codes", offset=w5_at, align_bytes=64)
+            nc.sync.dma_start(out=w5_codes[:].bitcast(I32), in_=w5_words.rearrange("g p n -> p g n").bitcast(I32))
+            for i, (name, codes, fmt, rows) in enumerate((("gate", w5_codes, E2M1, w5_scales), ("more", w6_codes, E4M3, w6_scales))):
+                plane = shared.tile([P, PASSES, N], U8, name=name + "_plane", offset=planes_at + PASSES * N * i, align_bytes=64)
+                nc.gpsimd.memset(plane[:].bitcast(I32), 0)
+                load_scale_rows(nc.sync, plane, rows)
+                for g in range(PASSES):
+                    last_weights[name, g] = (codes[:, g, :].bitcast(fmt), plane[:, g, :])
 
-        front(0)
-        front(1)
-        back(0)
-        prepare_up(1)
-        for s in range(STEPS):
-            c, h = divmod(s, 2)
-            if s + 2 < STEPS:
-                front(s + 2)
-            if s + 1 < STEPS:
-                back(s + 1)
-            if h == 0 and c + 2 < PAGES:
-                prepare_up(c + 2)
+        make_terms(0)
+        make_terms(1)
+        make_states(0)
+        prepare_page(1)
+        for s, (c, first, count) in enumerate(STEPS):
+            if s + 2 <= LAST_STEP:
+                make_terms(s + 2)
+            if s + 1 <= LAST_STEP:
+                make_states(s + 1)
+            if (first + count) * P == HALF and c + 2 < PAGES:
+                prepare_page(c + 2)
             scatter(s)
-            if s == 3 or s == 5:
-                prepare_w4((s - 3) // 2)
-            if s == 7:
-                load_packed()
-            if h == 1:
-                fetch(c)
-            if s == 7:
-                for mh in range(2):
-                    quantize_z(0, mh, 7, nc.scalar.copy)
+            if (first + count) * P == S:
+                if 1 <= c <= 2 * PASSES:
+                    round_w4(*divmod(c - 1, 2))
+                if c >= 1:
+                    place(c - 1, H_BANKS[min(s + 1, LAST_STEP) % 2])
+                if c == PASS_PAGES:
+                    load_w5_w6()
+                load_context(c)
+                if c < PAGES - 1:
+                    picks[c] = pick(c, 0, M)
+                if c == PASS_PAGES:
+                    for mh in range(2):
+                        quantize_z(0, mh, SPARE_BANKS[1])
+
+        last_page = PAGES - 1
+        halves = [pick(last_page, 2 * P * mh, 2 * P) for mh in range(2)]
+        quantize_w4()
+        for mh, picked in enumerate(halves):
+            z_bank = bank(SPARE_BANKS[mh], "z_bank")
+            add_transposed(blocks(z_bank)[:2], blocks(contexts[last_page])[2 * mh : 2 * mh + 2], blocks(picked))
+            round_z(last_page, mh, z_bank[:, 0 : 2 * P])
+            quantize_z(PASSES - 1, mh, SPARE_BANKS[mh])
 
         y_codes = keep.tile([P, M], U32, name="y_codes", align_bytes=64)
         y_plane = keep.tile([P, M], U8, name="y_plane", align_bytes=64)
-        out_rows = out_0.rearrange("(p t) m -> p t m", t=4)
+        out_rows = out_0.rearrange("(p t) m -> p t m", t=PACK)
         out_words = out_1[0].rearrange("p m t -> p (m t)").bitcast(I32)
-
-        def dealt(ap):
-            return ap.rearrange("m (p t) -> m t p", t=4)
-
-        def by_slot(ap):
-            return ap.rearrange("m (t p) -> m t p", t=4)
-
+        names = ("gate", "more", "base")
         sums = {}
+
+        def by_remainder(ap):
+            return ap.rearrange("m (p t) -> m t p", t=PACK)
+
+        def sorted_view(ap):
+            return ap.rearrange("m (t p) -> m t p", t=PACK)
 
         def multiply(q):
             mh, b = divmod(q, 2)
             cols = slice(b * P, (b + 1) * P)
-            sums[q] = [bank(3 * (q % 2) + i, "y_sum") for i in range(3)]
-            for g in range(2):
-                moving = (
-                    (packed["w5"][:, g, :].bitcast(E2M1), packed["s5"][:, g, :]),
-                    (packed["w6"][:, g, :].bitcast(E4M3), packed["s6"][:, g, :]),
-                    (w4_codes[g][:].bitcast(E4M3), w4_planes[g][:]),
+            sums[q] = {name: bank(len(names) * (q % 2) + i, "y_sum") for i, name in enumerate(names)}
+            if q < 2:
+                order = [(name, g) for g in range(PASSES) for name in names]
+            else:
+                order = [(name, g) for name in names for g in range(PASSES)]
+            for name, g in order:
+                codes, plane = last_weights[name, g]
+                nc.tensor.matmul_mx(
+                    out=sums[q][name][:], lhsT=z_codes[g, mh][:, cols].bitcast(E4M3), lhsT_scale=z_planes[g, mh][:, cols],
+                    rhs=codes, rhs_scale=plane, start=(g == 0), stop=(g == PASSES - 1),
                 )
-                for acc, (codes, plane) in zip(sums[q], moving):
-                    nc.tensor.matmul_mx(
-                        out=acc[:], lhsT=z_codes[g, mh][:, cols].bitcast(E4M3), lhsT_scale=z_planes[g, mh][:, cols],
-                        rhs=codes, rhs_scale=plane, start=(g == 0), stop=(g == 1),
-                    )
 
         def finish(q):
-            gate, more, base = sums[q]
             cols = slice(q * P, (q + 1) * P)
             opened = ring.tile([P, N], F32, name="opened")
-            nc.scalar.activation(by_slot(opened[:]), dealt(gate[:]), SIGMOID)
+            nc.scalar.activation(sorted_view(opened[:]), by_remainder(sums[q]["gate"][:]), SIGMOID)
             gated = ring.tile([P, N], F32, name="gated")
-            nc.vector.tensor_tensor(by_slot(gated[:]), dealt(more[:]), by_slot(opened[:]), MULT)
+            nc.vector.tensor_tensor(sorted_view(gated[:]), by_remainder(sums[q]["more"][:]), sorted_view(opened[:]), MULT)
             y_rows = ring.tile([P, N], F32, name="y_rows")
-            nc.vector.tensor_tensor(by_slot(y_rows[:]), dealt(base[:]), by_slot(gated[:]), ADD)
-            y_bank = bank(6 + q % 2, "y_bank")
-            for out, block in zip(blocks(y_bank), blocks(y_rows)):
-                nc.tensor.transpose(out, block, identity[:])
-            y_vals = ring.tile([P, 4, P], F32, name="y_vals")
+            nc.vector.tensor_tensor(sorted_view(y_rows[:]), by_remainder(sums[q]["base"][:]), sorted_view(gated[:]), ADD)
+            y_bank = bank(SPARE_BANKS[q % 2], "y_bank")
+            for turned, block in zip(blocks(y_bank), blocks(y_rows)):
+                nc.tensor.transpose(turned, block, identity[:])
+            y_vals = ring.tile([P, PACK, P], F32, name="y_vals")
             nc.scalar.copy(out=y_vals[:].rearrange("p t m -> p (t m)"), in_=y_bank[:])
             nc.sync.dma_start(out=out_rows[:, :, cols], in_=y_vals[:])
-            y_grouped = ring.tile([P, P, 4], BF16, name="y_grouped", align_bytes=64)
-            interleave(nc.vector.tensor_copy, y_grouped[:], y_vals[:])
+            y_grouped = ring.tile([P, P, PACK], BF16, name="y_grouped", align_bytes=64)
+            interleave(nc.scalar.copy if q < SCALAR_ROUNDS else nc.vector.tensor_copy, y_grouped[:], y_vals[:])
             nc.vector.quantize_mx(
                 out=y_codes[:, cols].bitcast(E4M3), scales=y_plane[:, cols],
                 in_=y_grouped[:].rearrange("p m t -> p (m t)"),
@@ -323,12 +364,12 @@ def tile_list_resumed_session_features_kernel(
             nc.sync.dma_start(out=out_words[:, cols], in_=y_codes[:, cols].bitcast(I32))
 
         multiply(0)
-        for q in range(4):
-            if q + 1 < 4:
+        for q in range(QUARTERS):
+            if q + 1 < QUARTERS:
                 multiply(q + 1)
             finish(q)
-        for q in range(4):
-            nc.scalar.dma_start(
-                out=out_2[0, 4 * q : 4 * q + 4, :].bitcast(I32),
-                in_=y_plane[32 * q : 32 * q + 4, :].bitcast(I32),
+        for quad in range(P // QUADRANT):
+            (nc.sync if quad % 2 == 0 else nc.scalar).dma_start(
+                out=out_2[0, 4 * quad : 4 * quad + 4, :].bitcast(I32),
+                in_=y_plane[QUADRANT * quad : QUADRANT * quad + 4, :].bitcast(I32),
             )

@@ -16,32 +16,29 @@ E4M3 = mybir.dt.float8_e4m3fn_x4
 E2M1 = mybir.dt.float4_e2m1fn_x4
 MULT = mybir.AluOpType.mult
 ADD = mybir.AluOpType.add
-SIGMOID = mybir.ActivationFunctionType.Sigmoid
+TANH = mybir.ActivationFunctionType.Tanh
 
 P = 128
 PACK = 4
 QUADRANT = 32
 STRIPE = 16
 BANK = 512
-BANK_BLOCKS = BANK // P
-PAGES = H // P
-PASSES = H // (P * PACK)
-PASS_PAGES = PAGES // PASSES
+PASS_ROWS = P * PACK
 HALF = S // 2
+PIECE = 256
 QUARTERS = M // P
-SCALAR_ROUNDS = 2
 
-STEPS = [(0, 0, 2), (0, 2, 2), (0, 4, 4)] + [(c, first, 4) for c in range(1, PAGES) for first in (0, 4)]
-LAST_STEP = len(STEPS) - 1
-
-B_BANK, D_BANK, A_BANKS, H_BANKS = 0, 2, (1, 5), (3, 4)
-SPARE_BANKS = (6, 7)
-
+FIRST_CHUNKS = [(0, 256, (0, 1, 2)), (256, 256, (3, 4, 5)), (512, 512, (6, 7, 3))]
+B_BANKS, A_BANK, D_BANK, H_BANKS, WORD_BANKS = (0, 3), 1, 2, (4, 5), (6, 7)
+SUM_BANKS = (0, 1, 2, 3, 6, 7, 4, 5)
+PLAIN_STEPS = 2 * (PACK - 1)
+STEPS = PLAIN_STEPS + S // P
+AHEAD = 2
+DEALT_STEPS = [((t, t + 1), start, PIECE) for start in (0, PIECE) for t in (0, 2)] + [((t,), HALF, HALF) for t in range(PACK)]
 KIB = 1024
-TABLE_AT = 0
-PLANE_AT = 16 * KIB
-FACTORS_AT = 20 * KIB
-LAST_STATES_AT = 32 * KIB
+TABLE_AT, LATE_RAW_AT, EARLY_RAW_AT, FIRST_AT, GROUPED_AT, CONTEXTS_AT, LAST_STATES_AT = [16 * KIB * i for i in range(7)]
+LAST_STATES_AT = CONTEXTS_AT + 8 * KIB
+W4_RAW_AT = LAST_STATES_AT + 4 * KIB
 
 
 def tile_list_resumed_session_features_kernel(
@@ -65,10 +62,11 @@ def tile_list_resumed_session_features_kernel(
         def entries(list_tile, start, count):
             return list_tile[:, start // STRIPE : (start + count) // STRIPE]
 
-        def load_scale_rows(queue, plane, rows):
+        def load_scale_rows(queue, plane, rows, shift=0):
             for quad in range(P // QUADRANT):
+                at = QUADRANT * quad + shift
                 queue.dma_start(
-                    out=plane[QUADRANT * quad : QUADRANT * quad + 4].bitcast(I32),
+                    out=plane[at : at + 4].bitcast(I32),
                     in_=rows[:, 4 * quad : 4 * quad + 4, :].rearrange("a q n -> q a n").bitcast(I32),
                 )
 
@@ -85,288 +83,411 @@ def tile_list_resumed_session_features_kernel(
             for i in range(n):
                 nc.tensor.matmul(sum_blocks[i], lhsT=late[i], rhs=identity[:], is_transpose=True, start=False, stop=(i == n - 1))
 
+        def quantize(name, grouped, width):
+            codes = keep.tile([P, width], U32, name=name + "_codes", align_bytes=64)
+            plane = keep.tile([P, width], U8, name=name + "_plane", align_bytes=64)
+            nc.vector.quantize_mx(out=codes[:].bitcast(E4M3), scales=plane[:], in_=grouped)
+            return codes, plane
+
+        w1_rows = w1.rearrange("(p t) r -> p t r", t=PACK)
+        w3_rows = w3.rearrange("(p t) r -> p t r", t=PACK)
+
+        def load_columns(name, rows, start, width, offset):
+            raw = shared.tile([P, PACK, width], F32, name=name, offset=offset)
+            nc.sync.dma_start(out=raw[:], in_=rows[:, :, start : start + width])
+            return raw
+
+        table_plane = keep.tile([P, 1, T], U8, name="table_plane")
+        nc.vector.memset(table_plane[:].bitcast(I32), 0)
+        w2_plane = keep.tile([P, 1, H], U8, name="w2_plane", align_bytes=64)
+        nc.vector.memset(w2_plane[:].bitcast(I32), 0)
+
         list1 = lists.tile([P, S // STRIPE], U16, name="list1")
         list2 = lists.tile([P, S // STRIPE], U16, name="list2")
         list3 = lists.tile([P, M // STRIPE], U16, name="list3")
         nc.sync.dma_start(list1[:], offs)
+        raw = {}
+        raw["w1", 0] = load_columns("w1_raw0", w1_rows, 0, P, EARLY_RAW_AT)
+        load_scale_rows(nc.sync, table_plane, tab_scales)
+        table = shared.tile([P, T], I32, name="table", offset=TABLE_AT)
+        nc.sync.dma_start(out=table[:], in_=tab_words[0].rearrange("p t i -> p (t i)").bitcast(I32))
+        w2_codes = keep.tile([P, 2 * H], U8, name="w2_codes", align_bytes=64)
+        nc.sync.dma_start(out=w2_codes[:].bitcast(I32), in_=w2_words[0].bitcast(I32))
+        load_scale_rows(nc.sync, w2_plane, w2_scales)
+        raw["w3", 0] = load_columns("w3_raw0", w3_rows, 0, P, EARLY_RAW_AT + 2 * KIB)
         nc.sync.dma_start(list2[:], offs2)
+        raw["w1", 1] = load_columns("w1_raw1", w1_rows, P, P, EARLY_RAW_AT + 4 * KIB)
+        raw["w3", 1] = load_columns("w3_raw1", w3_rows, P, P, EARLY_RAW_AT + 6 * KIB)
+        factors = [keep.tile([P, HALF], F32, name="factors%d" % h) for h in range(2)]
+        nc.sync.dma_start(out=factors[0][:], in_=wgs[:, 0:HALF])
+        nc.sync.dma_start(out=factors[1][:], in_=wgs[:, HALF:S])
         nc.sync.dma_start(list3[:], offs3)
+        raw["w1", 2] = load_columns("w1_raw2", w1_rows, 2 * P, 2 * P, EARLY_RAW_AT + 8 * KIB)
+        raw["w3", 2] = load_columns("w3_raw2", w3_rows, 2 * P, 2 * P, EARLY_RAW_AT + 12 * KIB)
+        raw["w1", 4] = load_columns("w1_raw4", w1_rows, PASS_ROWS, PASS_ROWS, LATE_RAW_AT)
+        raw["w3", 4] = load_columns("w3_raw4", w3_rows, PASS_ROWS, PASS_ROWS, LATE_RAW_AT + 8 * KIB)
+        plain_contexts = shared.tile([P, PACK, M], F32, name="plain_contexts", offset=CONTEXTS_AT)
+        nc.sync.dma_start(out=plain_contexts[:], in_=ctx[0:PASS_ROWS].rearrange("(c p) m -> p c m", p=P))
+        dealt_factors = keep.tile([P, PACK, S], F32, name="dealt_factors")
+        for quad in (0, 2, 1, 3):
+            nc.sync.dma_start(
+                out=dealt_factors[QUADRANT * quad : QUADRANT * (quad + 1)],
+                in_=wgs.rearrange("(q t) j -> q t j", t=PACK),
+            )
+        w4_rows = w4.rearrange("(g p t) n -> g p t n", p=P, t=PACK)
+        for g in range(2):
+            raw["w4", g] = load_columns("w4_raw%d" % g, w4_rows[g], 0, N, W4_RAW_AT + 8 * KIB * g)
+        dealt_contexts = shared.tile([P, PACK, M], F32, name="dealt_contexts", offset=EARLY_RAW_AT)
+        nc.sync.dma_start(out=dealt_contexts[:], in_=ctx[PASS_ROWS:H].rearrange("(p t) m -> p t m", t=PACK))
+        w6_raw = shared.tile([P, 2, N], I32, name="w6_raw", offset=EARLY_RAW_AT + 8 * KIB)
+        nc.sync.dma_start(out=w6_raw[:], in_=w6_words.rearrange("g p n t -> p g (n t)").bitcast(I32))
+        w5_raw = shared.tile([P, 2, N], U16, name="w5_raw", offset=EARLY_RAW_AT + 12 * KIB)
+        nc.sync.dma_start(out=w5_raw[:].bitcast(I32), in_=w5_words.rearrange("g p n -> p g n").bitcast(I32))
+        w56_raw_plane = keep.tile([P, 2, N], U8, name="w56_raw_plane")
+        nc.gpsimd.memset(w56_raw_plane[:].bitcast(I32), 0)
+        load_scale_rows(nc.sync, w56_raw_plane, w5_scales)
+        load_scale_rows(nc.sync, w56_raw_plane, w6_scales, shift=4)
 
-        table_plane = shared.tile([P, T], U8, name="table_plane", offset=PLANE_AT)
-        nc.vector.memset(table_plane[:].bitcast(I32), 0)
-        load_scale_rows(nc.scalar, table_plane[:].rearrange("p (a n) -> p a n", a=1), tab_scales)
-
-        w2_plane = keep.tile([P, 1, H], U8, name="w2_plane", align_bytes=64)
-        nc.gpsimd.memset(w2_plane[:].bitcast(I32), 0)
-        load_scale_rows(nc.gpsimd, w2_plane, w2_scales)
         identity = keep.tile([P, P], F32, name="identity")
         make_identity(nc, identity[:])
 
-        w1_rows = w1.rearrange("(p t) r -> p t r", t=PACK)
-        w3_rows = w3.rearrange("(p t) r -> p t r", t=PACK)
-        w13_codes = {}
-        w13_planes = {}
+        w13 = {}
 
-        def round_block(grouped, rows):
-            raw = ring.tile([P, PACK, P], F32, name="raw", bufs=4)
-            nc.sync.dma_start(out=raw[:], in_=rows)
-            interleave(nc.scalar.copy, grouped, raw[:])
+        def round_alone(name):
+            grouped = shared.tile([P, P, PACK], BF16, name=name + "_grouped0", align_bytes=64, offset=GROUPED_AT + KIB * (name == "w3"))
+            interleave(nc.scalar.copy, grouped[:], raw[name, 0][:])
+            w13[name, 0] = quantize(name + "_0", grouped[:].rearrange("p r t -> p (r t)"), P)
 
-        def prepare_page(c):
-            cols = slice(c * P, (c + 1) * P)
-            if c == 0:
-                grouped = shared.tile([P, 2, P, PACK], BF16, name="first_grouped", align_bytes=64, offset=FACTORS_AT)
-            else:
-                grouped = ring.tile([P, 2, P, PACK], BF16, name="w13_grouped", align_bytes=64)
-            for i, rows in enumerate((w1_rows, w3_rows)):
-                round_block(grouped[:, i], rows[:, :, cols])
-            w13_codes[c] = ring.tile([P, 2 * P], U32, name="w13_codes", align_bytes=64, bufs=3)
-            w13_planes[c] = ring.tile([P, 2 * P], U8, name="w13_plane", align_bytes=64, bufs=3)
-            nc.vector.quantize_mx(
-                out=w13_codes[c][:].bitcast(E4M3),
-                scales=w13_planes[c][:],
-                in_=grouped[:].rearrange("p w r t -> p (w r t)"),
-            )
+        w13_grouped = {}
 
-        prepare_page(0)
-        w2_codes = keep.tile([P, 2 * H], U8, name="w2_codes", align_bytes=64)
-        nc.sync.dma_start(out=w2_codes[:].bitcast(I32), in_=w2_words[0].bitcast(I32))
-        table = shared.tile([P, T], I32, name="table", offset=TABLE_AT)
-        nc.sync.dma_start(out=table[:], in_=tab_words[0].rearrange("p t i -> p (t i)").bitcast(I32))
-        factors = shared.tile([P, S], F32, name="factors", offset=FACTORS_AT)
-        nc.sync.dma_start(out=factors[:], in_=wgs)
+        def round_piece(first, width, at, piece):
+            if at == 0:
+                w13_grouped[first] = shared.tile(
+                    [P, 2, width, PACK], BF16, name="w13_grouped%d" % first, align_bytes=64, offset=GROUPED_AT + 2 * KIB * first,
+                )
+            for i, name in enumerate(("w1", "w3")):
+                interleave(nc.scalar.copy, w13_grouped[first][:, i, at : at + piece], raw[name, first][:, :, at : at + piece])
 
+        def round_both(first, width):
+            round_piece(first, width, 0, width)
+            quantize_both(first, width)
+
+        def quantize_both(first, width):
+            grouped = w13_grouped[first]
+            codes, plane = quantize("w13_%d" % first, grouped[:].rearrange("p w r t -> p (w r t)"), 2 * width)
+            for i, name in enumerate(("w1", "w3")):
+                w13[name, first] = (codes[:, i * width : (i + 1) * width], plane[:, i * width : (i + 1) * width])
+
+        round_alone("w1")
+        v_codes = [keep.tile([P, HALF], U32, name="v_codes%d" % h, align_bytes=64) for h in range(2)]
+        v_planes = [keep.tile([P, HALF], U8, name="v_plane%d" % h, align_bytes=64) for h in range(2)]
+        for h in range(2):
+            nc.vector.tensor_copy(v_planes[h][:], table_plane[:, 0, :].indirect(entries(list1, h * HALF, HALF)))
+        for h in range(2):
+            nc.vector.tensor_copy(v_codes[h][:], table[:].bitcast(U32).indirect(entries(list1, h * HALF, HALF)))
+        round_alone("w3")
         pages = [keep.tile([P, T2], F32, name="page%d" % i) for i in range(2)]
         for page in pages:
             nc.vector.memset(page[:], 0.0)
+        for i in range(2):
+            page = shared.tile([P, T2], F32, name="late_page%d" % i, offset=TABLE_AT + 4 * T2 * i)
+            for at in range(0, T2, BANK):
+                nc.gpsimd.memset(page[:, at : at + BANK], 0.0)
+            pages.append(page)
+        dealt_pages = pages[2:] + pages[:2]
 
-        v_codes = [
-            shared.tile([P, HALF], U32, name="v_codes%d" % h, align_bytes=64, offset=PLANE_AT + 4 * HALF * h)
-            for h in range(2)
-        ]
-        v_planes = [keep.tile([P, HALF], U8, name="v_plane%d" % h, align_bytes=64) for h in range(2)]
-        for h in range(2):
-            nc.vector.tensor_copy(v_planes[h][:], table_plane[:].indirect(entries(list1, h * HALF, HALF)))
-        for h in range(2):
-            nc.vector.tensor_copy(v_codes[h][:], table[:].bitcast(U32).indirect(entries(list1, h * HALF, HALF)))
+        def w2_columns(start, width):
+            return w2_codes[:, 2 * start : 2 * (start + width)].bitcast(E2M1), w2_plane[:, 0, start : start + width]
+
+        def w13_columns(name, start, width):
+            first = max(c for (w, c) in w13 if w == name and c * P <= start)
+            codes, plane = w13[name, first]
+            at = start - first * P
+            return codes[:, at : at + width].bitcast(E4M3), plane[:, at : at + width]
+
+        chunk_terms = []
+        for start, count, (b_at, a_at, d_at) in FIRST_CHUNKS:
+            h, at = divmod(start, HALF)
+            banks = [bank(i, "first_terms") for i in (b_at, a_at, d_at)]
+            weights = (w2_columns(0, P), w13_columns("w1", 0, P), w13_columns("w3", 0, P))
+            for term_bank, (codes, plane) in zip(banks, weights):
+                nc.tensor.matmul_mx(
+                    out=term_bank[:, 0:count], lhsT=codes, lhsT_scale=plane,
+                    rhs=v_codes[h][:, at : at + count].bitcast(E4M3), rhs_scale=v_planes[h][:, at : at + count],
+                    start=True, stop=True,
+                )
+            b_vals = shared.tile([P, count], F32, name="first_b%d" % start, offset=FIRST_AT + 4 * start)
+            nc.scalar.copy(out=b_vals[:], in_=banks[0][:, 0:count])
+            chunk_terms.append((banks, b_vals))
+
+        def first_product(i):
+            banks, b_vals = chunk_terms[i]
+            count = FIRST_CHUNKS[i][1]
+            product = shared.tile([P, count], F32, name="first_ab%d" % i, offset=FIRST_AT + 4 * (S + FIRST_CHUNKS[i][0]))
+            nc.vector.tensor_tensor(product[:], banks[1][:, 0:count], b_vals[:], MULT)
+            return product
+
+        def first_state(i, product):
+            count = FIRST_CHUNKS[i][1]
+            at = GROUPED_AT + 2 * KIB if i == 1 else FIRST_AT + 4 * (2 * S + FIRST_CHUNKS[i][0])
+            state = shared.tile([P, count], F32, name="first_h%d" % i, offset=at)
+            nc.vector.tensor_tensor(state[:], chunk_terms[i][0][2][:, 0:count], product[:], ADD)
+            return state
+
+        def fused_scatter(i, state):
+            start, count, unused = FIRST_CHUNKS[i]
+            nc.vector.tensor_tensor(
+                pages[0][:].indirect(entries(list2, start, count)), state[:], factors[0][:, start : start + count], MULT,
+            )
+
+        early = [first_product(i) for i in range(2)]
+        fused_scatter(0, first_state(0, early[0]))
+        round_both(1, P)
+        second = first_state(1, early[1])
+        late = first_product(2)
+        fused_scatter(1, second)
+        late = first_state(2, late)
+        round_both(2, 2 * P)
+        weighted_late = shared.tile([P, HALF], F32, name="first_weighted", offset=FIRST_AT + 4 * 3 * S)
+        nc.vector.tensor_tensor(weighted_late[:], late[:], factors[1][:], MULT)
+        nc.vector.tensor_copy(pages[0][:].indirect(entries(list2, HALF, HALF)), weighted_late[:])
 
         products = {}
         addends = {}
         states = {}
 
-        def make_terms(s):
-            c, first, count = STEPS[s]
-            h, at = divmod(first, BANK_BLOCKS)
-            width = count * P
-            b_bank, a_bank, d_bank = [bank(i, "terms") for i in (B_BANK, A_BANKS[s % 2], D_BANK)]
-            moving = (
-                (b_bank, w2_codes[:, 2 * P * c : 2 * P * (c + 1)].bitcast(E2M1), w2_plane[:, 0, P * c : P * (c + 1)]),
-                (a_bank, w13_codes[c][:, 0:P].bitcast(E4M3), w13_planes[c][:, 0:P]),
-                (d_bank, w13_codes[c][:, P : 2 * P].bitcast(E4M3), w13_planes[c][:, P : 2 * P]),
-            )
-            v_blocks = blocks(v_codes[h])[at : at + count]
-            v_scales = blocks(v_planes[h])[at : at + count]
-            for term_bank, codes, plane in moving:
-                for term_block, v_block, v_scale in zip(blocks(term_bank), v_blocks, v_scales):
+        def make_terms(u):
+            banks = [bank(i, "terms") for i in (B_BANKS[u % 2], A_BANK, D_BANK)]
+            if u < PLAIN_STEPS:
+                c, h = divmod(u + 2, 2)
+                start, width = c * P, P
+                v_blocks = list(zip(blocks(v_codes[h]), blocks(v_planes[h])))
+            else:
+                h, at = divmod(u - PLAIN_STEPS, PACK)
+                start, width = PASS_ROWS, PASS_ROWS
+                v_blocks = [(blocks(v_codes[h])[at], blocks(v_planes[h])[at])]
+            weights = (w2_columns(start, width), w13_columns("w1", start, width), w13_columns("w3", start, width))
+            for term_bank, (codes, plane) in zip(banks, weights):
+                for i, (v_block, v_scale) in enumerate(v_blocks):
                     nc.tensor.matmul_mx(
-                        out=term_block, lhsT=v_block.bitcast(E4M3), lhsT_scale=v_scale,
+                        out=term_bank[:, i * width : (i + 1) * width], lhsT=v_block.bitcast(E4M3), lhsT_scale=v_scale,
                         rhs=codes, rhs_scale=plane, start=True, stop=True,
                     )
-            b_vals = ring.tile([P, width], F32, name="b_vals", bufs=3)
-            nc.scalar.copy(out=b_vals[:], in_=b_bank[:, 0:width])
-            products[s] = ring.tile([P, width], F32, name="ab_vals", bufs=3)
-            nc.vector.tensor_tensor(products[s][:], a_bank[:, 0:width], b_vals[:], MULT)
-            addends[s] = ring.tile([P, width], F32, name="d_vals", bufs=3)
-            nc.scalar.copy(out=addends[s][:], in_=d_bank[:, 0:width])
+
+            def copy_out(name, term_bank, bufs):
+                vals = ring.tile([P, BANK], F32, name=name, bufs=bufs)
+                if u < PLAIN_STEPS:
+                    nc.scalar.copy(out=vals[:], in_=term_bank[:])
+                else:
+                    nc.scalar.copy(
+                        out=vals[:].rearrange("j (t p) -> j t p", t=PACK),
+                        in_=term_bank[:].rearrange("j (p t) -> j t p", t=PACK),
+                    )
+                return vals
+
+            b_vals = copy_out("b_vals", banks[0], 3)
+            a_vals = copy_out("a_vals", banks[1], 3)
+            addends[u] = copy_out("d_vals", banks[2], 7)
+            products[u] = ring.tile([P, BANK], F32, name="ab_vals", bufs=7)
+            nc.gpsimd.tensor_tensor(products[u][:], a_vals[:], b_vals[:], MULT)
 
         def make_states(s):
-            h_bank = bank(H_BANKS[s % 2], "h_bank")
-            count = STEPS[s][2]
-            add_transposed(blocks(h_bank)[:count], blocks(addends[s]), blocks(products[s]))
-            if s == LAST_STEP:
-                states[s] = shared.tile([P, count * P], F32, name="last_states", offset=LAST_STATES_AT)
+            if s < PLAIN_STEPS:
+                make_terms(s)
+                early_blocks, late_blocks = blocks(addends[s]), blocks(products[s])
+                factor = factors[s % 2][:].rearrange("p (i j) -> p i j", i=2)
             else:
-                states[s] = ring.tile([P, count * P], F32, name="states", bufs=4)
-            nc.scalar.copy(out=states[s][:], in_=h_bank[:, 0 : count * P])
+                ts, start, count = DEALT_STEPS[s - PLAIN_STEPS]
+                units = range(PLAIN_STEPS + start // P, PLAIN_STEPS + (start + count) // P)
+                for u in units:
+                    if u not in products:
+                        make_terms(u)
+                early_blocks = [blocks(addends[u])[t] for t in ts for u in units]
+                late_blocks = [blocks(products[u])[t] for t in ts for u in units]
+                factor = dealt_factors[:, ts[0] : ts[-1] + 1, start : start + count]
+                if len(ts) == 1:
+                    factor = factor.rearrange("p o (i j) -> p (o i) j", i=2)
+            h_bank = bank(H_BANKS[s % 2], "h_bank")
+            add_transposed(blocks(h_bank), early_blocks, late_blocks)
+            plain = ring.tile([P, BANK], F32, name="h_vals", bufs=3)
+            nc.scalar.copy(out=plain[:], in_=h_bank[:])
+            if s == STEPS - 1:
+                states[s] = shared.tile([P, BANK], F32, name="last_states", offset=LAST_STATES_AT)
+            else:
+                states[s] = ring.tile([P, BANK], F32, name="states", bufs=3)
+            nc.gpsimd.tensor_tensor(
+                states[s][:].rearrange("p (i j) -> p i j", i=2), plain[:].rearrange("p (i j) -> p i j", i=2), factor, MULT,
+            )
 
         def scatter(s):
-            c, first, count = STEPS[s]
-            nc.vector.tensor_tensor(
-                pages[c % 2][:].indirect(entries(list2, first * P, count * P)),
-                states[s][:], factors[:, first * P : (first + count) * P], MULT,
-            )
+            ts, start, count = DEALT_STEPS[s - PLAIN_STEPS]
+            for i, t in enumerate(ts):
+                nc.vector.tensor_copy(
+                    dealt_pages[t][:].indirect(entries(list2, start, count)), states[s][:, i * count : (i + 1) * count],
+                )
 
-        z_rows = {
-            (g, mh): keep.tile([P, 2, 2, P, 2], BF16, name="z_rows%d%d" % (g, mh))
-            for g in range(PASSES) for mh in range(2)
-        }
-        z_codes = {}
-        z_planes = {}
-        ctx_rows = ctx.rearrange("(c p) m -> c p m", p=P)
-        contexts = {}
+        z_rows = shared.tile([P, QUARTERS, 2, P, 2], BF16, name="z_rows", offset=GROUPED_AT)
         picks = {}
 
-        def round_z(c, mh, z_blocks):
-            g, cc = divmod(c, PASS_PAGES)
-            words = P // PACK
-            nc.scalar.copy(
-                out=z_rows[g, mh][:, :, :, words * cc : words * (cc + 1), :],
-                in_=z_blocks.rearrange("m (b p u e) -> m b u p e", b=2, u=2, e=2),
-            )
-
-        def load_context(c):
-            contexts[c] = shared.tile([P, M], F32, name="context%d" % c, offset=TABLE_AT + 4 * M * c)
-            nc.sync.dma_start(out=contexts[c][:], in_=ctx_rows[c])
-
-        def pick(c, start, count):
-            picked = ring.tile([P, count], F32, name="picked", bufs=3)
-            nc.vector.tensor_copy(picked[:], pages[c % 2][:].indirect(entries(list3, start, count)))
-            return picked
+        def pick(c):
+            picks[c] = ring.tile([P, M], F32, name="picked", bufs=3)
+            nc.vector.tensor_copy(picks[c][:], pages[c % 2][:].indirect(list3[:]))
 
         def place(c, bank_index):
             z_bank = bank(bank_index, "z_bank")
-            add_transposed(blocks(z_bank), blocks(contexts[c]), blocks(picks[c]))
-            for mh in range(2):
-                round_z(c, mh, z_bank[:, 2 * P * mh : 2 * P * (mh + 1)])
-
-        def quantize_z(g, mh, bank_index):
-            z_words = z_rows[g, mh][:].rearrange("m b u p e -> m (b u p e)").bitcast(F32)
-            word_bank = bank(bank_index, "word_bank")
-            for turned, block in zip(blocks(word_bank), blocks(z_words)):
-                nc.tensor.transpose(turned, block, identity[:])
-            grouped = ring.tile([P, 2 * P * PACK], BF16, name="z_grouped", align_bytes=64)
+            add_transposed(blocks(z_bank), blocks(plain_contexts[:, c, :]), blocks(picks[c]))
+            words = P // PACK
             nc.scalar.copy(
-                out=grouped[:].bitcast(F32).rearrange("p (b m u) -> p b m u", b=2, u=2),
-                in_=word_bank[:].rearrange("p (b u m) -> p b m u", b=2, u=2),
+                out=z_rows[:, :, :, words * c : words * (c + 1), :],
+                in_=z_bank[:].rearrange("m (b p u e) -> m b u p e", b=QUARTERS, u=2, e=2),
             )
-            z_codes[g, mh] = keep.tile([P, 2 * P], U32, name="z_codes%d%d" % (g, mh), align_bytes=64)
-            z_planes[g, mh] = keep.tile([P, 2 * P], U8, name="z_plane%d%d" % (g, mh), align_bytes=64)
-            nc.vector.quantize_mx(out=z_codes[g, mh][:].bitcast(E4M3), scales=z_planes[g, mh][:], in_=grouped[:])
 
-        w4_rows = w4.rearrange("(g p t) n -> g p t n", p=P, t=PACK)
+        def quantize_first_pass():
+            z_words = blocks(z_rows[:].rearrange("m b u p e -> m (b u p e)").bitcast(F32))
+            grouped = shared.tile([P, 2, 2 * P * PACK], BF16, name="z_grouped0", align_bytes=64, offset=GROUPED_AT + 4 * KIB)
+            for mh in range(2):
+                word_bank = bank(WORD_BANKS[mh], "word_bank")
+                for turned, block in zip(blocks(word_bank), z_words[4 * mh : 4 * mh + 4]):
+                    nc.tensor.transpose(turned, block, identity[:])
+                nc.scalar.copy(
+                    out=grouped[:, mh, :].bitcast(F32).rearrange("p (b m u) -> p b m u", b=2, u=2),
+                    in_=word_bank[:].rearrange("p (b u m) -> p b m u", b=2, u=2),
+                )
+            return quantize("z0", grouped[:].rearrange("p h c -> p (h c)"), M)
+
         w4_grouped = {}
-        last_weights = {}
 
         def round_w4(g, half):
             if half == 0:
-                w4_grouped[g] = keep.tile([P, N, PACK], BF16, name="w4_grouped%d" % g, align_bytes=64)
-            for i in (2 * half, 2 * half + 1):
-                cols = slice(i * P, (i + 1) * P)
-                round_block(w4_grouped[g][:, cols], w4_rows[g][:, :, cols])
+                w4_grouped[g] = shared.tile([P, PACK, P, PACK], BF16, name="w4_grouped%d" % g, align_bytes=64, offset=LATE_RAW_AT + 4 * KIB * g)
+            qs = slice(half * P // 2, (half + 1) * P // 2)
+            nc.scalar.copy(
+                out=w4_grouped[g][:].rearrange("p t q i -> p q t i")[:, qs],
+                in_=raw["w4", g][:].rearrange("p i (q t) -> p q t i", t=PACK)[:, qs],
+            )
 
-        def quantize_w4():
-            codes = shared.tile([P, PASSES, N], U32, name="w4_codes", align_bytes=64, offset=LAST_STATES_AT)
-            for g in range(PASSES):
-                plane = keep.tile([P, N], U8, name="w4_plane%d" % g, align_bytes=64)
-                nc.vector.quantize_mx(
-                    out=codes[:, g, :].bitcast(E4M3), scales=plane[:],
-                    in_=w4_grouped[g][:].rearrange("p n t -> p (n t)"),
+        w6_codes = shared.tile([P, 2, N], I32, name="w6_codes", align_bytes=64, offset=CONTEXTS_AT)
+        w5_codes = shared.tile([P, 2, N], U16, name="w5_codes", align_bytes=64, offset=CONTEXTS_AT + 4 * KIB)
+        w56_plane = shared.tile([P, 2, N], U8, name="w56_plane", align_bytes=64, offset=CONTEXTS_AT + 6 * KIB)
+
+        def deal(engine_copy, dealt, plain, g):
+            engine_copy(
+                out=dealt[:, g, :].rearrange("p (t q) -> p t q", t=PACK),
+                in_=plain[:, g, :].rearrange("p (q t) -> p t q", t=PACK),
+            )
+
+        pick(0)
+        for s in range(AHEAD):
+            make_states(s)
+        picked = shared.tile([P, PACK, M], F32, name="z_vals", offset=LATE_RAW_AT + 8 * KIB)
+
+        def pick_add(t, start, count):
+            nc.vector.tensor_tensor(
+                picked[:, t, start : start + count], dealt_pages[t][:].indirect(entries(list3, start, count)),
+                dealt_contexts[:, t, start : start + count], ADD,
+            )
+
+        for s in range(STEPS):
+            if s + AHEAD < STEPS:
+                make_states(s + AHEAD)
+            if s < 2:
+                round_piece(PACK, PASS_ROWS, s * 2 * P, 2 * P)
+            if s == 2:
+                quantize_both(PACK, PASS_ROWS)
+            if s < PLAIN_STEPS:
+                c, h = divmod(s + 2, 2)
+                nc.vector.tensor_copy(pages[c % 2][:].indirect(entries(list2, h * HALF, HALF)), states[s][:])
+                if h == 1:
+                    pick(c)
+            else:
+                scatter(s)
+                t = s - (STEPS - PACK)
+                if 0 <= t < PACK - 1:
+                    plain_pick = ring.tile([P, M], F32, name="picked", bufs=3)
+                    nc.vector.tensor_copy(plain_pick[:], dealt_pages[t][:].indirect(list3[:]))
+                    nc.gpsimd.tensor_tensor(picked[:, t, :], plain_pick[:], dealt_contexts[:, t, :], ADD)
+            if s % 2 == 1 and s // 2 < PACK:
+                place(s // 2, H_BANKS[(s + AHEAD) % 2])
+            if s == PLAIN_STEPS + 2:
+                z0_codes, z0_plane = quantize_first_pass()
+            if PLAIN_STEPS <= s < PLAIN_STEPS + 4:
+                round_w4(*divmod(s - PLAIN_STEPS, 2))
+            if s == PLAIN_STEPS + 4:
+                for g in range(2):
+                    deal(nc.gpsimd.tensor_copy, w6_codes, w6_raw, g)
+                    deal(nc.gpsimd.tensor_copy, w56_plane, w56_raw_plane, g)
+                    deal(nc.vector.tensor_copy, w5_codes, w5_raw, g)
+
+        z1 = {}
+        for q in range(QUARTERS):
+            pick_add(PACK - 1, q * P, P)
+        for q in range(QUARTERS):
+            grouped = shared.tile([P, P, PACK], BF16, name="z_grouped1%d" % q, align_bytes=64, offset=GROUPED_AT + KIB * (8 + q))
+            interleave(nc.scalar.copy, grouped[:], picked[:, :, q * P : (q + 1) * P])
+            z1[q] = quantize("z1%d" % q, grouped[:].rearrange("p m t -> p (m t)"), P)
+        w4_codes = shared.tile([P, 2, N], U32, name="w4_codes", align_bytes=64, offset=LAST_STATES_AT)
+        w4_plane = keep.tile([P, 2, N], U8, name="w4_plane", align_bytes=64)
+        for g in range(2):
+            nc.vector.quantize_mx(
+                out=w4_codes[:, g, :].bitcast(E4M3), scales=w4_plane[:, g, :],
+                in_=w4_grouped[g][:].rearrange("p t q i -> p (t q i)"),
+            )
+
+        def stationary(name, g, t):
+            cols = slice(t * P, (t + 1) * P)
+            if name == "gate":
+                return w5_codes[:, g, cols].bitcast(U8).bitcast(E2M1), w56_plane[:, g, cols]
+            if name == "more":
+                return w6_codes[:, g, cols].bitcast(E4M3), w56_plane[4:P, g, cols]
+            return w4_codes[:, g, cols].bitcast(E4M3), w4_plane[:, g, cols]
+
+        names = ("gate", "more", "base")
+        slots = [(q, name) for q in range(QUARTERS) for name in names]
+        sums = {}
+
+        def multiply(q, name, g):
+            if g == 0:
+                sums[q, name] = bank(SUM_BANKS[slots.index((q, name)) % len(SUM_BANKS)], "y_sum")
+                z_codes, z_plane = z0_codes[:, q * P : (q + 1) * P], z0_plane[:, q * P : (q + 1) * P]
+            else:
+                z_codes, z_plane = z1[q][0][:], z1[q][1][:]
+            for t, block in enumerate(blocks(sums[q, name])):
+                codes, plane = stationary(name, g, t)
+                nc.tensor.matmul_mx(
+                    out=block, lhsT=codes, lhsT_scale=plane, rhs=z_codes.bitcast(E4M3), rhs_scale=z_plane,
+                    start=(g == 0 and t == 0), stop=(g == 1 and t == PACK - 1),
                 )
-                last_weights["base", g] = (codes[:, g, :].bitcast(E4M3), plane[:])
-
-        def load_w5_w6():
-            w5_at = TABLE_AT + 4 * PASSES * N
-            planes_at = w5_at + 2 * PASSES * N
-            w6_codes = shared.tile([P, PASSES, N], U32, name="w6_codes", offset=TABLE_AT, align_bytes=64)
-            nc.sync.dma_start(out=w6_codes[:].bitcast(I32), in_=w6_words.rearrange("g p n t -> p g (n t)").bitcast(I32))
-            w5_codes = shared.tile([P, PASSES, 2 * N], U8, name="w5_codes", offset=w5_at, align_bytes=64)
-            nc.sync.dma_start(out=w5_codes[:].bitcast(I32), in_=w5_words.rearrange("g p n -> p g n").bitcast(I32))
-            for i, (name, codes, fmt, rows) in enumerate((("gate", w5_codes, E2M1, w5_scales), ("more", w6_codes, E4M3, w6_scales))):
-                plane = shared.tile([P, PASSES, N], U8, name=name + "_plane", offset=planes_at + PASSES * N * i, align_bytes=64)
-                nc.gpsimd.memset(plane[:].bitcast(I32), 0)
-                load_scale_rows(nc.sync, plane, rows)
-                for g in range(PASSES):
-                    last_weights[name, g] = (codes[:, g, :].bitcast(fmt), plane[:, g, :])
-
-        make_terms(0)
-        make_terms(1)
-        make_states(0)
-        prepare_page(1)
-        for s, (c, first, count) in enumerate(STEPS):
-            if s + 2 <= LAST_STEP:
-                make_terms(s + 2)
-            if s + 1 <= LAST_STEP:
-                make_states(s + 1)
-            if (first + count) * P == HALF and c + 2 < PAGES:
-                prepare_page(c + 2)
-            scatter(s)
-            if (first + count) * P == S:
-                if 1 <= c <= 2 * PASSES:
-                    round_w4(*divmod(c - 1, 2))
-                if c >= 1:
-                    place(c - 1, H_BANKS[min(s + 1, LAST_STEP) % 2])
-                if c == PASS_PAGES:
-                    load_w5_w6()
-                load_context(c)
-                if c < PAGES - 1:
-                    picks[c] = pick(c, 0, M)
-                if c == PASS_PAGES:
-                    for mh in range(2):
-                        quantize_z(0, mh, SPARE_BANKS[1])
-
-        last_page = PAGES - 1
-        halves = [pick(last_page, 2 * P * mh, 2 * P) for mh in range(2)]
-        quantize_w4()
-        for mh, picked in enumerate(halves):
-            z_bank = bank(SPARE_BANKS[mh], "z_bank")
-            add_transposed(blocks(z_bank)[:2], blocks(contexts[last_page])[2 * mh : 2 * mh + 2], blocks(picked))
-            round_z(last_page, mh, z_bank[:, 0 : 2 * P])
-            quantize_z(PASSES - 1, mh, SPARE_BANKS[mh])
 
         y_codes = keep.tile([P, M], U32, name="y_codes", align_bytes=64)
         y_plane = keep.tile([P, M], U8, name="y_plane", align_bytes=64)
         out_rows = out_0.rearrange("(p t) m -> p t m", t=PACK)
         out_words = out_1[0].rearrange("p m t -> p (m t)").bitcast(I32)
-        names = ("gate", "more", "base")
-        sums = {}
-
-        def by_remainder(ap):
-            return ap.rearrange("m (p t) -> m t p", t=PACK)
-
-        def sorted_view(ap):
-            return ap.rearrange("m (t p) -> m t p", t=PACK)
-
-        def multiply(q):
-            mh, b = divmod(q, 2)
-            cols = slice(b * P, (b + 1) * P)
-            sums[q] = {name: bank(len(names) * (q % 2) + i, "y_sum") for i, name in enumerate(names)}
-            if q < 2:
-                order = [(name, g) for g in range(PASSES) for name in names]
-            else:
-                order = [(name, g) for name in names for g in range(PASSES)]
-            for name, g in order:
-                codes, plane = last_weights[name, g]
-                nc.tensor.matmul_mx(
-                    out=sums[q][name][:], lhsT=z_codes[g, mh][:, cols].bitcast(E4M3), lhsT_scale=z_planes[g, mh][:, cols],
-                    rhs=codes, rhs_scale=plane, start=(g == 0), stop=(g == PASSES - 1),
-                )
 
         def finish(q):
             cols = slice(q * P, (q + 1) * P)
-            opened = ring.tile([P, N], F32, name="opened")
-            nc.scalar.activation(sorted_view(opened[:]), by_remainder(sums[q]["gate"][:]), SIGMOID)
-            gated = ring.tile([P, N], F32, name="gated")
-            nc.vector.tensor_tensor(sorted_view(gated[:]), by_remainder(sums[q]["more"][:]), sorted_view(opened[:]), MULT)
-            y_rows = ring.tile([P, N], F32, name="y_rows")
-            nc.vector.tensor_tensor(sorted_view(y_rows[:]), by_remainder(sums[q]["base"][:]), sorted_view(gated[:]), ADD)
-            y_bank = bank(SPARE_BANKS[q % 2], "y_bank")
-            for turned, block in zip(blocks(y_bank), blocks(y_rows)):
-                nc.tensor.transpose(turned, block, identity[:])
-            y_vals = ring.tile([P, PACK, P], F32, name="y_vals")
-            nc.scalar.copy(out=y_vals[:].rearrange("p t m -> p (t m)"), in_=y_bank[:])
+            opened = shared.tile([P, BANK], F32, name="opened%d" % q, offset=FIRST_AT + 2 * KIB * (q % 2))
+            nc.scalar.activation(opened[:], sums[q, "gate"][:], TANH, scale=0.5)
+            gated = shared.tile([P, BANK], F32, name="gated%d" % q, offset=FIRST_AT + 2 * KIB * (2 + q % 2))
+            nc.vector.scalar_tensor_tensor(gated[:], opened[:], 1.0, sums[q, "more"][:], ADD, MULT)
+            y_vals = shared.tile([P, PACK, P], F32, name="y_vals%d" % q, offset=FIRST_AT + 2 * KIB * (4 + q))
+            nc.vector.scalar_tensor_tensor(y_vals[:].rearrange("p t m -> p (t m)"), gated[:], 0.5, sums[q, "base"][:], MULT, ADD)
             nc.sync.dma_start(out=out_rows[:, :, cols], in_=y_vals[:])
             y_grouped = ring.tile([P, P, PACK], BF16, name="y_grouped", align_bytes=64)
-            interleave(nc.scalar.copy if q < SCALAR_ROUNDS else nc.vector.tensor_copy, y_grouped[:], y_vals[:])
+            interleave(nc.scalar.copy if q < QUARTERS - 1 else nc.vector.tensor_copy, y_grouped[:], y_vals[:])
             nc.vector.quantize_mx(
                 out=y_codes[:, cols].bitcast(E4M3), scales=y_plane[:, cols],
                 in_=y_grouped[:].rearrange("p m t -> p (m t)"),
             )
             nc.sync.dma_start(out=out_words[:, cols], in_=y_codes[:, cols].bitcast(I32))
 
-        multiply(0)
+        early_slots = slots[: len(SUM_BANKS)]
+        for q, name in early_slots:
+            multiply(q, name, 0)
         for q in range(QUARTERS):
-            if q + 1 < QUARTERS:
-                multiply(q + 1)
+            for name in names:
+                if (q, name) not in early_slots:
+                    multiply(q, name, 0)
+                multiply(q, name, 1)
             finish(q)
         for quad in range(P // QUADRANT):
             (nc.sync if quad % 2 == 0 else nc.scalar).dma_start(

@@ -38,7 +38,7 @@ DEALT_STEPS = [((t, t + 1), start, PIECE) for start in (0, PIECE) for t in (0, 2
 KIB = 1024
 TABLE_AT, LATE_RAW_AT, EARLY_RAW_AT, FIRST_AT, GROUPED_AT, CONTEXTS_AT, LAST_STATES_AT = [16 * KIB * i for i in range(7)]
 LAST_STATES_AT = CONTEXTS_AT + 8 * KIB
-W4_RAW_AT = LAST_STATES_AT + 4 * KIB
+W4_RAW_AT = TABLE_AT
 
 
 def tile_list_resumed_session_features_kernel(
@@ -186,14 +186,9 @@ def tile_list_resumed_session_features_kernel(
         for h in range(2):
             nc.vector.tensor_copy(v_codes[h][:], table[:].bitcast(U32).indirect(entries(list1, h * HALF, HALF)))
         round_alone("w3")
-        pages = [keep.tile([P, T2], F32, name="page%d" % i) for i in range(2)]
+        pages = [keep.tile([P, T2], F32, name="page%d" % i) for i in range(PACK)]
         for page in pages:
-            nc.vector.memset(page[:], 0.0)
-        for i in range(2):
-            page = shared.tile([P, T2], F32, name="late_page%d" % i, offset=TABLE_AT + 4 * T2 * i)
-            for at in range(0, T2, BANK):
-                nc.gpsimd.memset(page[:, at : at + BANK], 0.0)
-            pages.append(page)
+            nc.vector.memset(page[:].bitcast(I32), 0)
         dealt_pages = pages[2:] + pages[:2]
 
         def w2_columns(start, width):
@@ -414,8 +409,8 @@ def tile_list_resumed_session_features_kernel(
                 round_w4(*divmod(s - PLAIN_STEPS, 2))
             if s == PLAIN_STEPS + 4:
                 for g in range(2):
-                    deal(nc.gpsimd.tensor_copy, w6_codes, w6_raw, g)
-                    deal(nc.gpsimd.tensor_copy, w56_plane, w56_raw_plane, g)
+                    deal(nc.vector.tensor_copy, w6_codes, w6_raw, g)
+                    deal(nc.vector.tensor_copy, w56_plane, w56_raw_plane, g)
                     deal(nc.vector.tensor_copy, w5_codes, w5_raw, g)
 
         z1 = {}

@@ -36,9 +36,23 @@ STEPS = PLAIN_STEPS + S // P
 AHEAD = 2
 DEALT_STEPS = [((t, t + 1), start, PIECE) for start in (0, PIECE) for t in (0, 2)] + [((t,), HALF, HALF) for t in range(PACK)]
 KIB = 1024
-TABLE_AT, LATE_RAW_AT, EARLY_RAW_AT, FIRST_AT, GROUPED_AT, CONTEXTS_AT, LAST_STATES_AT = [16 * KIB * i for i in range(7)]
-LAST_STATES_AT = CONTEXTS_AT + 8 * KIB
-W4_RAW_AT = TABLE_AT
+H_SLOTS = 6
+TABLE_AT = 0
+LATE_AT = 16 * KIB
+FIRST_AT = 32 * KIB
+GROUPED_AT = 48 * KIB
+CONTEXTS_AT = 64 * KIB
+W3_RAW_AT = 71 * KIB
+DEALT_AT = 74 * KIB
+LAST_STATES_AT = 90 * KIB
+H_VALS_AT = 94 * KIB
+PAGES_AT = 106 * KIB
+W1_MID_AT = 138 * KIB
+PLANE_AT = 141 * KIB
+W3_MID_AT = 144 * KIB
+FACTORS_AT = 148 * KIB
+W1_RAW_AT = 152 * KIB
+PACKED_AT = W1_MID_AT
 
 
 def tile_list_resumed_session_features_kernel(
@@ -97,38 +111,39 @@ def tile_list_resumed_session_features_kernel(
             nc.sync.dma_start(out=raw[:], in_=rows[:, :, start : start + width])
             return raw
 
-        table_plane = keep.tile([P, 1, T], U8, name="table_plane")
+        table_plane = shared.tile([P, 1, T], U8, name="table_plane", offset=PLANE_AT)
         nc.vector.memset(table_plane[:].bitcast(I32), 0)
         w2_plane = keep.tile([P, 1, H], U8, name="w2_plane", align_bytes=64)
-        nc.vector.memset(w2_plane[:].bitcast(I32), 0)
+        nc.gpsimd.memset(w2_plane[:].bitcast(I32), 0)
 
         list1 = lists.tile([P, S // STRIPE], U16, name="list1")
         list2 = lists.tile([P, S // STRIPE], U16, name="list2")
         list3 = lists.tile([P, M // STRIPE], U16, name="list3")
         nc.sync.dma_start(list1[:], offs)
+        nc.sync.dma_start(list2[:], offs2)
+        nc.sync.dma_start(list3[:], offs3)
         raw = {}
-        raw["w1", 0] = load_columns("w1_raw0", w1_rows, 0, P, EARLY_RAW_AT)
-        load_scale_rows(nc.sync, table_plane, tab_scales)
+        raw["w1", 0] = load_columns("w1_raw0", w1_rows, 0, 2 * P, W1_RAW_AT)
+        load_scale_rows(nc.scalar, table_plane, tab_scales)
         table = shared.tile([P, T], I32, name="table", offset=TABLE_AT)
         nc.sync.dma_start(out=table[:], in_=tab_words[0].rearrange("p t i -> p (t i)").bitcast(I32))
         w2_codes = keep.tile([P, 2 * H], U8, name="w2_codes", align_bytes=64)
         nc.sync.dma_start(out=w2_codes[:].bitcast(I32), in_=w2_words[0].bitcast(I32))
-        load_scale_rows(nc.sync, w2_plane, w2_scales)
-        raw["w3", 0] = load_columns("w3_raw0", w3_rows, 0, P, EARLY_RAW_AT + 2 * KIB)
-        nc.sync.dma_start(list2[:], offs2)
-        raw["w1", 1] = load_columns("w1_raw1", w1_rows, P, P, EARLY_RAW_AT + 4 * KIB)
-        raw["w3", 1] = load_columns("w3_raw1", w3_rows, P, P, EARLY_RAW_AT + 6 * KIB)
-        factors = [keep.tile([P, HALF], F32, name="factors%d" % h) for h in range(2)]
-        nc.sync.dma_start(out=factors[0][:], in_=wgs[:, 0:HALF])
-        nc.sync.dma_start(out=factors[1][:], in_=wgs[:, HALF:S])
-        nc.sync.dma_start(list3[:], offs3)
-        raw["w1", 2] = load_columns("w1_raw2", w1_rows, 2 * P, 2 * P, EARLY_RAW_AT + 8 * KIB)
-        raw["w3", 2] = load_columns("w3_raw2", w3_rows, 2 * P, 2 * P, EARLY_RAW_AT + 12 * KIB)
-        raw["w1", 4] = load_columns("w1_raw4", w1_rows, PASS_ROWS, PASS_ROWS, LATE_RAW_AT)
-        raw["w3", 4] = load_columns("w3_raw4", w3_rows, PASS_ROWS, PASS_ROWS, LATE_RAW_AT + 8 * KIB)
+        load_scale_rows(nc.gpsimd, w2_plane, w2_scales)
+        raw["w3", 0] = load_columns("w3_raw0", w3_rows, 0, 2 * P, W3_RAW_AT)
+        w1_first = shared.tile([P, 2 * P, PACK], BF16, name="w1_first", align_bytes=64, offset=FACTORS_AT + KIB)
+        interleave(nc.scalar.copy, w1_first[:], raw["w1", 0][:])
+        w13 = {("w1", 0): quantize("w1_0", w1_first[:].rearrange("p r t -> p (r t)"), 2 * P)}
+        factors = [shared.tile([P, HALF], F32, name="factors%d" % h, offset=FACTORS_AT + 4 * HALF * h) for h in range(2)]
+        for h in range(2):
+            nc.sync.dma_start(out=factors[h][:], in_=wgs[:, h * HALF : (h + 1) * HALF])
+        raw["w1", 2] = load_columns("w1_raw2", w1_rows, 2 * P, 2 * P, W1_MID_AT)
+        raw["w3", 2] = load_columns("w3_raw2", w3_rows, 2 * P, 2 * P, W3_MID_AT)
+        raw["w1", 4] = load_columns("w1_raw4", w1_rows, PASS_ROWS, PASS_ROWS, TABLE_AT)
+        raw["w3", 4] = load_columns("w3_raw4", w3_rows, PASS_ROWS, PASS_ROWS, TABLE_AT + 8 * KIB)
         plain_contexts = shared.tile([P, PACK, M], F32, name="plain_contexts", offset=CONTEXTS_AT)
         nc.sync.dma_start(out=plain_contexts[:], in_=ctx[0:PASS_ROWS].rearrange("(c p) m -> p c m", p=P))
-        dealt_factors = keep.tile([P, PACK, S], F32, name="dealt_factors")
+        dealt_factors = shared.tile([P, PACK, S], F32, name="dealt_factors", offset=DEALT_AT)
         for quad in (0, 2, 1, 3):
             nc.sync.dma_start(
                 out=dealt_factors[QUADRANT * quad : QUADRANT * (quad + 1)],
@@ -136,14 +151,12 @@ def tile_list_resumed_session_features_kernel(
             )
         w4_rows = w4.rearrange("(g p t) n -> g p t n", p=P, t=PACK)
         for g in range(2):
-            raw["w4", g] = load_columns("w4_raw%d" % g, w4_rows[g], 0, N, W4_RAW_AT + 8 * KIB * g)
-        dealt_contexts = shared.tile([P, PACK, M], F32, name="dealt_contexts", offset=EARLY_RAW_AT)
-        nc.sync.dma_start(out=dealt_contexts[:], in_=ctx[PASS_ROWS:H].rearrange("(p t) m -> p t m", t=PACK))
-        w6_raw = shared.tile([P, 2, N], I32, name="w6_raw", offset=EARLY_RAW_AT + 8 * KIB)
+            raw["w4", g] = load_columns("w4_raw%d" % g, w4_rows[g], 0, N, TABLE_AT + 8 * KIB * g)
+        w6_raw = shared.tile([P, 2, N], I32, name="w6_raw", offset=PACKED_AT)
         nc.sync.dma_start(out=w6_raw[:], in_=w6_words.rearrange("g p n t -> p g (n t)").bitcast(I32))
-        w5_raw = shared.tile([P, 2, N], U16, name="w5_raw", offset=EARLY_RAW_AT + 12 * KIB)
+        w5_raw = shared.tile([P, 2, N], U16, name="w5_raw", offset=PACKED_AT + 6 * KIB)
         nc.sync.dma_start(out=w5_raw[:].bitcast(I32), in_=w5_words.rearrange("g p n -> p g n").bitcast(I32))
-        w56_raw_plane = keep.tile([P, 2, N], U8, name="w56_raw_plane")
+        w56_raw_plane = shared.tile([P, 2, N], U8, name="w56_raw_plane", offset=PACKED_AT + 8 * KIB)
         nc.gpsimd.memset(w56_raw_plane[:].bitcast(I32), 0)
         load_scale_rows(nc.sync, w56_raw_plane, w5_scales)
         load_scale_rows(nc.sync, w56_raw_plane, w6_scales, shift=4)
@@ -151,12 +164,10 @@ def tile_list_resumed_session_features_kernel(
         identity = keep.tile([P, P], F32, name="identity")
         make_identity(nc, identity[:])
 
-        w13 = {}
-
-        def round_alone(name):
-            grouped = shared.tile([P, P, PACK], BF16, name=name + "_grouped0", align_bytes=64, offset=GROUPED_AT + KIB * (name == "w3"))
-            interleave(nc.scalar.copy, grouped[:], raw[name, 0][:])
-            w13[name, 0] = quantize(name + "_0", grouped[:].rearrange("p r t -> p (r t)"), P)
+        def round_w3(c):
+            grouped = shared.tile([P, P, PACK], BF16, name="w3_grouped%d" % c, align_bytes=64, offset=GROUPED_AT + 2 * KIB * c)
+            interleave(nc.scalar.copy, grouped[:], raw["w3", 0][:, :, c * P : (c + 1) * P])
+            w13["w3", c] = quantize("w3_%d" % c, grouped[:].rearrange("p r t -> p (r t)"), P)
 
         w13_grouped = {}
 
@@ -178,18 +189,20 @@ def tile_list_resumed_session_features_kernel(
             for i, name in enumerate(("w1", "w3")):
                 w13[name, first] = (codes[:, i * width : (i + 1) * width], plane[:, i * width : (i + 1) * width])
 
-        round_alone("w1")
         v_codes = [keep.tile([P, HALF], U32, name="v_codes%d" % h, align_bytes=64) for h in range(2)]
         v_planes = [keep.tile([P, HALF], U8, name="v_plane%d" % h, align_bytes=64) for h in range(2)]
         for h in range(2):
             nc.vector.tensor_copy(v_planes[h][:], table_plane[:, 0, :].indirect(entries(list1, h * HALF, HALF)))
         for h in range(2):
             nc.vector.tensor_copy(v_codes[h][:], table[:].bitcast(U32).indirect(entries(list1, h * HALF, HALF)))
-        round_alone("w3")
-        pages = [keep.tile([P, T2], F32, name="page%d" % i) for i in range(PACK)]
-        for page in pages:
+        round_w3(0)
+        pages = [shared.tile([P, T2], F32, name="page%d" % i, offset=PAGES_AT + 4 * T2 * i) for i in range(PACK)]
+        for page in pages[:2]:
             nc.vector.memset(page[:].bitcast(I32), 0)
-        dealt_pages = pages[2:] + pages[:2]
+        for page in pages[2:]:
+            for at in range(0, T2, S):
+                nc.gpsimd.memset(page[:, at : at + S].bitcast(I32), 0)
+        dealt_pages = pages
 
         def w2_columns(start, width):
             return w2_codes[:, 2 * start : 2 * (start + width)].bitcast(E2M1), w2_plane[:, 0, start : start + width]
@@ -237,7 +250,7 @@ def tile_list_resumed_session_features_kernel(
 
         early = [first_product(i) for i in range(2)]
         fused_scatter(0, first_state(0, early[0]))
-        round_both(1, P)
+        round_w3(1)
         second = first_state(1, early[1])
         late = first_product(2)
         fused_scatter(1, second)
@@ -250,6 +263,7 @@ def tile_list_resumed_session_features_kernel(
         products = {}
         addends = {}
         states = {}
+        state_pairs = {}
 
         def make_terms(u):
             banks = [bank(i, "terms") for i in (B_BANKS[u % 2], A_BANK, D_BANK)]
@@ -282,9 +296,12 @@ def tile_list_resumed_session_features_kernel(
 
             b_vals = copy_out("b_vals", banks[0], 3)
             a_vals = copy_out("a_vals", banks[1], 3)
-            addends[u] = copy_out("d_vals", banks[2], 7)
-            products[u] = ring.tile([P, BANK], F32, name="ab_vals", bufs=7)
+            addends[u] = copy_out("d_vals", banks[2], 6)
+            products[u] = ring.tile([P, BANK], F32, name="ab_vals", bufs=6)
             nc.gpsimd.tensor_tensor(products[u][:], a_vals[:], b_vals[:], MULT)
+
+        def h_slot(s, name):
+            return shared.tile([P, BANK], F32, name=name, offset=H_VALS_AT + 4 * BANK * (s % H_SLOTS))
 
         def make_states(s):
             if s < PLAIN_STEPS:
@@ -304,14 +321,19 @@ def tile_list_resumed_session_features_kernel(
                     factor = factor.rearrange("p o (i j) -> p (o i) j", i=2)
             h_bank = bank(H_BANKS[s % 2], "h_bank")
             add_transposed(blocks(h_bank), early_blocks, late_blocks)
-            plain = ring.tile([P, BANK], F32, name="h_vals", bufs=3)
+            if s == STEPS - 1:
+                plain = shared.tile([P, BANK], F32, name="last_h_vals", offset=LATE_AT + 8 * KIB)
+            else:
+                plain = h_slot(s, "h_vals%d" % s)
             nc.scalar.copy(out=plain[:], in_=h_bank[:])
             if s == STEPS - 1:
-                states[s] = shared.tile([P, BANK], F32, name="last_states", offset=LAST_STATES_AT)
+                states[s] = shared.tile([P, BANK], F32, name="last_states", offset=LAST_STATES_AT + KIB)[:]
             else:
-                states[s] = ring.tile([P, BANK], F32, name="states", bufs=3)
+                if s % 2 == 0:
+                    state_pairs[s // 2] = ring.tile([P, S], F32, name="states", bufs=3)
+                states[s] = state_pairs[s // 2][:, (s % 2) * HALF : (s % 2 + 1) * HALF]
             nc.gpsimd.tensor_tensor(
-                states[s][:].rearrange("p (i j) -> p i j", i=2), plain[:].rearrange("p (i j) -> p i j", i=2), factor, MULT,
+                states[s].rearrange("p (i j) -> p i j", i=2), plain[:].rearrange("p (i j) -> p i j", i=2), factor, MULT,
             )
 
         def scatter(s):
@@ -324,9 +346,12 @@ def tile_list_resumed_session_features_kernel(
         z_rows = shared.tile([P, QUARTERS, 2, P, 2], BF16, name="z_rows", offset=GROUPED_AT)
         picks = {}
 
-        def pick(c):
-            picks[c] = ring.tile([P, M], F32, name="picked", bufs=3)
-            nc.vector.tensor_copy(picks[c][:], pages[c % 2][:].indirect(list3[:]))
+        def pick(c, slot):
+            if c == 0:
+                picks[c] = shared.tile([P, M], F32, name="picked0", offset=FIRST_AT)
+            else:
+                picks[c] = h_slot(slot, "picked%d" % c)
+            nc.vector.tensor_copy(picks[c][:], pages[c % PACK][:].indirect(list3[:]))
 
         def place(c, bank_index):
             z_bank = bank(bank_index, "z_bank")
@@ -348,13 +373,13 @@ def tile_list_resumed_session_features_kernel(
                     out=grouped[:, mh, :].bitcast(F32).rearrange("p (b m u) -> p b m u", b=2, u=2),
                     in_=word_bank[:].rearrange("p (b u m) -> p b m u", b=2, u=2),
                 )
-            return quantize("z0", grouped[:].rearrange("p h c -> p (h c)"), M)
+            return grouped
 
         w4_grouped = {}
 
         def round_w4(g, half):
             if half == 0:
-                w4_grouped[g] = shared.tile([P, PACK, P, PACK], BF16, name="w4_grouped%d" % g, align_bytes=64, offset=LATE_RAW_AT + 4 * KIB * g)
+                w4_grouped[g] = shared.tile([P, PACK, P, PACK], BF16, name="w4_grouped%d" % g, align_bytes=64, offset=LATE_AT + 4 * KIB * g)
             qs = slice(half * P // 2, (half + 1) * P // 2)
             nc.scalar.copy(
                 out=w4_grouped[g][:].rearrange("p t q i -> p q t i")[:, qs],
@@ -371,15 +396,21 @@ def tile_list_resumed_session_features_kernel(
                 in_=plain[:, g, :].rearrange("p (q t) -> p t q", t=PACK),
             )
 
-        pick(0)
+        dealt_contexts = shared.tile([P, PACK, M], F32, name="dealt_contexts", offset=FIRST_AT + 8 * KIB)
+        pick(0, H_SLOTS - 1)
         for s in range(AHEAD):
             make_states(s)
-        picked = shared.tile([P, PACK, M], F32, name="z_vals", offset=LATE_RAW_AT + 8 * KIB)
 
-        def pick_add(t, start, count):
+        def pick_add(t, q):
             nc.vector.tensor_tensor(
-                picked[:, t, start : start + count], dealt_pages[t][:].indirect(entries(list3, start, count)),
-                dealt_contexts[:, t, start : start + count], ADD,
+                picked[:, q, t, :], dealt_pages[t][:].indirect(entries(list3, q * P, P)),
+                dealt_contexts[:, t, q * P : (q + 1) * P], ADD,
+            )
+
+        def add_context(t):
+            nc.gpsimd.tensor_tensor(
+                picked[:, :, t, :], picks[PACK + t][:].rearrange("p (q m) -> p q m", q=QUARTERS),
+                dealt_contexts[:, t, :].rearrange("p (q m) -> p q m", q=QUARTERS), ADD,
             )
 
         for s in range(STEPS):
@@ -389,44 +420,61 @@ def tile_list_resumed_session_features_kernel(
                 round_piece(PACK, PASS_ROWS, s * 2 * P, 2 * P)
             if s == 2:
                 quantize_both(PACK, PASS_ROWS)
-            if s < PLAIN_STEPS:
-                c, h = divmod(s + 2, 2)
-                nc.vector.tensor_copy(pages[c % 2][:].indirect(entries(list2, h * HALF, HALF)), states[s][:])
-                if h == 1:
-                    pick(c)
+                nc.sync.dma_start(out=dealt_contexts[:], in_=ctx[PASS_ROWS:H].rearrange("(p t) m -> p t m", t=PACK))
+            if s < 2:
+                nc.vector.tensor_copy(pages[1][:].indirect(entries(list2, s * HALF, HALF)), states[s])
+            elif s < PLAIN_STEPS:
+                if s % 2 == 1:
+                    nc.vector.tensor_copy(pages[s // 2 + 1][:].indirect(list2[:]), state_pairs[s // 2][:])
+                    pick(s // 2, s)
             else:
                 scatter(s)
-                t = s - (STEPS - PACK)
-                if 0 <= t < PACK - 1:
-                    plain_pick = ring.tile([P, M], F32, name="picked", bufs=3)
-                    nc.vector.tensor_copy(plain_pick[:], dealt_pages[t][:].indirect(list3[:]))
-                    nc.gpsimd.tensor_tensor(picked[:, t, :], plain_pick[:], dealt_contexts[:, t, :], ADD)
-            if s % 2 == 1 and s // 2 < PACK:
-                place(s // 2, H_BANKS[(s + AHEAD) % 2])
-            if s == PLAIN_STEPS + 2:
-                z0_codes, z0_plane = quantize_first_pass()
-            if PLAIN_STEPS <= s < PLAIN_STEPS + 4:
-                round_w4(*divmod(s - PLAIN_STEPS, 2))
-            if s == PLAIN_STEPS + 4:
+            if s == PLAIN_STEPS:
+                pick(PACK - 1, s)
+            if s == STEPS - PACK + 1:
+                picked = shared.tile([P, QUARTERS, PACK, P], F32, name="z_vals", offset=LATE_AT + 8 * KIB)
+            t = s - (STEPS - PACK) - 1
+            if 0 <= t < 2:
+                pick(PACK + t, s)
+                add_context(t)
+            if t == 1:
+                pick(PACK + 2, s - 2)
+                add_context(2)
+                z0_codes = shared.tile([P, M], U32, name="z0_codes", align_bytes=64, offset=PAGES_AT + 4 * T2)
+                z0_plane = keep.tile([P, M], U8, name="z0_plane", align_bytes=64)
+                nc.vector.quantize_mx(
+                    out=z0_codes[:].bitcast(E4M3), scales=z0_plane[:], in_=z0_grouped[:].rearrange("p h c -> p (h c)"),
+                )
+            if s % 2 == 1 and 3 <= s < 3 + 2 * PACK:
+                place((s - 3) // 2, H_BANKS[(s + AHEAD) % 2])
+            if s == STEPS - PACK:
+                z0_grouped = quantize_first_pass()
                 for g in range(2):
                     deal(nc.vector.tensor_copy, w6_codes, w6_raw, g)
                     deal(nc.vector.tensor_copy, w56_plane, w56_raw_plane, g)
                     deal(nc.vector.tensor_copy, w5_codes, w5_raw, g)
+            if s >= STEPS - PACK:
+                round_w4(*divmod(s - (STEPS - PACK), 2))
 
         z1 = {}
-        for q in range(QUARTERS):
-            pick_add(PACK - 1, q * P, P)
-        for q in range(QUARTERS):
-            grouped = shared.tile([P, P, PACK], BF16, name="z_grouped1%d" % q, align_bytes=64, offset=GROUPED_AT + KIB * (8 + q))
-            interleave(nc.scalar.copy, grouped[:], picked[:, :, q * P : (q + 1) * P])
-            z1[q] = quantize("z1%d" % q, grouped[:].rearrange("p m t -> p (m t)"), P)
         w4_codes = shared.tile([P, 2, N], U32, name="w4_codes", align_bytes=64, offset=LAST_STATES_AT)
         w4_plane = keep.tile([P, 2, N], U8, name="w4_plane", align_bytes=64)
-        for g in range(2):
+
+        def quantize_w4(g):
             nc.vector.quantize_mx(
                 out=w4_codes[:, g, :].bitcast(E4M3), scales=w4_plane[:, g, :],
                 in_=w4_grouped[g][:].rearrange("p t q i -> p (t q i)"),
             )
+
+        quantize_w4(0)
+        for q in range(QUARTERS):
+            pick_add(PACK - 1, q)
+        for q in range(QUARTERS):
+            grouped = shared.tile([P, P, PACK], BF16, name="z_grouped1%d" % q, align_bytes=64, offset=GROUPED_AT + KIB * (8 + q))
+            interleave(nc.scalar.copy, grouped[:], picked[:, q])
+            z1[q] = quantize("z1%d" % q, grouped[:].rearrange("p m t -> p (m t)"), P)
+            if q == 0:
+                quantize_w4(1)
 
         def stationary(name, g, t):
             cols = slice(t * P, (t + 1) * P)

@@ -34,25 +34,34 @@ SUM_BANKS = (0, 1, 2, 3, 6, 7, 4, 5)
 PLAIN_STEPS = 2 * (PACK - 1)
 STEPS = PLAIN_STEPS + S // P
 AHEAD = 2
+PLAIN_ORDER = [(1, 0), (2, 0), (1, 1), (3, 0), (2, 1), (3, 1)]
 DEALT_STEPS = [((t, t + 1), start, PIECE) for start in (0, PIECE) for t in (0, 2)] + [((t,), HALF, HALF) for t in range(PACK)]
 KIB = 1024
-H_SLOTS = 6
+H_SLOTS = 4
 TABLE_AT = 0
-LATE_AT = 16 * KIB
-FIRST_AT = 32 * KIB
-GROUPED_AT = 48 * KIB
-CONTEXTS_AT = 64 * KIB
-W3_RAW_AT = 71 * KIB
-DEALT_AT = 74 * KIB
-LAST_STATES_AT = 90 * KIB
-H_VALS_AT = 94 * KIB
-PAGES_AT = 106 * KIB
-W1_MID_AT = 138 * KIB
-PLANE_AT = 141 * KIB
-W3_MID_AT = 144 * KIB
-FACTORS_AT = 148 * KIB
-W1_RAW_AT = 152 * KIB
+FIRST_AT = 16 * KIB
+GROUPED_AT = 32 * KIB
+LATE_AT = 48 * KIB
+W6_AT = 64 * KIB
+W5_AT = 68 * KIB
+W56_PLANE_AT = 70 * KIB
+PICKS_AT = 71 * KIB
+CONTEXTS_AT = 79 * KIB
+W3_RAW_AT = 86 * KIB
+DEALT_AT = 89 * KIB
+LAST_STATES_AT = 105 * KIB
+H_VALS_AT = 109 * KIB
+PAGES_AT = 117 * KIB
+W1_MID_AT = 149 * KIB
+W1_FIRST_AT = 152 * KIB
+W3_MID_AT = 153 * KIB
+FACTORS_AT = 157 * KIB
+W1_RAW_AT = FACTORS_AT
+PLANE_AT = FIRST_AT + 12 * KIB
 PACKED_AT = W1_MID_AT
+H_HOMES = {3: PICKS_AT + 2 * KIB, 5: PICKS_AT + 4 * KIB, 6: PICKS_AT + 6 * KIB, 12: W56_PLANE_AT, 13: W6_AT - KIB}
+PICK_HOMES = {0: FIRST_AT, 1: PICKS_AT + 2 * KIB, 2: PICKS_AT + 4 * KIB, 3: PICKS_AT + 6 * KIB,
+              4: H_VALS_AT + 2 * KIB * (11 % H_SLOTS), 5: PICKS_AT, 6: H_VALS_AT + 2 * KIB * (10 % H_SLOTS)}
 
 
 def tile_list_resumed_session_features_kernel(
@@ -131,7 +140,7 @@ def tile_list_resumed_session_features_kernel(
         nc.sync.dma_start(out=w2_codes[:].bitcast(I32), in_=w2_words[0].bitcast(I32))
         load_scale_rows(nc.gpsimd, w2_plane, w2_scales)
         raw["w3", 0] = load_columns("w3_raw0", w3_rows, 0, 2 * P, W3_RAW_AT)
-        w1_first = shared.tile([P, 2 * P, PACK], BF16, name="w1_first", align_bytes=64, offset=FACTORS_AT + KIB)
+        w1_first = shared.tile([P, 2 * P, PACK], BF16, name="w1_first", align_bytes=64, offset=W1_FIRST_AT)
         interleave(nc.scalar.copy, w1_first[:], raw["w1", 0][:])
         w13 = {("w1", 0): quantize("w1_0", w1_first[:].rearrange("p r t -> p (r t)"), 2 * P)}
         factors = [shared.tile([P, HALF], F32, name="factors%d" % h, offset=FACTORS_AT + 4 * HALF * h) for h in range(2)]
@@ -154,9 +163,9 @@ def tile_list_resumed_session_features_kernel(
             raw["w4", g] = load_columns("w4_raw%d" % g, w4_rows[g], 0, N, TABLE_AT + 8 * KIB * g)
         w6_raw = shared.tile([P, 2, N], I32, name="w6_raw", offset=PACKED_AT)
         nc.sync.dma_start(out=w6_raw[:], in_=w6_words.rearrange("g p n t -> p g (n t)").bitcast(I32))
-        w5_raw = shared.tile([P, 2, N], U16, name="w5_raw", offset=PACKED_AT + 6 * KIB)
+        w5_raw = shared.tile([P, 2, N], U16, name="w5_raw", offset=W3_MID_AT + KIB)
         nc.sync.dma_start(out=w5_raw[:].bitcast(I32), in_=w5_words.rearrange("g p n -> p g n").bitcast(I32))
-        w56_raw_plane = shared.tile([P, 2, N], U8, name="w56_raw_plane", offset=PACKED_AT + 8 * KIB)
+        w56_raw_plane = shared.tile([P, 2, N], U8, name="w56_raw_plane", offset=W3_MID_AT + 3 * KIB)
         nc.gpsimd.memset(w56_raw_plane[:].bitcast(I32), 0)
         load_scale_rows(nc.sync, w56_raw_plane, w5_scales)
         load_scale_rows(nc.sync, w56_raw_plane, w6_scales, shift=4)
@@ -256,7 +265,7 @@ def tile_list_resumed_session_features_kernel(
         fused_scatter(1, second)
         late = first_state(2, late)
         round_both(2, 2 * P)
-        weighted_late = shared.tile([P, HALF], F32, name="first_weighted", offset=FIRST_AT + 4 * 3 * S)
+        weighted_late = shared.tile([P, HALF], F32, name="first_weighted", offset=GROUPED_AT + 4 * KIB)
         nc.vector.tensor_tensor(weighted_late[:], late[:], factors[1][:], MULT)
         nc.vector.tensor_copy(pages[0][:].indirect(entries(list2, HALF, HALF)), weighted_late[:])
 
@@ -268,7 +277,7 @@ def tile_list_resumed_session_features_kernel(
         def make_terms(u):
             banks = [bank(i, "terms") for i in (B_BANKS[u % 2], A_BANK, D_BANK)]
             if u < PLAIN_STEPS:
-                c, h = divmod(u + 2, 2)
+                c, h = PLAIN_ORDER[u]
                 start, width = c * P, P
                 v_blocks = list(zip(blocks(v_codes[h]), blocks(v_planes[h])))
             else:
@@ -300,14 +309,11 @@ def tile_list_resumed_session_features_kernel(
             products[u] = ring.tile([P, BANK], F32, name="ab_vals", bufs=6)
             nc.gpsimd.tensor_tensor(products[u][:], a_vals[:], b_vals[:], MULT)
 
-        def h_slot(s, name):
-            return shared.tile([P, BANK], F32, name=name, offset=H_VALS_AT + 4 * BANK * (s % H_SLOTS))
-
         def make_states(s):
             if s < PLAIN_STEPS:
                 make_terms(s)
                 early_blocks, late_blocks = blocks(addends[s]), blocks(products[s])
-                factor = factors[s % 2][:].rearrange("p (i j) -> p i j", i=2)
+                factor = factors[PLAIN_ORDER[s][1]][:].rearrange("p (i j) -> p i j", i=2)
             else:
                 ts, start, count = DEALT_STEPS[s - PLAIN_STEPS]
                 units = range(PLAIN_STEPS + start // P, PLAIN_STEPS + (start + count) // P)
@@ -321,10 +327,7 @@ def tile_list_resumed_session_features_kernel(
                     factor = factor.rearrange("p o (i j) -> p (o i) j", i=2)
             h_bank = bank(H_BANKS[s % 2], "h_bank")
             add_transposed(blocks(h_bank), early_blocks, late_blocks)
-            if s == STEPS - 1:
-                plain = shared.tile([P, BANK], F32, name="last_h_vals", offset=LATE_AT + 8 * KIB)
-            else:
-                plain = h_slot(s, "h_vals%d" % s)
+            plain = shared.tile([P, BANK], F32, name="h_vals%d" % s, offset=H_HOMES.get(s, H_VALS_AT + 2 * KIB * (s % H_SLOTS)))
             nc.scalar.copy(out=plain[:], in_=h_bank[:])
             if s == STEPS - 1:
                 states[s] = shared.tile([P, BANK], F32, name="last_states", offset=LAST_STATES_AT + KIB)[:]
@@ -346,11 +349,8 @@ def tile_list_resumed_session_features_kernel(
         z_rows = shared.tile([P, QUARTERS, 2, P, 2], BF16, name="z_rows", offset=GROUPED_AT)
         picks = {}
 
-        def pick(c, slot):
-            if c == 0:
-                picks[c] = shared.tile([P, M], F32, name="picked0", offset=FIRST_AT)
-            else:
-                picks[c] = h_slot(slot, "picked%d" % c)
+        def pick(c):
+            picks[c] = shared.tile([P, M], F32, name="picked%d" % c, offset=PICK_HOMES[c])
             nc.vector.tensor_copy(picks[c][:], pages[c % PACK][:].indirect(list3[:]))
 
         def place(c, bank_index):
@@ -386,10 +386,6 @@ def tile_list_resumed_session_features_kernel(
                 in_=raw["w4", g][:].rearrange("p i (q t) -> p q t i", t=PACK)[:, qs],
             )
 
-        w6_codes = shared.tile([P, 2, N], I32, name="w6_codes", align_bytes=64, offset=CONTEXTS_AT)
-        w5_codes = shared.tile([P, 2, N], U16, name="w5_codes", align_bytes=64, offset=CONTEXTS_AT + 4 * KIB)
-        w56_plane = shared.tile([P, 2, N], U8, name="w56_plane", align_bytes=64, offset=CONTEXTS_AT + 6 * KIB)
-
         def deal(engine_copy, dealt, plain, g):
             engine_copy(
                 out=dealt[:, g, :].rearrange("p (t q) -> p t q", t=PACK),
@@ -397,7 +393,7 @@ def tile_list_resumed_session_features_kernel(
             )
 
         dealt_contexts = shared.tile([P, PACK, M], F32, name="dealt_contexts", offset=FIRST_AT + 8 * KIB)
-        pick(0, H_SLOTS - 1)
+        pick(0)
         for s in range(AHEAD):
             make_states(s)
 
@@ -416,29 +412,39 @@ def tile_list_resumed_session_features_kernel(
         for s in range(STEPS):
             if s + AHEAD < STEPS:
                 make_states(s + AHEAD)
+            if PLAIN_STEPS - AHEAD < s < PLAIN_STEPS + 2:
+                for u in (2 * s - 2, 2 * s - 1):
+                    make_terms(u)
+            if s + AHEAD == STEPS - 1:
+                w6_codes = shared.tile([P, 2, N], I32, name="w6_codes", align_bytes=64, offset=W6_AT)
+                w5_codes = shared.tile([P, 2, N], U16, name="w5_codes", align_bytes=64, offset=CONTEXTS_AT)
+                w56_plane = shared.tile([P, 2, N], U8, name="w56_plane", align_bytes=64, offset=W56_PLANE_AT)
+                for g in range(2):
+                    deal(nc.gpsimd.tensor_copy, w6_codes, w6_raw, g)
+                    deal(nc.gpsimd.tensor_copy, w56_plane, w56_raw_plane, g)
+                    deal(nc.vector.tensor_copy, w5_codes, w5_raw, g)
             if s < 2:
                 round_piece(PACK, PASS_ROWS, s * 2 * P, 2 * P)
             if s == 2:
                 quantize_both(PACK, PASS_ROWS)
                 nc.sync.dma_start(out=dealt_contexts[:], in_=ctx[PASS_ROWS:H].rearrange("(p t) m -> p t m", t=PACK))
-            if s < 2:
-                nc.vector.tensor_copy(pages[1][:].indirect(entries(list2, s * HALF, HALF)), states[s])
-            elif s < PLAIN_STEPS:
-                if s % 2 == 1:
-                    nc.vector.tensor_copy(pages[s // 2 + 1][:].indirect(list2[:]), state_pairs[s // 2][:])
-                    pick(s // 2, s)
+            if s < PLAIN_STEPS:
+                c, h = PLAIN_ORDER[s]
+                nc.vector.tensor_copy(pages[c][:].indirect(entries(list2, h * HALF, HALF)), states[s])
+                if s in (3, 5):
+                    pick(s // 2)
             else:
                 scatter(s)
             if s == PLAIN_STEPS:
-                pick(PACK - 1, s)
+                pick(PACK - 1)
             if s == STEPS - PACK + 1:
                 picked = shared.tile([P, QUARTERS, PACK, P], F32, name="z_vals", offset=LATE_AT + 8 * KIB)
             t = s - (STEPS - PACK) - 1
             if 0 <= t < 2:
-                pick(PACK + t, s)
+                pick(PACK + t)
                 add_context(t)
             if t == 1:
-                pick(PACK + 2, s - 2)
+                pick(PACK + 2)
                 add_context(2)
                 z0_codes = shared.tile([P, M], U32, name="z0_codes", align_bytes=64, offset=PAGES_AT + 4 * T2)
                 z0_plane = keep.tile([P, M], U8, name="z0_plane", align_bytes=64)
@@ -449,10 +455,6 @@ def tile_list_resumed_session_features_kernel(
                 place((s - 3) // 2, H_BANKS[(s + AHEAD) % 2])
             if s == STEPS - PACK:
                 z0_grouped = quantize_first_pass()
-                for g in range(2):
-                    deal(nc.vector.tensor_copy, w6_codes, w6_raw, g)
-                    deal(nc.vector.tensor_copy, w56_plane, w56_raw_plane, g)
-                    deal(nc.vector.tensor_copy, w5_codes, w5_raw, g)
             if s >= STEPS - PACK:
                 round_w4(*divmod(s - (STEPS - PACK), 2))
 

@@ -34,34 +34,34 @@ SUM_BANKS = (0, 1, 2, 3, 6, 7, 4, 5)
 PLAIN_STEPS = 2 * (PACK - 1)
 STEPS = PLAIN_STEPS + S // P
 AHEAD = 2
-PLAIN_ORDER = [(1, 0), (2, 0), (1, 1), (3, 0), (2, 1), (3, 1)]
+PAGE_TILES = (0, 1, 0, 3, 0, 1, 2, 3)
+PLAIN_ORDER = [(c, h) for c in range(1, PACK) for h in range(2)]
 DEALT_STEPS = [((t, t + 1), start, PIECE) for start in (0, PIECE) for t in (0, 2)] + [((t,), HALF, HALF) for t in range(PACK)]
 KIB = 1024
 H_SLOTS = 4
-TABLE_AT = 0
-FIRST_AT = 16 * KIB
-GROUPED_AT = 32 * KIB
-LATE_AT = 48 * KIB
-W6_AT = 64 * KIB
-W5_AT = 68 * KIB
-W56_PLANE_AT = 70 * KIB
-PICKS_AT = 71 * KIB
-CONTEXTS_AT = 79 * KIB
-W3_RAW_AT = 86 * KIB
-DEALT_AT = 89 * KIB
-LAST_STATES_AT = 105 * KIB
-H_VALS_AT = 109 * KIB
-PAGES_AT = 117 * KIB
-W1_MID_AT = 149 * KIB
-W1_FIRST_AT = 152 * KIB
-W3_MID_AT = 153 * KIB
-FACTORS_AT = 157 * KIB
+TABLE_AT = KIB
+FIRST_AT = 17 * KIB
+GROUPED_AT = 33 * KIB
+LATE_AT = 49 * KIB
+W6_AT = 65 * KIB
+W5_AT = 71 * KIB
+W56_PLANE_AT = 73 * KIB
+PICKS_AT = 74 * KIB
+CONTEXTS_AT = 82 * KIB
+W1_MID_AT = 89 * KIB
+FIRST_GROUPED_AT = 91 * KIB
+W3_MID_AT = 93 * KIB
+DEALT_AT = 96 * KIB
+LAST_STATES_AT = 112 * KIB
+H_VALS_AT = 116 * KIB
+PAGES_AT = 124 * KIB
+FACTORS_AT = 156 * KIB
 W1_RAW_AT = FACTORS_AT
+W3_RAW_AT = LATE_AT
 PLANE_AT = FIRST_AT + 12 * KIB
-PACKED_AT = W1_MID_AT
-H_HOMES = {3: PICKS_AT + 2 * KIB, 5: PICKS_AT + 4 * KIB, 6: PICKS_AT + 6 * KIB, 12: W56_PLANE_AT, 13: W6_AT - KIB}
-PICK_HOMES = {0: FIRST_AT, 1: PICKS_AT + 2 * KIB, 2: PICKS_AT + 4 * KIB, 3: PICKS_AT + 6 * KIB,
-              4: H_VALS_AT + 2 * KIB * (11 % H_SLOTS), 5: PICKS_AT, 6: H_VALS_AT + 2 * KIB * (10 % H_SLOTS)}
+H_HOMES = {2: PICKS_AT + 2 * KIB, 4: PICKS_AT + 4 * KIB, 6: PICKS_AT + 6 * KIB, 11: W5_AT - KIB, 12: W56_PLANE_AT, 13: W6_AT - KIB}
+PICK_HOMES = {0: GROUPED_AT + 12 * KIB, 1: PICKS_AT + 2 * KIB, 2: PICKS_AT + 4 * KIB, 3: PICKS_AT + 6 * KIB,
+              4: W5_AT - 2 * KIB, 5: PICKS_AT, 6: H_VALS_AT + 2 * KIB * (10 % H_SLOTS)}
 
 
 def tile_list_resumed_session_features_kernel(
@@ -133,16 +133,24 @@ def tile_list_resumed_session_features_kernel(
         nc.sync.dma_start(list3[:], offs3)
         raw = {}
         raw["w1", 0] = load_columns("w1_raw0", w1_rows, 0, 2 * P, W1_RAW_AT)
-        load_scale_rows(nc.scalar, table_plane, tab_scales)
+        raw["w3", 0] = load_columns("w3_raw0", w3_rows, 0, 2 * P, W3_RAW_AT)
+        load_scale_rows(nc.sync, table_plane, tab_scales)
         table = shared.tile([P, T], I32, name="table", offset=TABLE_AT)
         nc.sync.dma_start(out=table[:], in_=tab_words[0].rearrange("p t i -> p (t i)").bitcast(I32))
         w2_codes = keep.tile([P, 2 * H], U8, name="w2_codes", align_bytes=64)
         nc.sync.dma_start(out=w2_codes[:].bitcast(I32), in_=w2_words[0].bitcast(I32))
         load_scale_rows(nc.gpsimd, w2_plane, w2_scales)
-        raw["w3", 0] = load_columns("w3_raw0", w3_rows, 0, 2 * P, W3_RAW_AT)
-        w1_first = shared.tile([P, 2 * P, PACK], BF16, name="w1_first", align_bytes=64, offset=W1_FIRST_AT)
-        interleave(nc.scalar.copy, w1_first[:], raw["w1", 0][:])
-        w13 = {("w1", 0): quantize("w1_0", w1_first[:].rearrange("p r t -> p (r t)"), 2 * P)}
+        w13 = {}
+
+        def quantize_both(first, grouped, width):
+            codes, plane = quantize("w13_%d" % first, grouped[:].rearrange("p w r t -> p (w r t)"), 2 * width)
+            for i, name in enumerate(("w1", "w3")):
+                w13[name, first] = (codes[:, i * width : (i + 1) * width], plane[:, i * width : (i + 1) * width])
+
+        first_grouped = shared.tile([P, 2, 2 * P, PACK], BF16, name="first_grouped", align_bytes=64, offset=FIRST_GROUPED_AT)
+        for i, name in enumerate(("w1", "w3")):
+            interleave(nc.scalar.copy, first_grouped[:, i], raw[name, 0][:])
+        quantize_both(0, first_grouped, 2 * P)
         factors = [shared.tile([P, HALF], F32, name="factors%d" % h, offset=FACTORS_AT + 4 * HALF * h) for h in range(2)]
         for h in range(2):
             nc.sync.dma_start(out=factors[h][:], in_=wgs[:, h * HALF : (h + 1) * HALF])
@@ -160,43 +168,31 @@ def tile_list_resumed_session_features_kernel(
             )
         w4_rows = w4.rearrange("(g p t) n -> g p t n", p=P, t=PACK)
         for g in range(2):
-            raw["w4", g] = load_columns("w4_raw%d" % g, w4_rows[g], 0, N, TABLE_AT + 8 * KIB * g)
-        w6_raw = shared.tile([P, 2, N], I32, name="w6_raw", offset=PACKED_AT)
+            raw["w4", g] = load_columns("w4_raw%d" % g, w4_rows[g], 0, N, 8 * KIB * g)
+        w6_raw = shared.tile([P, 2, N], I32, name="w6_raw", offset=W1_MID_AT + KIB)
         nc.sync.dma_start(out=w6_raw[:], in_=w6_words.rearrange("g p n t -> p g (n t)").bitcast(I32))
         w5_raw = shared.tile([P, 2, N], U16, name="w5_raw", offset=W3_MID_AT + KIB)
         nc.sync.dma_start(out=w5_raw[:].bitcast(I32), in_=w5_words.rearrange("g p n -> p g n").bitcast(I32))
-        w56_raw_plane = shared.tile([P, 2, N], U8, name="w56_raw_plane", offset=W3_MID_AT + 3 * KIB)
-        nc.gpsimd.memset(w56_raw_plane[:].bitcast(I32), 0)
-        load_scale_rows(nc.sync, w56_raw_plane, w5_scales)
-        load_scale_rows(nc.sync, w56_raw_plane, w6_scales, shift=4)
 
         identity = keep.tile([P, P], F32, name="identity")
         make_identity(nc, identity[:])
 
-        def round_w3(c):
-            grouped = shared.tile([P, P, PACK], BF16, name="w3_grouped%d" % c, align_bytes=64, offset=GROUPED_AT + 2 * KIB * c)
-            interleave(nc.scalar.copy, grouped[:], raw["w3", 0][:, :, c * P : (c + 1) * P])
-            w13["w3", c] = quantize("w3_%d" % c, grouped[:].rearrange("p r t -> p (r t)"), P)
-
-        w13_grouped = {}
-
-        def round_piece(first, width, at, piece):
-            if at == 0:
-                w13_grouped[first] = shared.tile(
-                    [P, 2, width, PACK], BF16, name="w13_grouped%d" % first, align_bytes=64, offset=GROUPED_AT + 2 * KIB * first,
+        def round_middle():
+            grouped = shared.tile([P, 2, 2 * P, PACK], BF16, name="middle_grouped", align_bytes=64, offset=GROUPED_AT + 4 * KIB)
+            for i, name in enumerate(("w1", "w3")):
+                planar = raw[name, 2]
+                interleave(nc.scalar.copy, grouped[:, i, 0:P], planar[:, :, 0:P])
+                nc.gpsimd.tensor_scalar(
+                    grouped[:, i, P : 2 * P], planar[:, :, P : 2 * P].rearrange("p t c -> p c t"), 1.0, 0.0, MULT, ADD,
                 )
-            for i, name in enumerate(("w1", "w3")):
-                interleave(nc.scalar.copy, w13_grouped[first][:, i, at : at + piece], raw[name, first][:, :, at : at + piece])
+            quantize_both(2, grouped, 2 * P)
 
-        def round_both(first, width):
-            round_piece(first, width, 0, width)
-            quantize_both(first, width)
+        late_grouped = shared.tile([P, 2, PASS_ROWS, PACK], BF16, name="late_grouped", align_bytes=64, offset=GROUPED_AT + 8 * KIB)
 
-        def quantize_both(first, width):
-            grouped = w13_grouped[first]
-            codes, plane = quantize("w13_%d" % first, grouped[:].rearrange("p w r t -> p (w r t)"), 2 * width)
+        def round_late(half):
+            cols = slice(half * 2 * P, (half + 1) * 2 * P)
             for i, name in enumerate(("w1", "w3")):
-                w13[name, first] = (codes[:, i * width : (i + 1) * width], plane[:, i * width : (i + 1) * width])
+                interleave(nc.scalar.copy, late_grouped[:, i, cols], raw[name, PACK][:, :, cols])
 
         v_codes = [keep.tile([P, HALF], U32, name="v_codes%d" % h, align_bytes=64) for h in range(2)]
         v_planes = [keep.tile([P, HALF], U8, name="v_plane%d" % h, align_bytes=64) for h in range(2)]
@@ -204,7 +200,6 @@ def tile_list_resumed_session_features_kernel(
             nc.vector.tensor_copy(v_planes[h][:], table_plane[:, 0, :].indirect(entries(list1, h * HALF, HALF)))
         for h in range(2):
             nc.vector.tensor_copy(v_codes[h][:], table[:].bitcast(U32).indirect(entries(list1, h * HALF, HALF)))
-        round_w3(0)
         pages = [shared.tile([P, T2], F32, name="page%d" % i, offset=PAGES_AT + 4 * T2 * i) for i in range(PACK)]
         for page in pages[:2]:
             nc.vector.memset(page[:].bitcast(I32), 0)
@@ -246,28 +241,29 @@ def tile_list_resumed_session_features_kernel(
 
         def first_state(i, product):
             count = FIRST_CHUNKS[i][1]
-            at = GROUPED_AT + 2 * KIB if i == 1 else FIRST_AT + 4 * (2 * S + FIRST_CHUNKS[i][0])
+            at = FIRST_AT + 4 * (2 * S + FIRST_CHUNKS[i][0])
             state = shared.tile([P, count], F32, name="first_h%d" % i, offset=at)
             nc.vector.tensor_tensor(state[:], chunk_terms[i][0][2][:, 0:count], product[:], ADD)
             return state
 
-        def fused_scatter(i, state):
+        def weigh(i, state, at):
             start, count, unused = FIRST_CHUNKS[i]
-            nc.vector.tensor_tensor(
-                pages[0][:].indirect(entries(list2, start, count)), state[:], factors[0][:, start : start + count], MULT,
-            )
+            h, first = divmod(start, HALF)
+            weighted = shared.tile([P, count], F32, name="first_weighted%d" % i, offset=at)
+            nc.vector.tensor_tensor(weighted[:], state[:], factors[h][:, first : first + count], MULT)
+            return weighted
+
+        def first_scatter(i, weighted):
+            start, count, unused = FIRST_CHUNKS[i]
+            nc.vector.tensor_copy(pages[0][:].indirect(entries(list2, start, count)), weighted[:])
 
         early = [first_product(i) for i in range(2)]
-        fused_scatter(0, first_state(0, early[0]))
-        round_w3(1)
-        second = first_state(1, early[1])
+        early = [first_state(i, early[i]) for i in range(2)]
+        nc.vector.tensor_tensor(pages[0][:].indirect(entries(list2, 0, PIECE)), early[0][:], factors[0][:, 0:PIECE], MULT)
+        second = weigh(1, early[1], FIRST_AT + 12 * KIB)
         late = first_product(2)
-        fused_scatter(1, second)
+        first_scatter(1, second)
         late = first_state(2, late)
-        round_both(2, 2 * P)
-        weighted_late = shared.tile([P, HALF], F32, name="first_weighted", offset=GROUPED_AT + 4 * KIB)
-        nc.vector.tensor_tensor(weighted_late[:], late[:], factors[1][:], MULT)
-        nc.vector.tensor_copy(pages[0][:].indirect(entries(list2, HALF, HALF)), weighted_late[:])
 
         products = {}
         addends = {}
@@ -311,7 +307,8 @@ def tile_list_resumed_session_features_kernel(
 
         def make_states(s):
             if s < PLAIN_STEPS:
-                make_terms(s)
+                if s not in products:
+                    make_terms(s)
                 early_blocks, late_blocks = blocks(addends[s]), blocks(products[s])
                 factor = factors[PLAIN_ORDER[s][1]][:].rearrange("p (i j) -> p i j", i=2)
             else:
@@ -351,7 +348,7 @@ def tile_list_resumed_session_features_kernel(
 
         def pick(c):
             picks[c] = shared.tile([P, M], F32, name="picked%d" % c, offset=PICK_HOMES[c])
-            nc.vector.tensor_copy(picks[c][:], pages[c % PACK][:].indirect(list3[:]))
+            nc.vector.tensor_copy(picks[c][:], pages[PAGE_TILES[c]][:].indirect(list3[:]))
 
         def place(c, bank_index):
             z_bank = bank(bank_index, "z_bank")
@@ -393,7 +390,9 @@ def tile_list_resumed_session_features_kernel(
             )
 
         dealt_contexts = shared.tile([P, PACK, M], F32, name="dealt_contexts", offset=FIRST_AT + 8 * KIB)
-        pick(0)
+        make_terms(0)
+        round_middle()
+        first_scatter(2, weigh(2, late, GROUPED_AT + 4 * KIB))
         for s in range(AHEAD):
             make_states(s)
 
@@ -417,21 +416,29 @@ def tile_list_resumed_session_features_kernel(
                     make_terms(u)
             if s + AHEAD == STEPS - 1:
                 w6_codes = shared.tile([P, 2, N], I32, name="w6_codes", align_bytes=64, offset=W6_AT)
-                w5_codes = shared.tile([P, 2, N], U16, name="w5_codes", align_bytes=64, offset=CONTEXTS_AT)
+                w5_codes = shared.tile([P, 2, N], U16, name="w5_codes", align_bytes=64, offset=W5_AT)
                 w56_plane = shared.tile([P, 2, N], U8, name="w56_plane", align_bytes=64, offset=W56_PLANE_AT)
                 for g in range(2):
                     deal(nc.gpsimd.tensor_copy, w6_codes, w6_raw, g)
                     deal(nc.gpsimd.tensor_copy, w56_plane, w56_raw_plane, g)
-                    deal(nc.vector.tensor_copy, w5_codes, w5_raw, g)
-            if s < 2:
-                round_piece(PACK, PASS_ROWS, s * 2 * P, 2 * P)
+                    nc.gpsimd.tensor_copy(
+                        out=w5_codes[:, g, :].bitcast(U8).rearrange("p (t q b) -> p t q b", t=PACK, b=2),
+                        in_=w5_raw[:, g, :].bitcast(U8).rearrange("p (q t b) -> p t q b", t=PACK, b=2),
+                    )
+            if s == 0:
+                round_late(0)
+                round_late(1)
+                quantize_both(PACK, late_grouped, PASS_ROWS)
             if s == 2:
-                quantize_both(PACK, PASS_ROWS)
+                w56_raw_plane = shared.tile([P, 2, N], U8, name="w56_raw_plane", offset=16 * KIB)
+                nc.gpsimd.memset(w56_raw_plane[:].bitcast(I32), 0)
+                load_scale_rows(nc.sync, w56_raw_plane, w5_scales)
+                load_scale_rows(nc.sync, w56_raw_plane, w6_scales, shift=4)
                 nc.sync.dma_start(out=dealt_contexts[:], in_=ctx[PASS_ROWS:H].rearrange("(p t) m -> p t m", t=PACK))
             if s < PLAIN_STEPS:
                 c, h = PLAIN_ORDER[s]
-                nc.vector.tensor_copy(pages[c][:].indirect(entries(list2, h * HALF, HALF)), states[s])
-                if s in (3, 5):
+                nc.vector.tensor_copy(pages[PAGE_TILES[c]][:].indirect(entries(list2, h * HALF, HALF)), states[s])
+                if s % 2 == 0:
                     pick(s // 2)
             else:
                 scatter(s)
@@ -451,8 +458,8 @@ def tile_list_resumed_session_features_kernel(
                 nc.vector.quantize_mx(
                     out=z0_codes[:].bitcast(E4M3), scales=z0_plane[:], in_=z0_grouped[:].rearrange("p h c -> p (h c)"),
                 )
-            if s % 2 == 1 and 3 <= s < 3 + 2 * PACK:
-                place((s - 3) // 2, H_BANKS[(s + AHEAD) % 2])
+            if PLAIN_STEPS <= s < PLAIN_STEPS + PACK:
+                place(s - PLAIN_STEPS, H_BANKS[(s + AHEAD) % 2])
             if s == STEPS - PACK:
                 z0_grouped = quantize_first_pass()
             if s >= STEPS - PACK:

@@ -36,7 +36,7 @@ STEPS = PLAIN_STEPS + S // P
 AHEAD = 2
 PAGE_TILES = (0, 1, 0, 3, 0, 1, 2, 3)
 PLAIN_ORDER = [(c, h) for c in range(1, PACK) for h in range(2)]
-DEALT_STEPS = [((t, t + 1), start, PIECE) for start in (0, PIECE) for t in (0, 2)] + [((t,), HALF, HALF) for t in range(PACK)]
+DEALT_STEPS = [((t,), start, HALF) for start in (0, HALF) for t in range(PACK)]
 KIB = 1024
 H_SLOTS = 4
 TABLE_AT = KIB
@@ -195,9 +195,9 @@ def tile_list_resumed_session_features_kernel(
                 interleave(nc.scalar.copy, late_grouped[:, i, cols], raw[name, PACK][:, :, cols])
 
         v_codes = [keep.tile([P, HALF], U32, name="v_codes%d" % h, align_bytes=64) for h in range(2)]
-        v_planes = [keep.tile([P, HALF], U8, name="v_plane%d" % h, align_bytes=64) for h in range(2)]
-        for h in range(2):
-            nc.vector.tensor_copy(v_planes[h][:], table_plane[:, 0, :].indirect(entries(list1, h * HALF, HALF)))
+        v_plane = keep.tile([P, S], U8, name="v_plane", align_bytes=64)
+        nc.vector.tensor_copy(v_plane[:], table_plane[:, 0, :].indirect(list1[:]))
+        v_planes = [v_plane[:, h * HALF : (h + 1) * HALF] for h in range(2)]
         for h in range(2):
             nc.vector.tensor_copy(v_codes[h][:], table[:].bitcast(U32).indirect(entries(list1, h * HALF, HALF)))
         pages = [shared.tile([P, T2], F32, name="page%d" % i, offset=PAGES_AT + 4 * T2 * i) for i in range(PACK)]
@@ -301,8 +301,8 @@ def tile_list_resumed_session_features_kernel(
 
             b_vals = copy_out("b_vals", banks[0], 3)
             a_vals = copy_out("a_vals", banks[1], 3)
-            addends[u] = copy_out("d_vals", banks[2], 6)
-            products[u] = ring.tile([P, BANK], F32, name="ab_vals", bufs=6)
+            addends[u] = copy_out("d_vals", banks[2], 7)
+            products[u] = ring.tile([P, BANK], F32, name="ab_vals", bufs=7)
             nc.gpsimd.tensor_tensor(products[u][:], a_vals[:], b_vals[:], MULT)
 
         def make_states(s):
@@ -411,7 +411,10 @@ def tile_list_resumed_session_features_kernel(
         for s in range(STEPS):
             if s + AHEAD < STEPS:
                 make_states(s + AHEAD)
-            if PLAIN_STEPS - AHEAD < s < PLAIN_STEPS + 2:
+            if s == 3:
+                for u in (6, 7):
+                    make_terms(u)
+            if PLAIN_STEPS <= s < PLAIN_STEPS + 2:
                 for u in (2 * s - 2, 2 * s - 1):
                     make_terms(u)
             if s + AHEAD == STEPS - 1:
@@ -524,7 +527,7 @@ def tile_list_resumed_session_features_kernel(
             y_vals = shared.tile([P, PACK, P], F32, name="y_vals%d" % q, offset=FIRST_AT + 2 * KIB * (4 + q))
             nc.vector.scalar_tensor_tensor(y_vals[:].rearrange("p t m -> p (t m)"), gated[:], 0.5, sums[q, "base"][:], MULT, ADD)
             nc.sync.dma_start(out=out_rows[:, :, cols], in_=y_vals[:])
-            y_grouped = ring.tile([P, P, PACK], BF16, name="y_grouped", align_bytes=64)
+            y_grouped = shared.tile([P, P, PACK], BF16, name="y_grouped%d" % q, align_bytes=64, offset=GROUPED_AT + KIB * q)
             interleave(nc.scalar.copy if q < QUARTERS - 1 else nc.vector.tensor_copy, y_grouped[:], y_vals[:])
             nc.vector.quantize_mx(
                 out=y_codes[:, cols].bitcast(E4M3), scales=y_plane[:, cols],

@@ -424,10 +424,10 @@ def tile_list_resumed_session_features_kernel(
                 for g in range(2):
                     deal(nc.gpsimd.tensor_copy, w6_codes, w6_raw, g)
                     deal(nc.gpsimd.tensor_copy, w56_plane, w56_raw_plane, g)
-                    nc.gpsimd.tensor_copy(
-                        out=w5_codes[:, g, :].bitcast(U8).rearrange("p (t q b) -> p t q b", t=PACK, b=2),
-                        in_=w5_raw[:, g, :].bitcast(U8).rearrange("p (q t b) -> p t q b", t=PACK, b=2),
-                    )
+                nc.vector.tensor_copy(
+                    out=w5_codes[:].rearrange("p g (t q) -> p g t q", t=PACK),
+                    in_=w5_raw[:].rearrange("p g (q t) -> p g t q", t=PACK),
+                )
             if s == 0:
                 round_late(0)
                 round_late(1)

@@ -25,43 +25,32 @@ STRIPE = 16
 BANK = 512
 PASS_ROWS = P * PACK
 HALF = S // 2
-PIECE = 256
+CHUNK = 256
 QUARTERS = M // P
-
-FIRST_CHUNKS = [(0, 256, (0, 1, 2)), (256, 256, (3, 4, 5)), (512, 512, (6, 7, 3))]
-B_BANKS, A_BANK, D_BANK, H_BANKS, WORD_BANKS = (0, 3), 1, 2, (4, 5), (6, 7)
-SUM_BANKS = (0, 1, 2, 3, 6, 7, 4, 5)
-PLAIN_STEPS = 2 * (PACK - 1)
-STEPS = PLAIN_STEPS + S // P
+PAGES = H // P
+STEPS = 2 * (PAGES - 1)
 AHEAD = 2
-PAGE_TILES = (0, 1, 0, 3, 0, 1, 2, 3)
-PLAIN_ORDER = [(c, h) for c in range(1, PACK) for h in range(2)]
-DEALT_STEPS = [((t,), start, HALF) for start in (0, HALF) for t in range(PACK)]
+
+FIRST_BANKS = ((0, 1, 2), (3, 4, 5))
+B_BANKS, A_BANK, D_BANK, H_BANKS = (0, 3), 6, 7, (1, 2)
+WORD_BANKS = (4, 5)
+SUM_BANKS = (0, 3, 6, 7, 4, 5, 1, 2)
 KIB = 1024
-H_SLOTS = 4
-TABLE_AT = KIB
-FIRST_AT = 17 * KIB
-GROUPED_AT = 33 * KIB
-LATE_AT = 49 * KIB
-W6_AT = 65 * KIB
-W5_AT = 71 * KIB
-W56_PLANE_AT = 73 * KIB
-PICKS_AT = 74 * KIB
-CONTEXTS_AT = 82 * KIB
-W1_MID_AT = 89 * KIB
-FIRST_GROUPED_AT = 91 * KIB
-W3_MID_AT = 93 * KIB
-DEALT_AT = 96 * KIB
-LAST_STATES_AT = 112 * KIB
-H_VALS_AT = 116 * KIB
-PAGES_AT = 124 * KIB
-FACTORS_AT = 156 * KIB
-W1_RAW_AT = FACTORS_AT
-W3_RAW_AT = LATE_AT
-PLANE_AT = FIRST_AT + 12 * KIB
-H_HOMES = {2: PICKS_AT + 2 * KIB, 4: PICKS_AT + 4 * KIB, 6: PICKS_AT + 6 * KIB, 11: W5_AT - KIB, 12: W56_PLANE_AT, 13: W6_AT - KIB}
-PICK_HOMES = {0: GROUPED_AT + 12 * KIB, 1: PICKS_AT + 2 * KIB, 2: PICKS_AT + 4 * KIB, 3: PICKS_AT + 6 * KIB,
-              4: W5_AT - 2 * KIB, 5: PICKS_AT, 6: H_VALS_AT + 2 * KIB * (10 % H_SLOTS)}
+TABLE_AT = 0
+PAGE1_AT = 16 * KIB
+RAW_AT = 24 * KIB
+GROUPED_AT = 40 * KIB
+FIRST_AT = 56 * KIB
+STATES_AT = 72 * KIB
+PICKS_AT = 80 * KIB
+PICKED_AT = 90 * KIB
+Z0_AT = 88 * KIB
+DEALT_AT = 98 * KIB
+LAST_PICK_AT = 110 * KIB
+Z_ROWS_AT = 112 * KIB
+W4_RAW_AT = 116 * KIB
+STATE_SLOTS = 4
+GROUPS = {0: (0, P), 1: (2 * KIB, P), 2: (4 * KIB, 2 * P), 4: (8 * KIB, 2 * P), 6: (12 * KIB, 2 * P)}
 
 
 def tile_list_resumed_session_features_kernel(
@@ -99,6 +88,9 @@ def tile_list_resumed_session_features_kernel(
                 in_=planar.rearrange("p t (c i) -> p c t i", i=4),
             )
 
+        def gpsimd_round(out, in_):
+            nc.gpsimd.tensor_scalar(out, in_, 1.0, 0.0, MULT, ADD)
+
         def add_transposed(sum_blocks, early, late):
             n = len(sum_blocks)
             for i in range(n):
@@ -112,15 +104,19 @@ def tile_list_resumed_session_features_kernel(
             nc.vector.quantize_mx(out=codes[:].bitcast(E4M3), scales=plane[:], in_=grouped)
             return codes, plane
 
-        w1_rows = w1.rearrange("(p t) r -> p t r", t=PACK)
-        w3_rows = w3.rearrange("(p t) r -> p t r", t=PACK)
+        rows13 = {"w1": w1.rearrange("(p t) r -> p t r", t=PACK), "w3": w3.rearrange("(p t) r -> p t r", t=PACK)}
+        raw = {}
 
         def load_columns(name, rows, start, width, offset):
-            raw = shared.tile([P, PACK, width], F32, name=name, offset=offset)
-            nc.sync.dma_start(out=raw[:], in_=rows[:, :, start : start + width])
-            return raw
+            tile = shared.tile([P, PACK, width], F32, name=name, offset=offset)
+            nc.sync.dma_start(out=tile[:], in_=rows[:, :, start : start + width])
+            return tile
 
-        table_plane = shared.tile([P, 1, T], U8, name="table_plane", offset=PLANE_AT)
+        def load_w13(first, width, offset):
+            for i, name in enumerate(("w1", "w3")):
+                raw[name, first] = load_columns("%s_raw%d" % (name, first), rows13[name], first * P, width, offset + 16 * width * i)
+
+        table_plane = shared.tile([P, 1, T], U8, name="table_plane", offset=PAGE1_AT)
         nc.vector.memset(table_plane[:].bitcast(I32), 0)
         w2_plane = keep.tile([P, 1, H], U8, name="w2_plane", align_bytes=64)
         nc.gpsimd.memset(w2_plane[:].bitcast(I32), 0)
@@ -129,226 +125,196 @@ def tile_list_resumed_session_features_kernel(
         list2 = lists.tile([P, S // STRIPE], U16, name="list2")
         list3 = lists.tile([P, M // STRIPE], U16, name="list3")
         nc.sync.dma_start(list1[:], offs)
-        nc.sync.dma_start(list2[:], offs2)
-        nc.sync.dma_start(list3[:], offs3)
-        raw = {}
-        raw["w1", 0] = load_columns("w1_raw0", w1_rows, 0, 2 * P, W1_RAW_AT)
-        raw["w3", 0] = load_columns("w3_raw0", w3_rows, 0, 2 * P, W3_RAW_AT)
+        load_w13(0, P, RAW_AT)
         load_scale_rows(nc.sync, table_plane, tab_scales)
         table = shared.tile([P, T], I32, name="table", offset=TABLE_AT)
         nc.sync.dma_start(out=table[:], in_=tab_words[0].rearrange("p t i -> p (t i)").bitcast(I32))
-        w2_codes = keep.tile([P, 2 * H], U8, name="w2_codes", align_bytes=64)
-        nc.sync.dma_start(out=w2_codes[:].bitcast(I32), in_=w2_words[0].bitcast(I32))
-        load_scale_rows(nc.gpsimd, w2_plane, w2_scales)
-        w13 = {}
+        load_scale_rows(nc.sync, w2_plane, w2_scales)
+        w2_codes = [keep.tile([P, H], U8, name="w2_codes%d" % g, align_bytes=64) for g in range(2)]
+        nc.sync.dma_start(out=w2_codes[0][:].bitcast(I32), in_=w2_words[0][:, 0:H].bitcast(I32))
+        factors = [keep.tile([P, HALF], F32, name="factors%d" % h) for h in range(2)]
+        load_w13(1, P, RAW_AT + 4 * KIB)
+        nc.sync.dma_start(out=factors[0][:], in_=wgs[:, 0:HALF])
+        nc.sync.dma_start(list2[:], offs2)
+        load_w13(2, 2 * P, RAW_AT + 8 * KIB)
+        nc.sync.dma_start(out=factors[1][:], in_=wgs[:, HALF:S])
+        nc.sync.dma_start(list3[:], offs3)
+        load_w13(PACK, PASS_ROWS, TABLE_AT)
+        nc.sync.dma_start(out=w2_codes[1][:].bitcast(I32), in_=w2_words[0][:, H : 2 * H].bitcast(I32))
+        dealt_factors = []
 
-        def quantize_both(first, grouped, width):
-            codes, plane = quantize("w13_%d" % first, grouped[:].rearrange("p w r t -> p (w r t)"), 2 * width)
-            for i, name in enumerate(("w1", "w3")):
-                w13[name, first] = (codes[:, i * width : (i + 1) * width], plane[:, i * width : (i + 1) * width])
+        def load_dealt_factors():
+            t = len(dealt_factors)
+            dealt_factors.append(keep.tile([P, S], F32, name="dealt_factors%d" % t))
+            for quad in (0, 2, 1, 3):
+                nc.sync.dma_start(
+                    out=dealt_factors[t][QUADRANT * quad : QUADRANT * (quad + 1)],
+                    in_=wgs.rearrange("(q t) j -> t q j", t=PACK)[t],
+                )
 
-        first_grouped = shared.tile([P, 2, 2 * P, PACK], BF16, name="first_grouped", align_bytes=64, offset=FIRST_GROUPED_AT)
-        for i, name in enumerate(("w1", "w3")):
-            interleave(nc.scalar.copy, first_grouped[:, i], raw[name, 0][:])
-        quantize_both(0, first_grouped, 2 * P)
-        factors = [shared.tile([P, HALF], F32, name="factors%d" % h, offset=FACTORS_AT + 4 * HALF * h) for h in range(2)]
-        for h in range(2):
-            nc.sync.dma_start(out=factors[h][:], in_=wgs[:, h * HALF : (h + 1) * HALF])
-        raw["w1", 2] = load_columns("w1_raw2", w1_rows, 2 * P, 2 * P, W1_MID_AT)
-        raw["w3", 2] = load_columns("w3_raw2", w3_rows, 2 * P, 2 * P, W3_MID_AT)
-        raw["w1", 4] = load_columns("w1_raw4", w1_rows, PASS_ROWS, PASS_ROWS, TABLE_AT)
-        raw["w3", 4] = load_columns("w3_raw4", w3_rows, PASS_ROWS, PASS_ROWS, TABLE_AT + 8 * KIB)
-        plain_contexts = shared.tile([P, PACK, M], F32, name="plain_contexts", offset=CONTEXTS_AT)
+        plain_contexts = shared.tile([P, PACK, M], F32, name="plain_contexts", offset=RAW_AT)
         nc.sync.dma_start(out=plain_contexts[:], in_=ctx[0:PASS_ROWS].rearrange("(c p) m -> p c m", p=P))
-        dealt_factors = shared.tile([P, PACK, S], F32, name="dealt_factors", offset=DEALT_AT)
-        for quad in (0, 2, 1, 3):
-            nc.sync.dma_start(
-                out=dealt_factors[QUADRANT * quad : QUADRANT * (quad + 1)],
-                in_=wgs.rearrange("(q t) j -> q t j", t=PACK),
-            )
-        w4_rows = w4.rearrange("(g p t) n -> g p t n", p=P, t=PACK)
-        for g in range(2):
-            raw["w4", g] = load_columns("w4_raw%d" % g, w4_rows[g], 0, N, 8 * KIB * g)
-        w6_raw = shared.tile([P, 2, N], I32, name="w6_raw", offset=W1_MID_AT + KIB)
+        w6_raw = keep.tile([P, 2, N], I32, name="w6_raw")
         nc.sync.dma_start(out=w6_raw[:], in_=w6_words.rearrange("g p n t -> p g (n t)").bitcast(I32))
-        w5_raw = shared.tile([P, 2, N], U16, name="w5_raw", offset=W3_MID_AT + KIB)
+        load_dealt_factors()
+        w5_raw = keep.tile([P, 2, N], U16, name="w5_raw")
         nc.sync.dma_start(out=w5_raw[:].bitcast(I32), in_=w5_words.rearrange("g p n -> p g n").bitcast(I32))
+        w56_raw_plane = keep.tile([P, 2, N], U8, name="w56_raw_plane")
+        nc.gpsimd.memset(w56_raw_plane[:].bitcast(I32), 0)
+        for t in range(1, PACK):
+            load_dealt_factors()
+        load_scale_rows(nc.sync, w56_raw_plane, w5_scales)
+        load_scale_rows(nc.sync, w56_raw_plane, w6_scales, shift=4)
+        w4_rows = w4.rearrange("(g p t) n -> g p t n", p=P, t=PACK)
+        w4_raw = [load_columns("w4_raw%d" % g, w4_rows[g], 0, N, W4_RAW_AT + 8 * KIB * g) for g in range(2)]
 
         identity = keep.tile([P, P], F32, name="identity")
         make_identity(nc, identity[:])
 
-        def round_middle():
-            grouped = shared.tile([P, 2, 2 * P, PACK], BF16, name="middle_grouped", align_bytes=64, offset=GROUPED_AT + 4 * KIB)
-            for i, name in enumerate(("w1", "w3")):
-                planar = raw[name, 2]
-                interleave(nc.scalar.copy, grouped[:, i, 0:P], planar[:, :, 0:P])
-                nc.gpsimd.tensor_scalar(
-                    grouped[:, i, P : 2 * P], planar[:, :, P : 2 * P].rearrange("p t c -> p c t"), 1.0, 0.0, MULT, ADD,
+        grouped13 = {}
+        w13 = {}
+
+        def group_tile(first):
+            if first not in grouped13:
+                at, width = GROUPS[first]
+                grouped13[first] = shared.tile([P, 2, width, PACK], BF16, name="grouped%d" % first, align_bytes=64, offset=GROUPED_AT + at)
+            return grouped13[first]
+
+        def round_w13(first, i, engine_copy):
+            name = ("w1", "w3")[i]
+            if first < PACK:
+                interleave(engine_copy, group_tile(first)[:, i], raw[name, first][:])
+            else:
+                t = first - PACK
+                engine_copy(
+                    out=group_tile(first)[:, i].rearrange("p (t q) i -> p q t i", t=2),
+                    in_=raw[name, PACK][:].rearrange("p i (q t) -> p q t i", t=PACK)[:, :, t : t + 2, :],
                 )
-            quantize_both(2, grouped, 2 * P)
 
-        late_grouped = shared.tile([P, 2, PASS_ROWS, PACK], BF16, name="late_grouped", align_bytes=64, offset=GROUPED_AT + 8 * KIB)
-
-        def round_late(half):
-            cols = slice(half * 2 * P, (half + 1) * 2 * P)
+        def quantize_w13(first):
+            width = GROUPS[first][1]
+            codes, plane = quantize("w13_%d" % first, grouped13[first][:].rearrange("p w r t -> p (w r t)"), 2 * width)
             for i, name in enumerate(("w1", "w3")):
-                interleave(nc.scalar.copy, late_grouped[:, i, cols], raw[name, PACK][:, :, cols])
+                for c in range(width // P):
+                    cols = slice(i * width + c * P, i * width + (c + 1) * P)
+                    w13[name, first + c] = (codes[:, cols].bitcast(E4M3), plane[:, cols])
 
+        dealt = {}
+        w2_dealt_plane = keep.tile([P, PASS_ROWS], U8, name="w2_dealt_plane", align_bytes=64)
+
+        def page_weights(c):
+            t = c % PACK
+            if c < PACK:
+                w2_page = (w2_codes[0][:, 2 * P * t : 2 * P * (t + 1)].bitcast(E2M1), w2_plane[:, 0, P * t : P * (t + 1)])
+            else:
+                w2_page = (dealt["w2"][:, 2 * P * t : 2 * P * (t + 1)].bitcast(E2M1), w2_dealt_plane[:, P * t : P * (t + 1)])
+            return w2_page, w13["w1", c], w13["w3", c]
+
+        pages = [keep.tile([P, T2], F32, name="page0")]
+        nc.vector.memset(pages[0][:].bitcast(I32), 0)
+        for i in range(2):
+            round_w13(0, i, nc.scalar.copy)
+        quantize_w13(0)
         v_codes = [keep.tile([P, HALF], U32, name="v_codes%d" % h, align_bytes=64) for h in range(2)]
         v_plane = keep.tile([P, S], U8, name="v_plane", align_bytes=64)
         nc.vector.tensor_copy(v_plane[:], table_plane[:, 0, :].indirect(list1[:]))
         v_planes = [v_plane[:, h * HALF : (h + 1) * HALF] for h in range(2)]
         for h in range(2):
             nc.vector.tensor_copy(v_codes[h][:], table[:].bitcast(U32).indirect(entries(list1, h * HALF, HALF)))
-        pages = [shared.tile([P, T2], F32, name="page%d" % i, offset=PAGES_AT + 4 * T2 * i) for i in range(PACK)]
-        for page in pages[:2]:
-            nc.vector.memset(page[:].bitcast(I32), 0)
-        for page in pages[2:]:
-            for at in range(0, T2, S):
-                nc.gpsimd.memset(page[:, at : at + S].bitcast(I32), 0)
-        dealt_pages = pages
+        pages.append(shared.tile([P, T2], F32, name="page1", offset=PAGE1_AT))
+        for at in range(0, T2, S):
+            nc.gpsimd.memset(pages[1][:, at : at + S].bitcast(I32), 0)
 
-        def w2_columns(start, width):
-            return w2_codes[:, 2 * start : 2 * (start + width)].bitcast(E2M1), w2_plane[:, 0, start : start + width]
+        nc.gpsimd.tensor_copy(
+            out=w2_dealt_plane[:].rearrange("p (t q) -> p t q", t=PACK),
+            in_=w2_plane[:, 0, PASS_ROWS:H].rearrange("p (q t) -> p t q", t=PACK),
+        )
 
-        def w13_columns(name, start, width):
-            first = max(c for (w, c) in w13 if w == name and c * P <= start)
-            codes, plane = w13[name, first]
-            at = start - first * P
-            return codes[:, at : at + width].bitcast(E4M3), plane[:, at : at + width]
+        first_banks = {}
+        first = {}
 
-        chunk_terms = []
-        for start, count, (b_at, a_at, d_at) in FIRST_CHUNKS:
-            h, at = divmod(start, HALF)
-            banks = [bank(i, "first_terms") for i in (b_at, a_at, d_at)]
-            weights = (w2_columns(0, P), w13_columns("w1", 0, P), w13_columns("w3", 0, P))
-            for term_bank, (codes, plane) in zip(banks, weights):
+        def first_terms(h):
+            first_banks[h] = [bank(i, "first_terms") for i in FIRST_BANKS[h]]
+            for term_bank, (codes, plane) in zip(first_banks[h], page_weights(0)):
                 nc.tensor.matmul_mx(
-                    out=term_bank[:, 0:count], lhsT=codes, lhsT_scale=plane,
-                    rhs=v_codes[h][:, at : at + count].bitcast(E4M3), rhs_scale=v_planes[h][:, at : at + count],
-                    start=True, stop=True,
+                    out=term_bank[:], lhsT=codes, lhsT_scale=plane,
+                    rhs=v_codes[h][:].bitcast(E4M3), rhs_scale=v_planes[h], start=True, stop=True,
                 )
-            b_vals = shared.tile([P, count], F32, name="first_b%d" % start, offset=FIRST_AT + 4 * start)
-            nc.scalar.copy(out=b_vals[:], in_=banks[0][:, 0:count])
-            chunk_terms.append((banks, b_vals))
 
-        def first_product(i):
-            banks, b_vals = chunk_terms[i]
-            count = FIRST_CHUNKS[i][1]
-            product = shared.tile([P, count], F32, name="first_ab%d" % i, offset=FIRST_AT + 4 * (S + FIRST_CHUNKS[i][0]))
-            nc.vector.tensor_tensor(product[:], banks[1][:, 0:count], b_vals[:], MULT)
-            return product
+        def first_tile(kind, h, home=None):
+            at = FIRST_AT + 4 * (S * ("b", "ab", "h", "weighted").index(kind) + HALF * h)
+            first[kind, h] = shared.tile([P, HALF], F32, name="first_%s%d" % (kind, h), offset=at if home is None else home)
+            return first[kind, h][:]
 
-        def first_state(i, product):
-            count = FIRST_CHUNKS[i][1]
-            at = FIRST_AT + 4 * (2 * S + FIRST_CHUNKS[i][0])
-            state = shared.tile([P, count], F32, name="first_h%d" % i, offset=at)
-            nc.vector.tensor_tensor(state[:], chunk_terms[i][0][2][:, 0:count], product[:], ADD)
-            return state
+        def first_b(h):
+            nc.scalar.copy(out=first_tile("b", h), in_=first_banks[h][0][:])
 
-        def weigh(i, state, at):
-            start, count, unused = FIRST_CHUNKS[i]
-            h, first = divmod(start, HALF)
-            weighted = shared.tile([P, count], F32, name="first_weighted%d" % i, offset=at)
-            nc.vector.tensor_tensor(weighted[:], state[:], factors[h][:, first : first + count], MULT)
-            return weighted
+        def first_product(h):
+            nc.vector.tensor_tensor(first_tile("ab", h), first_banks[h][1][:], first["b", h][:], MULT)
 
-        def first_scatter(i, weighted):
-            start, count, unused = FIRST_CHUNKS[i]
-            nc.vector.tensor_copy(pages[0][:].indirect(entries(list2, start, count)), weighted[:])
+        def first_state(h, home=None):
+            nc.vector.tensor_tensor(first_tile("h", h, home), first_banks[h][2][:], first["ab", h][:], ADD)
 
-        early = [first_product(i) for i in range(2)]
-        early = [first_state(i, early[i]) for i in range(2)]
-        nc.vector.tensor_tensor(pages[0][:].indirect(entries(list2, 0, PIECE)), early[0][:], factors[0][:, 0:PIECE], MULT)
-        second = weigh(1, early[1], FIRST_AT + 12 * KIB)
-        late = first_product(2)
-        first_scatter(1, second)
-        late = first_state(2, late)
+        def first_weigh(h, home=None):
+            nc.gpsimd.tensor_tensor(first_tile("weighted", h, home), first["h", h][:], factors[h][:], MULT)
+
+        def first_scatter(h):
+            nc.vector.tensor_copy(pages[0][:].indirect(entries(list2, h * HALF, HALF)), first["weighted", h][:])
 
         products = {}
         addends = {}
         states = {}
-        state_pairs = {}
+
+        def pick_home(c):
+            return LAST_PICK_AT if c == PAGES - 2 else PICKS_AT + 2 * KIB * (c % 4)
+
+        def deal_home(u):
+            return DEALT_AT + 2 * KIB * (u // 2)
 
         def make_terms(u):
+            c, h = 1 + u // 2, u % 2
             banks = [bank(i, "terms") for i in (B_BANKS[u % 2], A_BANK, D_BANK)]
-            if u < PLAIN_STEPS:
-                c, h = PLAIN_ORDER[u]
-                start, width = c * P, P
-                v_blocks = list(zip(blocks(v_codes[h]), blocks(v_planes[h])))
-            else:
-                h, at = divmod(u - PLAIN_STEPS, PACK)
-                start, width = PASS_ROWS, PASS_ROWS
-                v_blocks = [(blocks(v_codes[h])[at], blocks(v_planes[h])[at])]
-            weights = (w2_columns(start, width), w13_columns("w1", start, width), w13_columns("w3", start, width))
-            for term_bank, (codes, plane) in zip(banks, weights):
-                for i, (v_block, v_scale) in enumerate(v_blocks):
+            for term_bank, (codes, plane) in zip(banks, page_weights(c)):
+                for block, v_block, v_scale in zip(blocks(term_bank), blocks(v_codes[h]), blocks(v_planes[h])):
                     nc.tensor.matmul_mx(
-                        out=term_bank[:, i * width : (i + 1) * width], lhsT=v_block.bitcast(E4M3), lhsT_scale=v_scale,
-                        rhs=codes, rhs_scale=plane, start=True, stop=True,
+                        out=block, lhsT=v_block.bitcast(E4M3), lhsT_scale=v_scale, rhs=codes, rhs_scale=plane, start=True, stop=True,
                     )
 
             def copy_out(name, term_bank, bufs):
                 vals = ring.tile([P, BANK], F32, name=name, bufs=bufs)
-                if u < PLAIN_STEPS:
-                    nc.scalar.copy(out=vals[:], in_=term_bank[:])
-                else:
-                    nc.scalar.copy(
-                        out=vals[:].rearrange("j (t p) -> j t p", t=PACK),
-                        in_=term_bank[:].rearrange("j (p t) -> j t p", t=PACK),
-                    )
+                nc.scalar.copy(out=vals[:], in_=term_bank[:])
                 return vals
 
-            b_vals = copy_out("b_vals", banks[0], 3)
-            a_vals = copy_out("a_vals", banks[1], 3)
-            addends[u] = copy_out("d_vals", banks[2], 7)
-            products[u] = ring.tile([P, BANK], F32, name="ab_vals", bufs=7)
+            b_vals = copy_out("b_vals", banks[0], 2)
+            a_vals = copy_out("ad_vals", banks[1], 3)
+            addends[u] = copy_out("ad_vals", banks[2], 3)
+            products[u] = ring.tile([P, BANK], F32, name="ab_vals", bufs=3)
             nc.gpsimd.tensor_tensor(products[u][:], a_vals[:], b_vals[:], MULT)
 
-        def make_states(s):
-            if s < PLAIN_STEPS:
-                if s not in products:
-                    make_terms(s)
-                early_blocks, late_blocks = blocks(addends[s]), blocks(products[s])
-                factor = factors[PLAIN_ORDER[s][1]][:].rearrange("p (i j) -> p i j", i=2)
+        def make_states(u):
+            c, h = 1 + u // 2, u % 2
+            factor = factors[h][:] if c < PACK else dealt_factors[c - PACK][:, h * HALF : (h + 1) * HALF]
+            h_bank = bank(H_BANKS[u % 2], "h_bank")
+            add_transposed(blocks(h_bank), blocks(addends[u]), blocks(products[u]))
+            if u == STEPS - 1:
+                plain = shared.tile([P, BANK], F32, name="last_h_vals", offset=PICKED_AT - KIB // 2)
+            elif u % 2 == 0:
+                plain = shared.tile([P, BANK], F32, name="h_vals%d" % u, offset=pick_home(u // 2))
             else:
-                ts, start, count = DEALT_STEPS[s - PLAIN_STEPS]
-                units = range(PLAIN_STEPS + start // P, PLAIN_STEPS + (start + count) // P)
-                for u in units:
-                    if u not in products:
-                        make_terms(u)
-                early_blocks = [blocks(addends[u])[t] for t in ts for u in units]
-                late_blocks = [blocks(products[u])[t] for t in ts for u in units]
-                factor = dealt_factors[:, ts[0] : ts[-1] + 1, start : start + count]
-                if len(ts) == 1:
-                    factor = factor.rearrange("p o (i j) -> p (o i) j", i=2)
-            h_bank = bank(H_BANKS[s % 2], "h_bank")
-            add_transposed(blocks(h_bank), early_blocks, late_blocks)
-            plain = shared.tile([P, BANK], F32, name="h_vals%d" % s, offset=H_HOMES.get(s, H_VALS_AT + 2 * KIB * (s % H_SLOTS)))
+                plain = shared.tile([P, BANK], F32, name="h_vals%d" % u, offset=deal_home(u))
             nc.scalar.copy(out=plain[:], in_=h_bank[:])
-            if s == STEPS - 1:
-                states[s] = shared.tile([P, BANK], F32, name="last_states", offset=LAST_STATES_AT + KIB)[:]
-            else:
-                if s % 2 == 0:
-                    state_pairs[s // 2] = ring.tile([P, S], F32, name="states", bufs=3)
-                states[s] = state_pairs[s // 2][:, (s % 2) * HALF : (s % 2 + 1) * HALF]
-            nc.gpsimd.tensor_tensor(
-                states[s].rearrange("p (i j) -> p i j", i=2), plain[:].rearrange("p (i j) -> p i j", i=2), factor, MULT,
-            )
+            states[u] = shared.tile([P, HALF], F32, name="states%d" % u, offset=STATES_AT + 2 * KIB * (u % STATE_SLOTS))
+            nc.gpsimd.tensor_tensor(states[u][:], plain[:], factor, MULT)
 
-        def scatter(s):
-            ts, start, count = DEALT_STEPS[s - PLAIN_STEPS]
-            for i, t in enumerate(ts):
-                nc.vector.tensor_copy(
-                    dealt_pages[t][:].indirect(entries(list2, start, count)), states[s][:, i * count : (i + 1) * count],
-                )
+        def scatter(u):
+            nc.vector.tensor_copy(pages[(1 + u // 2) % 2][:].indirect(entries(list2, (u % 2) * HALF, HALF)), states[u][:])
 
-        z_rows = shared.tile([P, QUARTERS, 2, P, 2], BF16, name="z_rows", offset=GROUPED_AT)
+        z_rows = shared.tile([P, QUARTERS, 2, P, 2], BF16, name="z_rows", offset=Z_ROWS_AT)
         picks = {}
 
         def pick(c):
-            picks[c] = shared.tile([P, M], F32, name="picked%d" % c, offset=PICK_HOMES[c])
-            nc.vector.tensor_copy(picks[c][:], pages[PAGE_TILES[c]][:].indirect(list3[:]))
+            picks[c] = shared.tile([P, M], F32, name="picked%d" % c, offset=pick_home(c))
+            nc.vector.tensor_copy(picks[c][:], pages[c % 2][:].indirect(list3[:]))
 
         def place(c, bank_index):
             z_bank = bank(bank_index, "z_bank")
@@ -359,48 +325,52 @@ def tile_list_resumed_session_features_kernel(
                 in_=z_bank[:].rearrange("m (b p u e) -> m b u p e", b=QUARTERS, u=2, e=2),
             )
 
-        def quantize_first_pass():
+        z0_grouped = keep.tile([P, 2, 2 * P * PACK], BF16, name="z_grouped0", align_bytes=64)
+
+        def turn_first_pass(mh, bank_index):
             z_words = blocks(z_rows[:].rearrange("m b u p e -> m (b u p e)").bitcast(F32))
-            grouped = shared.tile([P, 2, 2 * P * PACK], BF16, name="z_grouped0", align_bytes=64, offset=GROUPED_AT + 4 * KIB)
-            for mh in range(2):
-                word_bank = bank(WORD_BANKS[mh], "word_bank")
-                for turned, block in zip(blocks(word_bank), z_words[4 * mh : 4 * mh + 4]):
-                    nc.tensor.transpose(turned, block, identity[:])
-                nc.scalar.copy(
-                    out=grouped[:, mh, :].bitcast(F32).rearrange("p (b m u) -> p b m u", b=2, u=2),
-                    in_=word_bank[:].rearrange("p (b u m) -> p b m u", b=2, u=2),
-                )
-            return grouped
+            word_bank = bank(bank_index, "word_bank")
+            for turned, block in zip(blocks(word_bank), z_words[4 * mh : 4 * mh + 4]):
+                nc.tensor.transpose(turned, block, identity[:])
+            nc.scalar.copy(
+                out=z0_grouped[:, mh, :].bitcast(F32).rearrange("p (b m u) -> p b m u", b=2, u=2),
+                in_=word_bank[:].rearrange("p (b u m) -> p b m u", b=2, u=2),
+            )
 
         w4_grouped = {}
 
-        def round_w4(g, half):
-            if half == 0:
-                w4_grouped[g] = shared.tile([P, PACK, P, PACK], BF16, name="w4_grouped%d" % g, align_bytes=64, offset=LATE_AT + 4 * KIB * g)
-            qs = slice(half * P // 2, (half + 1) * P // 2)
+        def round_w4(g):
+            w4_grouped[g] = shared.tile([P, PACK, P, PACK], BF16, name="w4_grouped%d" % g, align_bytes=64, offset=(PICKS_AT + 4 * KIB, Z_ROWS_AT)[g])
             nc.scalar.copy(
-                out=w4_grouped[g][:].rearrange("p t q i -> p q t i")[:, qs],
-                in_=raw["w4", g][:].rearrange("p i (q t) -> p q t i", t=PACK)[:, qs],
+                out=w4_grouped[g][:].rearrange("p t q i -> p q t i"),
+                in_=w4_raw[g][:].rearrange("p i (q t) -> p q t i", t=PACK),
             )
 
-        def deal(engine_copy, dealt, plain, g):
-            engine_copy(
-                out=dealt[:, g, :].rearrange("p (t q) -> p t q", t=PACK),
-                in_=plain[:, g, :].rearrange("p (q t) -> p t q", t=PACK),
+        def deal(dealt, plain):
+            nc.gpsimd.tensor_copy(out=dealt.rearrange("p (t q) -> p t q", t=PACK), in_=plain.rearrange("p (q t) -> p t q", t=PACK))
+
+        def deal_pairs(dealt, plain):
+            nc.gpsimd.tensor_copy(
+                out=dealt.rearrange("p (t q b) -> p t q b", t=PACK, b=2), in_=plain.rearrange("p (q t b) -> p t q b", t=PACK, b=2),
             )
 
-        dealt_contexts = shared.tile([P, PACK, M], F32, name="dealt_contexts", offset=FIRST_AT + 8 * KIB)
-        make_terms(0)
-        round_middle()
-        first_scatter(2, weigh(2, late, GROUPED_AT + 4 * KIB))
-        for s in range(AHEAD):
-            make_states(s)
+        def dealt_tile(key, shape, dtype, u):
+            dealt[key] = shared.tile(shape, dtype, name="dealt%d" % u, align_bytes=64, offset=deal_home(u))
+            return dealt[key]
 
-        def pick_add(t, q):
-            nc.vector.tensor_tensor(
-                picked[:, q, t, :], dealt_pages[t][:].indirect(entries(list3, q * P, P)),
-                dealt_contexts[:, t, q * P : (q + 1) * P], ADD,
-            )
+        def deal_after(u):
+            if u == 1:
+                deal_pairs(dealt_tile("w2", [P, H], U8, u)[:], w2_codes[1][:])
+            elif u < 7:
+                g = (u - 3) // 2
+                deal(dealt_tile(("w6", g), [P, N], I32, u)[:], w6_raw[:, g, :])
+            elif u < 11:
+                g = (u - 7) // 2
+                deal_pairs(dealt_tile(("w5", g), [P, 2 * N], U8, u)[:], w5_raw[:, g, :].bitcast(U8))
+            else:
+                plane = dealt_tile("plane", [P, 2, N], U8, u)
+                for g in range(2):
+                    deal(plane[:, g, :], w56_raw_plane[:, g, :])
 
         def add_context(t):
             nc.gpsimd.tensor_tensor(
@@ -408,73 +378,76 @@ def tile_list_resumed_session_features_kernel(
                 dealt_contexts[:, t, :].rearrange("p (q m) -> p q m", q=QUARTERS), ADD,
             )
 
-        for s in range(STEPS):
-            if s + AHEAD < STEPS:
-                make_states(s + AHEAD)
-            if s == 3:
-                for u in (6, 7):
-                    make_terms(u)
-            if PLAIN_STEPS <= s < PLAIN_STEPS + 2:
-                for u in (2 * s - 2, 2 * s - 1):
-                    make_terms(u)
-            if s + AHEAD == STEPS - 1:
-                w6_codes = shared.tile([P, 2, N], I32, name="w6_codes", align_bytes=64, offset=W6_AT)
-                w5_codes = shared.tile([P, 2, N], U16, name="w5_codes", align_bytes=64, offset=W5_AT)
-                w56_plane = shared.tile([P, 2, N], U8, name="w56_plane", align_bytes=64, offset=W56_PLANE_AT)
-                for g in range(2):
-                    deal(nc.gpsimd.tensor_copy, w6_codes, w6_raw, g)
-                    deal(nc.gpsimd.tensor_copy, w56_plane, w56_raw_plane, g)
-                nc.vector.tensor_copy(
-                    out=w5_codes[:].rearrange("p g (t q) -> p g t q", t=PACK),
-                    in_=w5_raw[:].rearrange("p g (q t) -> p g t q", t=PACK),
-                )
-            if s == 0:
-                round_late(0)
-                round_late(1)
-                quantize_both(PACK, late_grouped, PASS_ROWS)
-            if s == 2:
-                w56_raw_plane = shared.tile([P, 2, N], U8, name="w56_raw_plane", offset=16 * KIB)
-                nc.gpsimd.memset(w56_raw_plane[:].bitcast(I32), 0)
-                load_scale_rows(nc.sync, w56_raw_plane, w5_scales)
-                load_scale_rows(nc.sync, w56_raw_plane, w6_scales, shift=4)
-                nc.sync.dma_start(out=dealt_contexts[:], in_=ctx[PASS_ROWS:H].rearrange("(p t) m -> p t m", t=PACK))
-            if s < PLAIN_STEPS:
-                c, h = PLAIN_ORDER[s]
-                nc.vector.tensor_copy(pages[PAGE_TILES[c]][:].indirect(entries(list2, h * HALF, HALF)), states[s])
-                if s % 2 == 0:
-                    pick(s // 2)
-            else:
-                scatter(s)
-            if s == PLAIN_STEPS:
-                pick(PACK - 1)
-            if s == STEPS - PACK + 1:
-                picked = shared.tile([P, QUARTERS, PACK, P], F32, name="z_vals", offset=LATE_AT + 8 * KIB)
-            t = s - (STEPS - PACK) - 1
-            if 0 <= t < 2:
-                pick(PACK + t)
-                add_context(t)
-            if t == 1:
-                pick(PACK + 2)
-                add_context(2)
-                z0_codes = shared.tile([P, M], U32, name="z0_codes", align_bytes=64, offset=PAGES_AT + 4 * T2)
+        first_terms(0)
+        first_b(0)
+        for i in range(2):
+            round_w13(1, i, nc.scalar.copy)
+        first_product(0)
+        quantize_w13(1)
+        first_state(0, GROUPED_AT + GROUPS[1][0])
+        first_weigh(0)
+        first_terms(1)
+        first_b(1)
+        first_product(1)
+        first_state(1)
+        first_scatter(0)
+        make_terms(0)
+        for i in range(2):
+            round_w13(2, i, nc.scalar.copy)
+        quantize_w13(2)
+        first_weigh(1, RAW_AT + 12 * KIB)
+        first_scatter(1)
+        dealt_contexts = shared.tile([P, PACK, M], F32, name="dealt_contexts", offset=RAW_AT + 8 * KIB)
+        nc.sync.dma_start(out=dealt_contexts[:], in_=ctx[PASS_ROWS:H].rearrange("(p t) m -> p t m", t=PACK))
+        make_terms(1)
+        make_states(0)
+        for u in range(STEPS):
+            if u + 2 < STEPS:
+                make_terms(u + 2)
+            if u + 1 < STEPS:
+                make_states(u + 1)
+            if u in (0, 1, 3, 4):
+                round_w13(PACK + 2 * (u // 3), u % 3, nc.scalar.copy)
+                if u % 3 == 1:
+                    quantize_w13(PACK + 2 * (u // 3))
+            if u % 2 == 0 and u + 2 < STEPS:
+                deal_after(u + 1)
+            if u % 2 == 0 and 2 <= u < 10:
+                place(u // 2 - 1, H_BANKS[(u + 1) % 2])
+            if u in (9, 10):
+                turn_first_pass(u - 9, H_BANKS[(u + 1) % 2])
+            if u in (9, 11):
+                round_w4((u - 9) // 2)
+            if u < STEPS - 1:
+                scatter(u)
+            if u % 2 == 0:
+                pick(u // 2)
+            if u == STEPS - 1:
+                z0_codes = shared.tile([P, M], U32, name="z0_codes", align_bytes=64, offset=Z0_AT)
                 z0_plane = keep.tile([P, M], U8, name="z0_plane", align_bytes=64)
                 nc.vector.quantize_mx(
                     out=z0_codes[:].bitcast(E4M3), scales=z0_plane[:], in_=z0_grouped[:].rearrange("p h c -> p (h c)"),
                 )
-            if PLAIN_STEPS <= s < PLAIN_STEPS + PACK:
-                place(s - PLAIN_STEPS, H_BANKS[(s + AHEAD) % 2])
-            if s == STEPS - PACK:
-                z0_grouped = quantize_first_pass()
-            if s >= STEPS - PACK:
-                round_w4(*divmod(s - (STEPS - PACK), 2))
+                scatter(u)
+            if u == STEPS - 2:
+                picked = shared.tile([P, QUARTERS, PACK, P], F32, name="z_vals", offset=PICKED_AT)
+                for t in range(PACK - 1):
+                    add_context(t)
+
+        def pick_add(t, q):
+            nc.vector.tensor_tensor(
+                picked[:, q, t, :], pages[1][:].indirect(entries(list3, q * P, P)),
+                dealt_contexts[:, t, q * P : (q + 1) * P], ADD,
+            )
 
         z1 = {}
-        w4_codes = shared.tile([P, 2, N], U32, name="w4_codes", align_bytes=64, offset=LAST_STATES_AT)
+        w4_codes = {}
         w4_plane = keep.tile([P, 2, N], U8, name="w4_plane", align_bytes=64)
 
         def quantize_w4(g):
+            w4_codes[g] = shared.tile([P, N], U32, name="w4_codes%d" % g, align_bytes=64, offset=STATES_AT + KIB * (1 + 2 * g))
             nc.vector.quantize_mx(
-                out=w4_codes[:, g, :].bitcast(E4M3), scales=w4_plane[:, g, :],
+                out=w4_codes[g][:].bitcast(E4M3), scales=w4_plane[:, g, :],
                 in_=w4_grouped[g][:].rearrange("p t q i -> p (t q i)"),
             )
 
@@ -482,7 +455,7 @@ def tile_list_resumed_session_features_kernel(
         for q in range(QUARTERS):
             pick_add(PACK - 1, q)
         for q in range(QUARTERS):
-            grouped = shared.tile([P, P, PACK], BF16, name="z_grouped1%d" % q, align_bytes=64, offset=GROUPED_AT + KIB * (8 + q))
+            grouped = shared.tile([P, P, PACK], BF16, name="z_grouped1%d" % q, align_bytes=64, offset=GROUPED_AT + KIB * q)
             interleave(nc.scalar.copy, grouped[:], picked[:, q])
             z1[q] = quantize("z1%d" % q, grouped[:].rearrange("p m t -> p (m t)"), P)
             if q == 0:
@@ -491,10 +464,10 @@ def tile_list_resumed_session_features_kernel(
         def stationary(name, g, t):
             cols = slice(t * P, (t + 1) * P)
             if name == "gate":
-                return w5_codes[:, g, cols].bitcast(U8).bitcast(E2M1), w56_plane[:, g, cols]
+                return dealt["w5", g][:, 2 * t * P : 2 * (t + 1) * P].bitcast(E2M1), dealt["plane"][:, g, cols]
             if name == "more":
-                return w6_codes[:, g, cols].bitcast(E4M3), w56_plane[4:P, g, cols]
-            return w4_codes[:, g, cols].bitcast(E4M3), w4_plane[:, g, cols]
+                return dealt["w6", g][:, cols].bitcast(E4M3), dealt["plane"][4:P, g, cols]
+            return w4_codes[g][:, cols].bitcast(E4M3), w4_plane[:, g, cols]
 
         names = ("gate", "more", "base")
         slots = [(q, name) for q in range(QUARTERS) for name in names]
@@ -527,7 +500,7 @@ def tile_list_resumed_session_features_kernel(
             y_vals = shared.tile([P, PACK, P], F32, name="y_vals%d" % q, offset=FIRST_AT + 2 * KIB * (4 + q))
             nc.vector.scalar_tensor_tensor(y_vals[:].rearrange("p t m -> p (t m)"), gated[:], 0.5, sums[q, "base"][:], MULT, ADD)
             nc.sync.dma_start(out=out_rows[:, :, cols], in_=y_vals[:])
-            y_grouped = shared.tile([P, P, PACK], BF16, name="y_grouped%d" % q, align_bytes=64, offset=GROUPED_AT + KIB * q)
+            y_grouped = shared.tile([P, P, PACK], BF16, name="y_grouped%d" % q, align_bytes=64, offset=GROUPED_AT + KIB * (8 + q))
             interleave(nc.scalar.copy if q < QUARTERS - 1 else nc.vector.tensor_copy, y_grouped[:], y_vals[:])
             nc.vector.quantize_mx(
                 out=y_codes[:, cols].bitcast(E4M3), scales=y_plane[:, cols],

@@ -29,15 +29,15 @@ CHUNK = 256
 QUARTERS = M // P
 PAGES = H // P
 STEPS = 2 * (PAGES - 1)
-AHEAD = 2
+SPREAD = 8
 
-FIRST_BANKS = ((0, 1, 2), (3, 4, 5))
-B_BANKS, A_BANK, D_BANK, H_BANKS = (0, 3), 6, 7, (1, 2)
-WORD_BANKS = (4, 5)
-SUM_BANKS = (0, 3, 6, 7, 4, 5, 1, 2)
+FIRST_BANKS = ((4, 5, 1), (4, 2, 5))
+B_BANKS, A_BANK, D_BANK, H_BANKS = (1, 2), 6, 7, (0, 3)
+SUM_BANKS = (1, 2, 6, 7, 4, 5, 0, 3)
 KIB = 1024
 TABLE_AT = 0
 PAGE1_AT = 16 * KIB
+PLANE_AT = 24 * KIB
 RAW_AT = 24 * KIB
 GROUPED_AT = 40 * KIB
 FIRST_AT = 56 * KIB
@@ -98,8 +98,11 @@ def tile_list_resumed_session_features_kernel(
             for i in range(n):
                 nc.tensor.matmul(sum_blocks[i], lhsT=late[i], rhs=identity[:], is_transpose=True, start=False, stop=(i == n - 1))
 
-        def quantize(name, grouped, width):
-            codes = keep.tile([P, width], U32, name=name + "_codes", align_bytes=64)
+        def quantize(name, grouped, width, home=None):
+            if home is None:
+                codes = keep.tile([P, width], U32, name=name + "_codes", align_bytes=64)
+            else:
+                codes = shared.tile([P, width], U32, name=name + "_codes", align_bytes=64, offset=home)
             plane = keep.tile([P, width], U8, name=name + "_plane", align_bytes=64)
             nc.vector.quantize_mx(out=codes[:].bitcast(E4M3), scales=plane[:], in_=grouped)
             return codes, plane
@@ -116,29 +119,36 @@ def tile_list_resumed_session_features_kernel(
             for i, name in enumerate(("w1", "w3")):
                 raw[name, first] = load_columns("%s_raw%d" % (name, first), rows13[name], first * P, width, offset + 16 * width * i)
 
-        table_plane = shared.tile([P, 1, T], U8, name="table_plane", offset=PAGE1_AT)
+        table_plane = shared.tile([P, 1, T], U8, name="table_plane", offset=PLANE_AT - KIB)
         nc.vector.memset(table_plane[:].bitcast(I32), 0)
         w2_plane = keep.tile([P, 1, H], U8, name="w2_plane", align_bytes=64)
         nc.gpsimd.memset(w2_plane[:].bitcast(I32), 0)
+        load_scale_rows(nc.gpsimd, w2_plane, w2_scales)
 
         list1 = lists.tile([P, S // STRIPE], U16, name="list1")
         list2 = lists.tile([P, S // STRIPE], U16, name="list2")
         list3 = lists.tile([P, M // STRIPE], U16, name="list3")
         nc.sync.dma_start(list1[:], offs)
-        load_w13(0, P, RAW_AT)
-        load_scale_rows(nc.sync, table_plane, tab_scales)
-        table = shared.tile([P, T], I32, name="table", offset=TABLE_AT)
-        nc.sync.dma_start(out=table[:], in_=tab_words[0].rearrange("p t i -> p (t i)").bitcast(I32))
-        load_scale_rows(nc.sync, w2_plane, w2_scales)
+        load_w13(0, P, RAW_AT + 4 * KIB)
         w2_codes = [keep.tile([P, H], U8, name="w2_codes%d" % g, align_bytes=64) for g in range(2)]
         nc.sync.dma_start(out=w2_codes[0][:].bitcast(I32), in_=w2_words[0][:, 0:H].bitcast(I32))
+        nc.sync.dma_start(out=table_plane[0:P:SPREAD, 0, :].bitcast(I32), in_=tab_scales[0].bitcast(I32))
+        table = shared.tile([P, T], I32, name="table", offset=TABLE_AT)
+        nc.sync.dma_start(out=table[:], in_=tab_words[0].rearrange("p t i -> p (t i)").bitcast(I32))
         factors = [keep.tile([P, HALF], F32, name="factors%d" % h) for h in range(2)]
-        load_w13(1, P, RAW_AT + 4 * KIB)
         nc.sync.dma_start(out=factors[0][:], in_=wgs[:, 0:HALF])
         nc.sync.dma_start(list2[:], offs2)
+        nc.sync.dma_start(list3[:], offs3)
+        spread_plane = keep.tile([P, S], U8, name="spread_plane")
+        nc.vector.tensor_copy(spread_plane[:], table_plane[:, 0, :].indirect(list1[:]))
+        v_plane = keep.tile([P, S], U8, name="v_plane", align_bytes=64)
+        nc.gpsimd.memset(v_plane[:].bitcast(I32), 0)
+        for quad in range(P // QUADRANT):
+            at = QUADRANT * quad
+            nc.scalar.dma_start(out=v_plane[at : at + 4].bitcast(I32), in_=spread_plane[at : at + QUADRANT : SPREAD].bitcast(I32))
+        load_w13(1, P, PLANE_AT)
         load_w13(2, 2 * P, RAW_AT + 8 * KIB)
         nc.sync.dma_start(out=factors[1][:], in_=wgs[:, HALF:S])
-        nc.sync.dma_start(list3[:], offs3)
         load_w13(PACK, PASS_ROWS, TABLE_AT)
         nc.sync.dma_start(out=w2_codes[1][:].bitcast(I32), in_=w2_words[0][:, H : 2 * H].bitcast(I32))
         dealt_factors = []
@@ -160,7 +170,7 @@ def tile_list_resumed_session_features_kernel(
         w5_raw = keep.tile([P, 2, N], U16, name="w5_raw")
         nc.sync.dma_start(out=w5_raw[:].bitcast(I32), in_=w5_words.rearrange("g p n -> p g n").bitcast(I32))
         w56_raw_plane = keep.tile([P, 2, N], U8, name="w56_raw_plane")
-        nc.gpsimd.memset(w56_raw_plane[:].bitcast(I32), 0)
+        nc.vector.memset(w56_raw_plane[:].bitcast(I32), 0)
         for t in range(1, PACK):
             load_dealt_factors()
         load_scale_rows(nc.sync, w56_raw_plane, w5_scales)
@@ -182,7 +192,9 @@ def tile_list_resumed_session_features_kernel(
 
         def round_w13(first, i, engine_copy):
             name = ("w1", "w3")[i]
-            if first < PACK:
+            if engine_copy is gpsimd_round:
+                engine_copy(group_tile(first)[:, i], raw[name, first][:].rearrange("p t c -> p c t"))
+            elif first < PACK:
                 interleave(engine_copy, group_tile(first)[:, i], raw[name, first][:])
             else:
                 t = first - PACK
@@ -191,9 +203,9 @@ def tile_list_resumed_session_features_kernel(
                     in_=raw[name, PACK][:].rearrange("p i (q t) -> p q t i", t=PACK)[:, :, t : t + 2, :],
                 )
 
-        def quantize_w13(first):
+        def quantize_w13(first, home=None):
             width = GROUPS[first][1]
-            codes, plane = quantize("w13_%d" % first, grouped13[first][:].rearrange("p w r t -> p (w r t)"), 2 * width)
+            codes, plane = quantize("w13_%d" % first, grouped13[first][:].rearrange("p w r t -> p (w r t)"), 2 * width, home)
             for i, name in enumerate(("w1", "w3")):
                 for c in range(width // P):
                     cols = slice(i * width + c * P, i * width + (c + 1) * P)
@@ -216,8 +228,6 @@ def tile_list_resumed_session_features_kernel(
             round_w13(0, i, nc.scalar.copy)
         quantize_w13(0)
         v_codes = [keep.tile([P, HALF], U32, name="v_codes%d" % h, align_bytes=64) for h in range(2)]
-        v_plane = keep.tile([P, S], U8, name="v_plane", align_bytes=64)
-        nc.vector.tensor_copy(v_plane[:], table_plane[:, 0, :].indirect(list1[:]))
         v_planes = [v_plane[:, h * HALF : (h + 1) * HALF] for h in range(2)]
         for h in range(2):
             nc.vector.tensor_copy(v_codes[h][:], table[:].bitcast(U32).indirect(entries(list1, h * HALF, HALF)))
@@ -235,7 +245,8 @@ def tile_list_resumed_session_features_kernel(
 
         def first_terms(h):
             first_banks[h] = [bank(i, "first_terms") for i in FIRST_BANKS[h]]
-            for term_bank, (codes, plane) in zip(first_banks[h], page_weights(0)):
+            w2_page, w1_page, w3_page = page_weights(0)
+            for term_bank, (codes, plane) in zip(first_banks[h], (w1_page, w2_page, w3_page)):
                 nc.tensor.matmul_mx(
                     out=term_bank[:], lhsT=codes, lhsT_scale=plane,
                     rhs=v_codes[h][:].bitcast(E4M3), rhs_scale=v_planes[h], start=True, stop=True,
@@ -381,19 +392,19 @@ def tile_list_resumed_session_features_kernel(
         first_terms(0)
         first_b(0)
         for i in range(2):
-            round_w13(1, i, nc.scalar.copy)
+            round_w13(1, i, gpsimd_round)
         first_product(0)
-        quantize_w13(1)
-        first_state(0, GROUPED_AT + GROUPS[1][0])
+        first_state(0)
         first_weigh(0)
         first_terms(1)
         first_b(1)
         first_product(1)
         first_state(1)
+        quantize_w13(1, FIRST_AT + 4 * 2 * S)
         first_scatter(0)
+        round_w13(2, 0, nc.scalar.copy)
+        round_w13(2, 1, gpsimd_round)
         make_terms(0)
-        for i in range(2):
-            round_w13(2, i, nc.scalar.copy)
         quantize_w13(2)
         first_weigh(1, RAW_AT + 12 * KIB)
         first_scatter(1)

@@ -456,21 +456,21 @@ def tile_list_resumed_session_features_kernel(
         w4_plane = keep.tile([P, 2, N], U8, name="w4_plane", align_bytes=64)
 
         def quantize_w4(g):
-            w4_codes[g] = shared.tile([P, N], U32, name="w4_codes%d" % g, align_bytes=64, offset=STATES_AT + KIB * (1 + 2 * g))
+            w4_codes[g] = shared.tile([P, N], U32, name="w4_codes%d" % g, align_bytes=64, offset=GROUPED_AT + KIB * (9 + 4 * g) // 2)
             nc.vector.quantize_mx(
                 out=w4_codes[g][:].bitcast(E4M3), scales=w4_plane[:, g, :],
                 in_=w4_grouped[g][:].rearrange("p t q i -> p (t q i)"),
             )
 
-        quantize_w4(0)
         for q in range(QUARTERS):
             pick_add(PACK - 1, q)
         for q in range(QUARTERS):
-            grouped = shared.tile([P, P, PACK], BF16, name="z_grouped1%d" % q, align_bytes=64, offset=GROUPED_AT + KIB * q)
+            grouped = shared.tile([P, P, PACK], BF16, name="z_grouped1%d" % q, align_bytes=64, offset=GROUPED_AT + KIB * (0, 6, 1, 2)[q])
             interleave(nc.scalar.copy, grouped[:], picked[:, q])
             z1[q] = quantize("z1%d" % q, grouped[:].rearrange("p m t -> p (m t)"), P)
-            if q == 0:
-                quantize_w4(1)
+            if q == 1:
+                for g in range(2):
+                    quantize_w4(g)
 
         def stationary(name, g, t):
             cols = slice(t * P, (t + 1) * P)
@@ -481,12 +481,11 @@ def tile_list_resumed_session_features_kernel(
             return w4_codes[g][:, cols].bitcast(E4M3), w4_plane[:, g, cols]
 
         names = ("gate", "more", "base")
-        slots = [(q, name) for q in range(QUARTERS) for name in names]
         sums = {}
 
         def multiply(q, name, g):
             if g == 0:
-                sums[q, name] = bank(SUM_BANKS[slots.index((q, name)) % len(SUM_BANKS)], "y_sum")
+                sums[q, name] = bank(SUM_BANKS[2 * q + (name == "more")], "y_sum")
                 z_codes, z_plane = z0_codes[:, q * P : (q + 1) * P], z0_plane[:, q * P : (q + 1) * P]
             else:
                 z_codes, z_plane = z1[q][0][:], z1[q][1][:]
@@ -506,12 +505,14 @@ def tile_list_resumed_session_features_kernel(
             cols = slice(q * P, (q + 1) * P)
             opened = shared.tile([P, BANK], F32, name="opened%d" % q, offset=FIRST_AT + 2 * KIB * (q % 2))
             nc.scalar.activation(opened[:], sums[q, "gate"][:], TANH, scale=0.5)
+            for g in range(2):
+                multiply(q, "base", g)
             gated = shared.tile([P, BANK], F32, name="gated%d" % q, offset=FIRST_AT + 2 * KIB * (2 + q % 2))
             nc.vector.scalar_tensor_tensor(gated[:], opened[:], 1.0, sums[q, "more"][:], ADD, MULT)
             y_vals = shared.tile([P, PACK, P], F32, name="y_vals%d" % q, offset=FIRST_AT + 2 * KIB * (4 + q))
             nc.vector.scalar_tensor_tensor(y_vals[:].rearrange("p t m -> p (t m)"), gated[:], 0.5, sums[q, "base"][:], MULT, ADD)
             nc.sync.dma_start(out=out_rows[:, :, cols], in_=y_vals[:])
-            y_grouped = shared.tile([P, P, PACK], BF16, name="y_grouped%d" % q, align_bytes=64, offset=GROUPED_AT + KIB * (8 + q))
+            y_grouped = shared.tile([P, P, PACK], BF16, name="y_grouped%d" % q, align_bytes=64, offset=GROUPED_AT + KIB * (10 + q))
             interleave(nc.scalar.copy if q < QUARTERS - 1 else nc.vector.tensor_copy, y_grouped[:], y_vals[:])
             nc.vector.quantize_mx(
                 out=y_codes[:, cols].bitcast(E4M3), scales=y_plane[:, cols],
@@ -519,13 +520,11 @@ def tile_list_resumed_session_features_kernel(
             )
             nc.sync.dma_start(out=out_words[:, cols], in_=y_codes[:, cols].bitcast(I32))
 
-        early_slots = slots[: len(SUM_BANKS)]
-        for q, name in early_slots:
-            multiply(q, name, 0)
         for q in range(QUARTERS):
-            for name in names:
-                if (q, name) not in early_slots:
-                    multiply(q, name, 0)
+            for name in names[:2]:
+                multiply(q, name, 0)
+        for q in range(QUARTERS):
+            for name in names[:2]:
                 multiply(q, name, 1)
             finish(q)
         for quad in range(P // QUADRANT):

@@ -50,7 +50,7 @@ LAST_PICK_AT = 110 * KIB
 Z_ROWS_AT = 112 * KIB
 W4_RAW_AT = 116 * KIB
 STATE_SLOTS = 4
-GROUPS = {0: (0, P), 1: (2 * KIB, P), 2: (4 * KIB, 2 * P), 4: (8 * KIB, 2 * P), 6: (12 * KIB, 2 * P)}
+GROUPS = {0: (0, 2 * P), 2: (4 * KIB, 2 * P), 4: (8 * KIB, 2 * P), 6: (12 * KIB, 2 * P)}
 
 
 def tile_list_resumed_session_features_kernel(
@@ -129,7 +129,7 @@ def tile_list_resumed_session_features_kernel(
         list2 = lists.tile([P, S // STRIPE], U16, name="list2")
         list3 = lists.tile([P, M // STRIPE], U16, name="list3")
         nc.sync.dma_start(list1[:], offs)
-        load_w13(0, P, RAW_AT + 4 * KIB)
+        load_w13(0, 2 * P, W4_RAW_AT)
         w2_codes = [keep.tile([P, H], U8, name="w2_codes%d" % g, align_bytes=64) for g in range(2)]
         nc.sync.dma_start(out=w2_codes[0][:].bitcast(I32), in_=w2_words[0][:, 0:H].bitcast(I32))
         nc.sync.dma_start(out=table_plane[0:P:SPREAD, 0, :].bitcast(I32), in_=tab_scales[0].bitcast(I32))
@@ -146,7 +146,6 @@ def tile_list_resumed_session_features_kernel(
         for quad in range(P // QUADRANT):
             at = QUADRANT * quad
             nc.scalar.dma_start(out=v_plane[at : at + 4].bitcast(I32), in_=spread_plane[at : at + QUADRANT : SPREAD].bitcast(I32))
-        load_w13(1, P, PLANE_AT)
         load_w13(2, 2 * P, RAW_AT + 8 * KIB)
         nc.sync.dma_start(out=factors[1][:], in_=wgs[:, HALF:S])
         load_w13(PACK, PASS_ROWS, TABLE_AT)
@@ -391,8 +390,6 @@ def tile_list_resumed_session_features_kernel(
 
         first_terms(0)
         first_b(0)
-        for i in range(2):
-            round_w13(1, i, gpsimd_round)
         first_product(0)
         first_state(0)
         first_weigh(0)
@@ -400,9 +397,8 @@ def tile_list_resumed_session_features_kernel(
         first_b(1)
         first_product(1)
         first_state(1)
-        quantize_w13(1, FIRST_AT + 4 * 2 * S)
         first_scatter(0)
-        round_w13(2, 0, nc.scalar.copy)
+        round_w13(2, 0, gpsimd_round)
         round_w13(2, 1, gpsimd_round)
         make_terms(0)
         quantize_w13(2)

@@ -49,7 +49,8 @@ DEALT_AT = 98 * KIB
 LAST_PICK_AT = 110 * KIB
 Z_ROWS_AT = 112 * KIB
 W4_RAW_AT = 116 * KIB
-STATE_SLOTS = 4
+CONTEXTS_AT = 132 * KIB
+STATE_SLOTS = 2
 GROUPS = {0: (0, 2 * P), 2: (4 * KIB, 2 * P), 4: (8 * KIB, 2 * P), 6: (12 * KIB, 2 * P)}
 
 
@@ -70,6 +71,10 @@ def tile_list_resumed_session_features_kernel(
 
         def blocks(ap):
             return [ap[:, i * P : (i + 1) * P] for i in range(ap.shape[1] // P)]
+
+        def halves(ap):
+            middle_column = ap.shape[1] // 2
+            return [ap[:, 0:middle_column], ap[:, middle_column : 2 * middle_column]]
 
         def entries(list_tile, start, count):
             return list_tile[:, start // STRIPE : (start + count) // STRIPE]
@@ -257,13 +262,16 @@ def tile_list_resumed_session_features_kernel(
             return first[kind, h][:]
 
         def first_b(h):
-            nc.scalar.copy(out=first_tile("b", h), in_=first_banks[h][0][:])
+            for vals, terms in zip(halves(first_tile("b", h)), halves(first_banks[h][0])):
+                nc.scalar.copy(out=vals, in_=terms)
 
         def first_product(h):
-            nc.vector.tensor_tensor(first_tile("ab", h), first_banks[h][1][:], first["b", h][:], MULT)
+            for vals, terms, other in zip(halves(first_tile("ab", h)), halves(first_banks[h][1]), halves(first["b", h])):
+                nc.vector.tensor_tensor(vals, terms, other, MULT)
 
         def first_state(h, home=None):
-            nc.vector.tensor_tensor(first_tile("h", h, home), first_banks[h][2][:], first["ab", h][:], ADD)
+            for vals, terms, other in zip(halves(first_tile("h", h, home)), halves(first_banks[h][2]), halves(first["ab", h])):
+                nc.vector.tensor_tensor(vals, terms, other, ADD)
 
         def first_weigh(h, home=None):
             nc.gpsimd.tensor_tensor(first_tile("weighted", h, home), first["h", h][:], factors[h][:], MULT)
@@ -398,13 +406,20 @@ def tile_list_resumed_session_features_kernel(
         first_product(1)
         first_state(1)
         first_scatter(0)
-        round_w13(2, 0, gpsimd_round)
-        round_w13(2, 1, gpsimd_round)
+        middle = {}
+        for i, at in ((1, GROUPED_AT + GROUPS[2][0]), (0, FIRST_AT + 4 * HALF)):
+            middle[i] = shared.tile([P, 2 * P, PACK], BF16, name="middle%d" % i, align_bytes=64, offset=at)
+        gpsimd_round(middle[1][:], raw["w3", 2][:].rearrange("p t c -> p c t"))
         make_terms(0)
-        quantize_w13(2)
-        first_weigh(1, RAW_AT + 12 * KIB)
+        interleave(nc.scalar.copy, middle[0][:], raw["w1", 2][:])
+        for i, name in enumerate(("w1", "w3")):
+            home = RAW_AT + 10 * KIB + KIB * i
+            codes, plane = quantize(name + "_2", middle[i][:].rearrange("p r t -> p (r t)"), 2 * P, home)
+            for c in range(2):
+                w13[name, 2 + c] = (codes[:, c * P : (c + 1) * P].bitcast(E4M3), plane[:, c * P : (c + 1) * P])
+        first_weigh(1, RAW_AT + 8 * KIB)
         first_scatter(1)
-        dealt_contexts = shared.tile([P, PACK, M], F32, name="dealt_contexts", offset=RAW_AT + 8 * KIB)
+        dealt_contexts = shared.tile([P, PACK, M], F32, name="dealt_contexts", offset=CONTEXTS_AT)
         nc.sync.dma_start(out=dealt_contexts[:], in_=ctx[PASS_ROWS:H].rearrange("(p t) m -> p t m", t=PACK))
         make_terms(1)
         make_states(0)

@@ -120,8 +120,9 @@ def tile_list_resumed_session_features_kernel(
             nc.sync.dma_start(out=tile[:], in_=rows[:, :, start : start + width])
             return tile
 
-        def load_w13(first, width, offset):
-            for i, name in enumerate(("w1", "w3")):
+        def load_w13(first, width, offset, which=(0, 1)):
+            for i in which:
+                name = ("w1", "w3")[i]
                 raw[name, first] = load_columns("%s_raw%d" % (name, first), rows13[name], first * P, width, offset + 16 * width * i)
 
         table_plane = shared.tile([P, 1, T], U8, name="table_plane", offset=PLANE_AT - KIB)
@@ -134,10 +135,11 @@ def tile_list_resumed_session_features_kernel(
         list2 = lists.tile([P, S // STRIPE], U16, name="list2")
         list3 = lists.tile([P, M // STRIPE], U16, name="list3")
         nc.sync.dma_start(list1[:], offs)
-        load_w13(0, 2 * P, W4_RAW_AT)
+        load_w13(0, 2 * P, W4_RAW_AT, (0,))
         w2_codes = [keep.tile([P, H], U8, name="w2_codes%d" % g, align_bytes=64) for g in range(2)]
         nc.sync.dma_start(out=w2_codes[0][:].bitcast(I32), in_=w2_words[0][:, 0:H].bitcast(I32))
         nc.sync.dma_start(out=table_plane[0:P:SPREAD, 0, :].bitcast(I32), in_=tab_scales[0].bitcast(I32))
+        load_w13(0, 2 * P, W4_RAW_AT, (1,))
         table = shared.tile([P, T], I32, name="table", offset=TABLE_AT)
         nc.sync.dma_start(out=table[:], in_=tab_words[0].rearrange("p t i -> p (t i)").bitcast(I32))
         factors = [keep.tile([P, HALF], F32, name="factors%d" % h) for h in range(2)]
@@ -236,8 +238,7 @@ def tile_list_resumed_session_features_kernel(
         for h in range(2):
             nc.vector.tensor_copy(v_codes[h][:], table[:].bitcast(U32).indirect(entries(list1, h * HALF, HALF)))
         pages.append(shared.tile([P, T2], F32, name="page1", offset=PAGE1_AT))
-        for at in range(0, T2, S):
-            nc.gpsimd.memset(pages[1][:, at : at + S].bitcast(I32), 0)
+        nc.gpsimd.memset(pages[1][:].bitcast(I32), 0)
 
         nc.gpsimd.tensor_copy(
             out=w2_dealt_plane[:].rearrange("p (t q) -> p t q", t=PACK),

@@ -377,19 +377,20 @@ def tile_list_resumed_session_features_kernel(
             dealt[key] = shared.tile(shape, dtype, name="dealt%d" % u, align_bytes=64, offset=deal_home(u))
             return dealt[key]
 
+        def deal_words(dealt, plain):
+            nc.scalar.copy(out=dealt.rearrange("p (t q) -> p t q", t=PACK), in_=plain.rearrange("p (q t) -> p t q", t=PACK))
+
         def deal_after(u):
             if u == 1:
-                deal_pairs(dealt_tile("w2", [P, H], U8, u)[:], w2_codes[1][:])
+                deal_words(dealt_tile("w2", [P, H], U8, u)[:].bitcast(U16), w2_codes[1][:].bitcast(U16))
             elif u < 7:
                 g = (u - 3) // 2
-                deal(dealt_tile(("w6", g), [P, N], I32, u)[:], w6_raw[:, g, :])
+                deal_words(dealt_tile(("w6", g), [P, N], U32, u)[:], w6_raw[:, g, :].bitcast(U32))
             elif u < 11:
                 g = (u - 7) // 2
-                deal_pairs(dealt_tile(("w5", g), [P, 2 * N], U8, u)[:], w5_raw[:, g, :].bitcast(U8))
-            else:
-                plane = dealt_tile("plane", [P, 2, N], U8, u)
-                for g in range(2):
-                    deal(plane[:, g, :], w56_raw_plane[:, g, :])
+                deal_words(dealt_tile(("w5", g), [P, 2 * N], U8, u)[:].bitcast(U16), w5_raw[:, g, :])
+                dealt["plane", g] = shared.tile([P, N], U8, name="dealt_plane%d" % g, align_bytes=64, offset=deal_home(u) + KIB)
+                deal(dealt["plane", g][:], w56_raw_plane[:, g, :])
 
         def add_context(t):
             nc.gpsimd.tensor_tensor(
@@ -487,9 +488,9 @@ def tile_list_resumed_session_features_kernel(
         def stationary(name, g, t):
             cols = slice(t * P, (t + 1) * P)
             if name == "gate":
-                return dealt["w5", g][:, 2 * t * P : 2 * (t + 1) * P].bitcast(E2M1), dealt["plane"][:, g, cols]
+                return dealt["w5", g][:, 2 * t * P : 2 * (t + 1) * P].bitcast(E2M1), dealt["plane", g][:, cols]
             if name == "more":
-                return dealt["w6", g][:, cols].bitcast(E4M3), dealt["plane"][4:P, g, cols]
+                return dealt["w6", g][:, cols].bitcast(E4M3), dealt["plane", g][4:P, cols]
             return w4_codes[g][:, cols].bitcast(E4M3), w4_plane[:, g, cols]
 
         names = ("gate", "more", "base")

@@ -31,7 +31,8 @@ PAGES = H // P
 STEPS = 2 * (PAGES - 1)
 SPREAD = 8
 
-FIRST_BANKS = ((4, 5, 1), (4, 2, 5))
+FIRST_BANKS = ((4, 5, 1), (0, 2, 3))
+EARLY_BANK = 6
 B_BANKS, A_BANK, D_BANK, H_BANKS = (1, 2), 6, 7, (0, 3)
 SUM_BANKS = (1, 2, 6, 7, 4, 5, 0, 3)
 KIB = 1024
@@ -235,8 +236,9 @@ def tile_list_resumed_session_features_kernel(
         quantize_w13(0)
         v_codes = [keep.tile([P, HALF], U32, name="v_codes%d" % h, align_bytes=64) for h in range(2)]
         v_planes = [v_plane[:, h * HALF : (h + 1) * HALF] for h in range(2)]
-        for h in range(2):
-            nc.vector.tensor_copy(v_codes[h][:], table[:].bitcast(U32).indirect(entries(list1, h * HALF, HALF)))
+        for start, count in ((0, CHUNK), (CHUNK, CHUNK), (HALF, HALF)):
+            gathered = v_codes[start // HALF][:, start % HALF : start % HALF + count]
+            nc.vector.tensor_copy(gathered, table[:].bitcast(U32).indirect(entries(list1, start, count)))
         pages.append(shared.tile([P, T2], F32, name="page1", offset=PAGE1_AT))
         nc.gpsimd.memset(pages[1][:].bitcast(I32), 0)
 
@@ -249,13 +251,15 @@ def tile_list_resumed_session_features_kernel(
         first = {}
 
         def first_terms(h):
-            first_banks[h] = [bank(i, "first_terms") for i in FIRST_BANKS[h]]
+            first_banks[h] = [halves(bank(i, "first_terms")) for i in FIRST_BANKS[h]]
+            if h == 0:
+                first_banks[h][0][0] = halves(bank(EARLY_BANK, "first_terms"))[0]
             w2_page, w1_page, w3_page = page_weights(0)
-            for term_bank, (codes, plane) in zip(first_banks[h], (w1_page, w2_page, w3_page)):
-                nc.tensor.matmul_mx(
-                    out=term_bank[:], lhsT=codes, lhsT_scale=plane,
-                    rhs=v_codes[h][:].bitcast(E4M3), rhs_scale=v_planes[h], start=True, stop=True,
-                )
+            for term_halves, (codes, plane) in zip(first_banks[h], (w1_page, w2_page, w3_page)):
+                for term, v_half, v_scale in zip(term_halves, halves(v_codes[h]), halves(v_planes[h])):
+                    nc.tensor.matmul_mx(
+                        out=term, lhsT=codes, lhsT_scale=plane, rhs=v_half.bitcast(E4M3), rhs_scale=v_scale, start=True, stop=True,
+                    )
 
         def first_tile(kind, h, home=None):
             at = FIRST_AT + 4 * (S * ("b", "ab", "h", "weighted").index(kind) + HALF * h)
@@ -263,15 +267,15 @@ def tile_list_resumed_session_features_kernel(
             return first[kind, h][:]
 
         def first_b(h):
-            for vals, terms in zip(halves(first_tile("b", h)), halves(first_banks[h][0])):
+            for vals, terms in zip(halves(first_tile("b", h)), first_banks[h][0]):
                 nc.scalar.copy(out=vals, in_=terms)
 
         def first_product(h):
-            for vals, terms, other in zip(halves(first_tile("ab", h)), halves(first_banks[h][1]), halves(first["b", h])):
+            for vals, terms, other in zip(halves(first_tile("ab", h)), first_banks[h][1], halves(first["b", h])):
                 nc.vector.tensor_tensor(vals, terms, other, MULT)
 
         def first_state(h, home=None):
-            for vals, terms, other in zip(halves(first_tile("h", h, home)), halves(first_banks[h][2]), halves(first["ab", h])):
+            for vals, terms, other in zip(halves(first_tile("h", h, home)), first_banks[h][2], halves(first["ab", h])):
                 nc.vector.tensor_tensor(vals, terms, other, ADD)
 
         def first_weigh(h, home=None):
@@ -292,7 +296,7 @@ def tile_list_resumed_session_features_kernel(
 
         def make_terms(u):
             c, h = 1 + u // 2, u % 2
-            banks = [bank(i, "terms") for i in (B_BANKS[u % 2], A_BANK, D_BANK)]
+            banks = [bank(i, "terms") for i in (FIRST_BANKS[0][0] if u == 0 else B_BANKS[u % 2], A_BANK, D_BANK)]
             for term_bank, (codes, plane) in zip(banks, page_weights(c)):
                 for block, v_block, v_scale in zip(blocks(term_bank), blocks(v_codes[h]), blocks(v_planes[h])):
                     nc.tensor.matmul_mx(
@@ -377,18 +381,20 @@ def tile_list_resumed_session_features_kernel(
             dealt[key] = shared.tile(shape, dtype, name="dealt%d" % u, align_bytes=64, offset=deal_home(u))
             return dealt[key]
 
-        def deal_words(dealt, plain):
-            nc.scalar.copy(out=dealt.rearrange("p (t q) -> p t q", t=PACK), in_=plain.rearrange("p (q t) -> p t q", t=PACK))
+        def deal_words(dealt, plain, run):
+            nc.scalar.copy(
+                out=dealt.rearrange("p (t b i) -> p b t i", t=PACK, i=run), in_=plain.rearrange("p (b i t) -> p b t i", t=PACK, i=run),
+            )
 
         def deal_after(u):
             if u == 1:
-                deal_words(dealt_tile("w2", [P, H], U8, u)[:].bitcast(U16), w2_codes[1][:].bitcast(U16))
+                deal_words(dealt_tile("w2", [P, H], U8, u)[:].bitcast(U16), w2_codes[1][:].bitcast(U16), 8)
             elif u < 7:
                 g = (u - 3) // 2
-                deal_words(dealt_tile(("w6", g), [P, N], U32, u)[:], w6_raw[:, g, :].bitcast(U32))
+                deal_words(dealt_tile(("w6", g), [P, N], U32, u)[:], w6_raw[:, g, :].bitcast(U32), 4)
             elif u < 11:
                 g = (u - 7) // 2
-                deal_words(dealt_tile(("w5", g), [P, 2 * N], U8, u)[:].bitcast(U16), w5_raw[:, g, :])
+                deal_words(dealt_tile(("w5", g), [P, 2 * N], U8, u)[:].bitcast(U16), w5_raw[:, g, :], 8)
                 dealt["plane", g] = shared.tile([P, N], U8, name="dealt_plane%d" % g, align_bytes=64, offset=deal_home(u) + KIB)
                 deal(dealt["plane", g][:], w56_raw_plane[:, g, :])
 
@@ -409,7 +415,7 @@ def tile_list_resumed_session_features_kernel(
         first_state(1)
         first_scatter(0)
         middle = {}
-        for i, at in ((1, GROUPED_AT + GROUPS[2][0]), (0, FIRST_AT + 4 * HALF)):
+        for i, at in ((1, FIRST_AT + 8 * S), (0, FIRST_AT + 4 * HALF)):
             middle[i] = shared.tile([P, 2 * P, PACK], BF16, name="middle%d" % i, align_bytes=64, offset=at)
         gpsimd_round(middle[1][:], raw["w3", 2][:].rearrange("p t c -> p c t"))
         make_terms(0)

@@ -389,10 +389,10 @@ def tile_list_resumed_session_features_kernel(
         def deal_after(u):
             if u == 1:
                 deal_words(dealt_tile("w2", [P, H], U8, u)[:].bitcast(U16), w2_codes[1][:].bitcast(U16), 8)
-            elif u < 7:
-                g = (u - 3) // 2
+            elif u in (5, 11):
+                g = u // 11
                 deal_words(dealt_tile(("w6", g), [P, N], U32, u)[:], w6_raw[:, g, :].bitcast(U32), 4)
-            elif u < 11:
+            elif u > 5:
                 g = (u - 7) // 2
                 deal_words(dealt_tile(("w5", g), [P, 2 * N], U8, u)[:].bitcast(U16), w5_raw[:, g, :], 8)
                 dealt["plane", g] = shared.tile([P, N], U8, name="dealt_plane%d" % g, align_bytes=64, offset=deal_home(u) + KIB)
@@ -436,10 +436,10 @@ def tile_list_resumed_session_features_kernel(
                 make_terms(u + 2)
             if u + 1 < STEPS:
                 make_states(u + 1)
-            if u in (0, 1, 3, 4):
-                round_w13(PACK + 2 * (u // 3), u % 3, nc.scalar.copy)
-                if u % 3 == 1:
-                    quantize_w13(PACK + 2 * (u // 3))
+            if u < 4:
+                round_w13(PACK + 2 * (u // 2), u % 2, nc.scalar.copy)
+                if u % 2 == 1:
+                    quantize_w13(PACK + 2 * (u // 2))
             if u % 2 == 0 and u + 2 < STEPS:
                 deal_after(u + 1)
             if u % 2 == 0 and 2 <= u < 10:

from contextlib import ExitStack

import concourse.mybir as mybir
from concourse.masks import make_identity

K, H, N, T, S, T2, M = 512, 1024, 512, 4096, 1024, 2048, 512
FLOPS = 2 * (3 * K * H * S + 3 * H * N * M)

F32 = mybir.dt.float32
BF16 = mybir.dt.bfloat16
I32 = mybir.dt.int32
U32 = mybir.dt.uint32
U16 = mybir.dt.uint16
U8 = mybir.dt.uint8
E4M3 = mybir.dt.float8_e4m3fn_x4
E2M1 = mybir.dt.float4_e2m1fn_x4
MULT = mybir.AluOpType.mult
ADD = mybir.AluOpType.add
TANH = mybir.ActivationFunctionType.Tanh

P = 128
PACK = 4
QUADRANT = 32
STRIPE = 16
BANK = 512
PASS_ROWS = P * PACK
HALF = S // 2
CHUNK = 256
QUARTERS = M // P
PAGES = H // P
STEPS = 2 * (PAGES - 1)
SPREAD = 8

FIRST_BANKS = ((4, 5, 1), (0, 2, 3))
EARLY_BANK = 6
B_BANKS, A_BANK, D_BANK, H_BANKS = (1, 2), 6, 7, (0, 3)
SUM_BANKS = (1, 2, 6, 7, 4, 5, 0, 3)
KIB = 1024
TABLE_AT = 0
PAGE1_AT = 16 * KIB
PLANE_AT = 24 * KIB
RAW_AT = 24 * KIB
GROUPED_AT = 40 * KIB
FIRST_AT = 56 * KIB
STATES_AT = 72 * KIB
PICKS_AT = 80 * KIB
PICKED_AT = 90 * KIB
Z0_AT = 88 * KIB
DEALT_AT = 98 * KIB
LAST_PICK_AT = 110 * KIB
Z_ROWS_AT = 112 * KIB
W4_RAW_AT = 116 * KIB
CONTEXTS_AT = 132 * KIB
STATE_SLOTS = 2
GROUPS = {0: (0, 2 * P), 2: (4 * KIB, 2 * P), 4: (8 * KIB, 2 * P), 6: (12 * KIB, 2 * P)}


def tile_list_resumed_session_features_kernel(
    tc, tab_words, tab_scales, offs, offs2, offs3, w1, w2_words, w2_scales, w3, wgs, ctx, w4,
    w5_words, w5_scales, w6_words, w6_scales, out_0, out_1, out_2,
):
    nc = tc.nc
    with ExitStack() as stack:
        lists = stack.enter_context(tc.tile_pool(name="lists", bufs=1))
        keep = stack.enter_context(tc.tile_pool(name="keep", bufs=1))
        shared = stack.enter_context(tc.tile_pool(name="shared", bufs=1))
        ring = stack.enter_context(tc.tile_pool(name="ring", bufs=2))
        psum = stack.enter_context(tc.psum_pool(name="psum", bufs=1))

        def bank(index, name):
            return psum.tile([P, BANK], F32, name=name, tag="bank%d" % index)

        def blocks(ap):
            return [ap[:, i * P : (i + 1) * P] for i in range(ap.shape[1] // P)]

        def halves(ap):
            middle_column = ap.shape[1] // 2
            return [ap[:, 0:middle_column], ap[:, middle_column : 2 * middle_column]]

        def entries(list_tile, start, count):
            return list_tile[:, start // STRIPE : (start + count) // STRIPE]

        def load_scale_rows(queue, plane, rows, shift=0):
            for quad in range(P // QUADRANT):
                at = QUADRANT * quad + shift
                queue.dma_start(
                    out=plane[at : at + 4].bitcast(I32),
                    in_=rows[:, 4 * quad : 4 * quad + 4, :].rearrange("a q n -> q a n").bitcast(I32),
                )

        def interleave(engine_copy, grouped, planar):
            engine_copy(
                out=grouped.rearrange("p (c i) t -> p c t i", i=4),
                in_=planar.rearrange("p t (c i) -> p c t i", i=4),
            )

        def gpsimd_round(out, in_):
            nc.gpsimd.tensor_scalar(out, in_, 1.0, 0.0, MULT, ADD)

        def add_transposed(sum_blocks, early, late):
            n = len(sum_blocks)
            for i in range(n):
                nc.tensor.matmul(sum_blocks[i], lhsT=early[i], rhs=identity[:], is_transpose=True, start=(i == 0), stop=False)
            for i in range(n):
                nc.tensor.matmul(sum_blocks[i], lhsT=late[i], rhs=identity[:], is_transpose=True, start=False, stop=(i == n - 1))

        def quantize(name, grouped, width, home=None):
            if home is None:
                codes = keep.tile([P, width], U32, name=name + "_codes", align_bytes=64)
            else:
                codes = shared.tile([P, width], U32, name=name + "_codes", align_bytes=64, offset=home)
            plane = keep.tile([P, width], U8, name=name + "_plane", align_bytes=64)
            nc.vector.quantize_mx(out=codes[:].bitcast(E4M3), scales=plane[:], in_=grouped)
            return codes, plane

        rows13 = {"w1": w1.rearrange("(p t) r -> p t r", t=PACK), "w3": w3.rearrange("(p t) r -> p t r", t=PACK)}
        raw = {}

        def load_columns(name, rows, start, width, offset):
            tile = shared.tile([P, PACK, width], F32, name=name, offset=offset)
            nc.sync.dma_start(out=tile[:], in_=rows[:, :, start : start + width])
            return tile

        def load_w13(first, width, offset, which=(0, 1)):
            for i in which:
                name = ("w1", "w3")[i]
                raw[name, first] = load_columns("%s_raw%d" % (name, first), rows13[name], first * P, width, offset + 16 * width * i)

        table_plane = shared.tile([P, 1, T], U8, name="table_plane", offset=PLANE_AT - KIB)
        nc.vector.memset(table_plane[:].bitcast(I32), 0)
        w2_plane = keep.tile([P, 1, H], U8, name="w2_plane", align_bytes=64)
        nc.gpsimd.memset(w2_plane[:].bitcast(I32), 0)
        load_scale_rows(nc.gpsimd, w2_plane, w2_scales)

        list1 = lists.tile([P, S // STRIPE], U16, name="list1")
        list2 = lists.tile([P, S // STRIPE], U16, name="list2")
        list3 = lists.tile([P, M // STRIPE], U16, name="list3")
        nc.sync.dma_start(list1[:], offs)
        load_w13(0, 2 * P, W4_RAW_AT, (0,))
        w2_codes = [keep.tile([P, H], U8, name="w2_codes%d" % g, align_bytes=64) for g in range(2)]
        nc.sync.dma_start(out=w2_codes[0][:].bitcast(I32), in_=w2_words[0][:, 0:H].bitcast(I32))
        nc.sync.dma_start(out=table_plane[0:P:SPREAD, 0, :].bitcast(I32), in_=tab_scales[0].bitcast(I32))
        load_w13(0, 2 * P, W4_RAW_AT, (1,))
        table = shared.tile([P, T], I32, name="table", offset=TABLE_AT)
        nc.sync.dma_start(out=table[:], in_=tab_words[0].rearrange("p t i -> p (t i)").bitcast(I32))
        factors = [keep.tile([P, HALF], F32, name="factors%d" % h) for h in range(2)]
        nc.sync.dma_start(out=factors[0][:], in_=wgs[:, 0:HALF])
        nc.sync.dma_start(list2[:], offs2)
        nc.sync.dma_start(list3[:], offs3)
        spread_plane = keep.tile([P, S], U8, name="spread_plane")
        nc.vector.tensor_copy(spread_plane[:], table_plane[:, 0, :].indirect(list1[:]))
        v_plane = keep.tile([P, S], U8, name="v_plane", align_bytes=64)
        nc.gpsimd.memset(v_plane[:].bitcast(I32), 0)
        for quad in range(P // QUADRANT):
            at = QUADRANT * quad
            nc.scalar.dma_start(out=v_plane[at : at + 4].bitcast(I32), in_=spread_plane[at : at + QUADRANT : SPREAD].bitcast(I32))
        load_w13(2, 2 * P, RAW_AT + 8 * KIB)
        nc.sync.dma_start(out=factors[1][:], in_=wgs[:, HALF:S])
        load_w13(PACK, PASS_ROWS, TABLE_AT)
        nc.sync.dma_start(out=w2_codes[1][:].bitcast(I32), in_=w2_words[0][:, H : 2 * H].bitcast(I32))
        dealt_factors = []

        def load_dealt_factors():
            t = len(dealt_factors)
            dealt_factors.append(keep.tile([P, S], F32, name="dealt_factors%d" % t))
            for quad in (0, 2, 1, 3):
                nc.sync.dma_start(
                    out=dealt_factors[t][QUADRANT * quad : QUADRANT * (quad + 1)],
                    in_=wgs.rearrange("(q t) j -> t q j", t=PACK)[t],
                )

        plain_contexts = shared.tile([P, PACK, M], F32, name="plain_contexts", offset=RAW_AT)
        nc.sync.dma_start(out=plain_contexts[:], in_=ctx[0:PASS_ROWS].rearrange("(c p) m -> p c m", p=P))
        w6_raw = keep.tile([P, 2, N], I32, name="w6_raw")
        nc.sync.dma_start(out=w6_raw[:], in_=w6_words.rearrange("g p n t -> p g (n t)").bitcast(I32))
        load_dealt_factors()
        w5_raw = keep.tile([P, 2, N], U16, name="w5_raw")
        nc.sync.dma_start(out=w5_raw[:].bitcast(I32), in_=w5_words.rearrange("g p n -> p g n").bitcast(I32))
        w56_raw_plane = keep.tile([P, 2, N], U8, name="w56_raw_plane")
        nc.vector.memset(w56_raw_plane[:].bitcast(I32), 0)
        for t in range(1, PACK):
            load_dealt_factors()
        load_scale_rows(nc.sync, w56_raw_plane, w5_scales)
        load_scale_rows(nc.sync, w56_raw_plane, w6_scales, shift=4)
        w4_rows = w4.rearrange("(g p t) n -> g p t n", p=P, t=PACK)
        w4_raw = [load_columns("w4_raw%d" % g, w4_rows[g], 0, N, W4_RAW_AT + 8 * KIB * g) for g in range(2)]

        identity = keep.tile([P, P], F32, name="identity")
        make_identity(nc, identity[:])

        grouped13 = {}
        w13 = {}

        def group_tile(first):
            if first not in grouped13:
                at, width = GROUPS[first]
                grouped13[first] = shared.tile([P, 2, width, PACK], BF16, name="grouped%d" % first, align_bytes=64, offset=GROUPED_AT + at)
            return grouped13[first]

        def round_w13(first, i, engine_copy):
            name = ("w1", "w3")[i]
            if engine_copy is gpsimd_round:
                engine_copy(group_tile(first)[:, i], raw[name, first][:].rearrange("p t c -> p c t"))
            elif first < PACK:
                interleave(engine_copy, group_tile(first)[:, i], raw[name, first][:])
            else:
                t = first - PACK
                engine_copy(
                    out=group_tile(first)[:, i].rearrange("p (t q) i -> p q t i", t=2),
                    in_=raw[name, PACK][:].rearrange("p i (q t) -> p q t i", t=PACK)[:, :, t : t + 2, :],
                )

        def quantize_w13(first, home=None):
            width = GROUPS[first][1]
            codes, plane = quantize("w13_%d" % first, grouped13[first][:].rearrange("p w r t -> p (w r t)"), 2 * width, home)
            for i, name in enumerate(("w1", "w3")):
                for c in range(width // P):
                    cols = slice(i * width + c * P, i * width + (c + 1) * P)
                    w13[name, first + c] = (codes[:, cols].bitcast(E4M3), plane[:, cols])

        dealt = {}
        w2_dealt_plane = keep.tile([P, PASS_ROWS], U8, name="w2_dealt_plane", align_bytes=64)

        def page_weights(c):
            t = c % PACK
            if c < PACK:
                w2_page = (w2_codes[0][:, 2 * P * t : 2 * P * (t + 1)].bitcast(E2M1), w2_plane[:, 0, P * t : P * (t + 1)])
            else:
                w2_page = (dealt["w2"][:, 2 * P * t : 2 * P * (t + 1)].bitcast(E2M1), w2_dealt_plane[:, P * t : P * (t + 1)])
            return w2_page, w13["w1", c], w13["w3", c]

        pages = [keep.tile([P, T2], F32, name="page0")]
        nc.vector.memset(pages[0][:].bitcast(I32), 0)
        for i in range(2):
            round_w13(0, i, nc.scalar.copy)
        quantize_w13(0)
        v_codes = [keep.tile([P, HALF], U32, name="v_codes%d" % h, align_bytes=64) for h in range(2)]
        v_planes = [v_plane[:, h * HALF : (h + 1) * HALF] for h in range(2)]
        for start, count in ((0, CHUNK), (CHUNK, CHUNK), (HALF, HALF)):
            gathered = v_codes[start // HALF][:, start % HALF : start % HALF + count]
            nc.vector.tensor_copy(gathered, table[:].bitcast(U32).indirect(entries(list1, start, count)))
        pages.append(shared.tile([P, T2], F32, name="page1", offset=PAGE1_AT))
        nc.gpsimd.memset(pages[1][:].bitcast(I32), 0)

        nc.gpsimd.tensor_copy(
            out=w2_dealt_plane[:].rearrange("p (t q) -> p t q", t=PACK),
            in_=w2_plane[:, 0, PASS_ROWS:H].rearrange("p (q t) -> p t q", t=PACK),
        )

        first_banks = {}
        first = {}

        def first_terms(h):
            first_banks[h] = [halves(bank(i, "first_terms")) for i in FIRST_BANKS[h]]
            if h == 0:
                first_banks[h][0][0] = halves(bank(EARLY_BANK, "first_terms"))[0]
            w2_page, w1_page, w3_page = page_weights(0)
            for term_halves, (codes, plane) in zip(first_banks[h], (w1_page, w2_page, w3_page)):
                for term, v_half, v_scale in zip(term_halves, halves(v_codes[h]), halves(v_planes[h])):
                    nc.tensor.matmul_mx(
                        out=term, lhsT=codes, lhsT_scale=plane, rhs=v_half.bitcast(E4M3), rhs_scale=v_scale, start=True, stop=True,
                    )

        def first_tile(kind, h, home=None):
            at = FIRST_AT + 4 * (S * ("b", "ab", "h", "weighted").index(kind) + HALF * h)
            first[kind, h] = shared.tile([P, HALF], F32, name="first_%s%d" % (kind, h), offset=at if home is None else home)
            return first[kind, h][:]

        def first_b(h):
            for vals, terms in zip(halves(first_tile("b", h)), first_banks[h][0]):
                nc.scalar.copy(out=vals, in_=terms)

        def first_product(h):
            for vals, terms, other in zip(halves(first_tile("ab", h)), first_banks[h][1], halves(first["b", h])):
                nc.vector.tensor_tensor(vals, terms, other, MULT)

        def first_state(h, home=None):
            for vals, terms, other in zip(halves(first_tile("h", h, home)), first_banks[h][2], halves(first["ab", h])):
                nc.vector.tensor_tensor(vals, terms, other, ADD)

        def first_weigh(h, home=None):
            nc.gpsimd.tensor_tensor(first_tile("weighted", h, home), first["h", h][:], factors[h][:], MULT)

        def first_scatter(h):
            nc.vector.tensor_copy(pages[0][:].indirect(entries(list2, h * HALF, HALF)), first["weighted", h][:])

        products = {}
        addends = {}
        states = {}

        def pick_home(c):
            return LAST_PICK_AT if c == PAGES - 2 else PICKS_AT + 2 * KIB * (c % 4)

        def deal_home(u):
            return DEALT_AT + 2 * KIB * (u // 2)

        def make_terms(u):
            c, h = 1 + u // 2, u % 2
            banks = [bank(i, "terms") for i in (FIRST_BANKS[0][0] if u == 0 else B_BANKS[u % 2], A_BANK, D_BANK)]
            for term_bank, (codes, plane) in zip(banks, page_weights(c)):
                for block, v_block, v_scale in zip(blocks(term_bank), blocks(v_codes[h]), blocks(v_planes[h])):
                    nc.tensor.matmul_mx(
                        out=block, lhsT=v_block.bitcast(E4M3), lhsT_scale=v_scale, rhs=codes, rhs_scale=plane, start=True, stop=True,
                    )

            def copy_out(name, term_bank, bufs):
                vals = ring.tile([P, BANK], F32, name=name, bufs=bufs)
                nc.scalar.copy(out=vals[:], in_=term_bank[:])
                return vals

            b_vals = copy_out("b_vals", banks[0], 2)
            a_vals = copy_out("ad_vals", banks[1], 3)
            addends[u] = copy_out("ad_vals", banks[2], 3)
            products[u] = ring.tile([P, BANK], F32, name="ab_vals", bufs=3)
            nc.gpsimd.tensor_tensor(products[u][:], a_vals[:], b_vals[:], MULT)

        def make_states(u):
            c, h = 1 + u // 2, u % 2
            factor = factors[h][:] if c < PACK else dealt_factors[c - PACK][:, h * HALF : (h + 1) * HALF]
            h_bank = bank(H_BANKS[u % 2], "h_bank")
            add_transposed(blocks(h_bank), blocks(addends[u]), blocks(products[u]))
            if u == STEPS - 1:
                plain = shared.tile([P, BANK], F32, name="last_h_vals", offset=PICKED_AT - KIB // 2)
            elif u % 2 == 0:
                plain = shared.tile([P, BANK], F32, name="h_vals%d" % u, offset=pick_home(u // 2))
            else:
                plain = shared.tile([P, BANK], F32, name="h_vals%d" % u, offset=deal_home(u))
            nc.scalar.copy(out=plain[:], in_=h_bank[:])
            states[u] = shared.tile([P, HALF], F32, name="states%d" % u, offset=STATES_AT + 2 * KIB * (u % STATE_SLOTS))
            nc.gpsimd.tensor_tensor(states[u][:], plain[:], factor, MULT)

        def scatter(u):
            nc.vector.tensor_copy(pages[(1 + u // 2) % 2][:].indirect(entries(list2, (u % 2) * HALF, HALF)), states[u][:])

        z_rows = shared.tile([P, QUARTERS, 2, P, 2], BF16, name="z_rows", offset=Z_ROWS_AT)
        picks = {}

        def pick(c):
            picks[c] = shared.tile([P, M], F32, name="picked%d" % c, offset=pick_home(c))
            nc.vector.tensor_copy(picks[c][:], pages[c % 2][:].indirect(list3[:]))

        def place(c, bank_index):
            z_bank = bank(bank_index, "z_bank")
            add_transposed(blocks(z_bank), blocks(plain_contexts[:, c, :]), blocks(picks[c]))
            words = P // PACK
            nc.scalar.copy(
                out=z_rows[:, :, :, words * c : words * (c + 1), :],
                in_=z_bank[:].rearrange("m (b p u e) -> m b u p e", b=QUARTERS, u=2, e=2),
            )

        z0_grouped = keep.tile([P, 2, 2 * P * PACK], BF16, name="z_grouped0", align_bytes=64)

        def turn_first_pass(mh, bank_index):
            z_words = blocks(z_rows[:].rearrange("m b u p e -> m (b u p e)").bitcast(F32))
            word_bank = bank(bank_index, "word_bank")
            for turned, block in zip(blocks(word_bank), z_words[4 * mh : 4 * mh + 4]):
                nc.tensor.transpose(turned, block, identity[:])
            nc.scalar.copy(
                out=z0_grouped[:, mh, :].bitcast(F32).rearrange("p (b m u) -> p b m u", b=2, u=2),
                in_=word_bank[:].rearrange("p (b u m) -> p b m u", b=2, u=2),
            )

        w4_grouped = {}

        def round_w4(g):
            w4_grouped[g] = shared.tile([P, PACK, P, PACK], BF16, name="w4_grouped%d" % g, align_bytes=64, offset=(PICKS_AT + 4 * KIB, Z_ROWS_AT)[g])
            nc.scalar.copy(
                out=w4_grouped[g][:].rearrange("p t q i -> p q t i"),
                in_=w4_raw[g][:].rearrange("p i (q t) -> p q t i", t=PACK),
            )

        def deal(dealt, plain):
            nc.gpsimd.tensor_copy(out=dealt.rearrange("p (t q) -> p t q", t=PACK), in_=plain.rearrange("p (q t) -> p t q", t=PACK))

        def deal_pairs(dealt, plain):
            nc.gpsimd.tensor_copy(
                out=dealt.rearrange("p (t q b) -> p t q b", t=PACK, b=2), in_=plain.rearrange("p (q t b) -> p t q b", t=PACK, b=2),
            )

        def dealt_tile(key, shape, dtype, u):
            dealt[key] = shared.tile(shape, dtype, name="dealt%d" % u, align_bytes=64, offset=deal_home(u))
            return dealt[key]

        def deal_words(dealt, plain, run):
            nc.scalar.copy(
                out=dealt.rearrange("p (t b i) -> p b t i", t=PACK, i=run), in_=plain.rearrange("p (b i t) -> p b t i", t=PACK, i=run),
            )

        def deal_after(u):
            if u == 1:
                deal_words(dealt_tile("w2", [P, H], U8, u)[:].bitcast(U16), w2_codes[1][:].bitcast(U16), 8)
            elif u in (5, 11):
                g = u // 11
                deal_words(dealt_tile(("w6", g), [P, N], U32, u)[:], w6_raw[:, g, :].bitcast(U32), 4)
            elif u > 5:
                g = (u - 7) // 2
                deal_words(dealt_tile(("w5", g), [P, 2 * N], U8, u)[:].bitcast(U16), w5_raw[:, g, :], 8)
                dealt["plane", g] = shared.tile([P, N], U8, name="dealt_plane%d" % g, align_bytes=64, offset=deal_home(u) + KIB)
                deal(dealt["plane", g][:], w56_raw_plane[:, g, :])

        def add_context(t):
            nc.gpsimd.tensor_tensor(
                picked[:, :, t, :], picks[PACK + t][:].rearrange("p (q m) -> p q m", q=QUARTERS),
                dealt_contexts[:, t, :].rearrange("p (q m) -> p q m", q=QUARTERS), ADD,
            )

        first_terms(0)
        first_b(0)
        first_product(0)
        first_state(0)
        first_weigh(0)
        first_terms(1)
        first_b(1)
        first_product(1)
        first_state(1)
        first_scatter(0)
        middle = {}
        for i, at in ((1, FIRST_AT + 8 * S), (0, FIRST_AT + 4 * HALF)):
            middle[i] = shared.tile([P, 2 * P, PACK], BF16, name="middle%d" % i, align_bytes=64, offset=at)
        gpsimd_round(middle[1][:], raw["w3", 2][:].rearrange("p t c -> p c t"))
        make_terms(0)
        interleave(nc.scalar.copy, middle[0][:], raw["w1", 2][:])
        for i, name in enumerate(("w1", "w3")):
            home = RAW_AT + 10 * KIB + KIB * i
            codes, plane = quantize(name + "_2", middle[i][:].rearrange("p r t -> p (r t)"), 2 * P, home)
            for c in range(2):
                w13[name, 2 + c] = (codes[:, c * P : (c + 1) * P].bitcast(E4M3), plane[:, c * P : (c + 1) * P])
        first_weigh(1, RAW_AT + 8 * KIB)
        first_scatter(1)
        dealt_contexts = shared.tile([P, PACK, M], F32, name="dealt_contexts", offset=CONTEXTS_AT)
        nc.sync.dma_start(out=dealt_contexts[:], in_=ctx[PASS_ROWS:H].rearrange("(p t) m -> p t m", t=PACK))
        make_terms(1)
        make_states(0)
        for u in range(STEPS):
            if u + 2 < STEPS:
                make_terms(u + 2)
            if u + 1 < STEPS:
                make_states(u + 1)
            if u < 4:
                round_w13(PACK + 2 * (u // 2), u % 2, nc.scalar.copy)
                if u % 2 == 1:
                    quantize_w13(PACK + 2 * (u // 2))
            if u % 2 == 0 and u + 2 < STEPS:
                deal_after(u + 1)
            if u % 2 == 0 and 2 <= u < 10:
                place(u // 2 - 1, H_BANKS[(u + 1) % 2])
            if u in (9, 10):
                turn_first_pass(u - 9, H_BANKS[(u + 1) % 2])
            if u in (9, 11):
                round_w4((u - 9) // 2)
            if u < STEPS - 1:
                scatter(u)
            if u % 2 == 0:
                pick(u // 2)
            if u == STEPS - 1:
                z0_codes = shared.tile([P, M], U32, name="z0_codes", align_bytes=64, offset=Z0_AT)
                z0_plane = keep.tile([P, M], U8, name="z0_plane", align_bytes=64)
                nc.vector.quantize_mx(
                    out=z0_codes[:].bitcast(E4M3), scales=z0_plane[:], in_=z0_grouped[:].rearrange("p h c -> p (h c)"),
                )
                scatter(u)
            if u == STEPS - 2:
                picked = shared.tile([P, QUARTERS, PACK, P], F32, name="z_vals", offset=PICKED_AT)
                for t in range(PACK - 1):
                    add_context(t)

        def pick_add(t, q):
            nc.vector.tensor_tensor(
                picked[:, q, t, :], pages[1][:].indirect(entries(list3, q * P, P)),
                dealt_contexts[:, t, q * P : (q + 1) * P], ADD,
            )

        z1 = {}
        w4_codes = {}
        w4_plane = keep.tile([P, 2, N], U8, name="w4_plane", align_bytes=64)

        def quantize_w4(g):
            w4_codes[g] = shared.tile([P, N], U32, name="w4_codes%d" % g, align_bytes=64, offset=GROUPED_AT + KIB * (9 + 4 * g) // 2)
            nc.vector.quantize_mx(
                out=w4_codes[g][:].bitcast(E4M3), scales=w4_plane[:, g, :],
                in_=w4_grouped[g][:].rearrange("p t q i -> p (t q i)"),
            )

        for q in range(QUARTERS):
            pick_add(PACK - 1, q)
        for q in range(QUARTERS):
            grouped = shared.tile([P, P, PACK], BF16, name="z_grouped1%d" % q, align_bytes=64, offset=GROUPED_AT + KIB * (0, 6, 1, 2)[q])
            interleave(nc.scalar.copy, grouped[:], picked[:, q])
            z1[q] = quantize("z1%d" % q, grouped[:].rearrange("p m t -> p (m t)"), P)
            if q == 1:
                for g in range(2):
                    quantize_w4(g)

        def stationary(name, g, t):
            cols = slice(t * P, (t + 1) * P)
            if name == "gate":
                return dealt["w5", g][:, 2 * t * P : 2 * (t + 1) * P].bitcast(E2M1), dealt["plane", g][:, cols]
            if name == "more":
                return dealt["w6", g][:, cols].bitcast(E4M3), dealt["plane", g][4:P, cols]
            return w4_codes[g][:, cols].bitcast(E4M3), w4_plane[:, g, cols]

        names = ("gate", "more", "base")
        sums = {}

        def multiply(q, name, g):
            if g == 0:
                sums[q, name] = bank(SUM_BANKS[2 * q + (name == "more")], "y_sum")
                z_codes, z_plane = z0_codes[:, q * P : (q + 1) * P], z0_plane[:, q * P : (q + 1) * P]
            else:
                z_codes, z_plane = z1[q][0][:], z1[q][1][:]
            for t, block in enumerate(blocks(sums[q, name])):
                codes, plane = stationary(name, g, t)
                nc.tensor.matmul_mx(
                    out=block, lhsT=codes, lhsT_scale=plane, rhs=z_codes.bitcast(E4M3), rhs_scale=z_plane,
                    start=(g == 0 and t == 0), stop=(g == 1 and t == PACK - 1),
                )

        y_codes = keep.tile([P, M], U32, name="y_codes", align_bytes=64)
        y_plane = keep.tile([P, M], U8, name="y_plane", align_bytes=64)
        out_rows = out_0.rearrange("(p t) m -> p t m", t=PACK)
        out_words = out_1[0].rearrange("p m t -> p (m t)").bitcast(I32)

        def finish(q):
            cols = slice(q * P, (q + 1) * P)
            opened = shared.tile([P, BANK], F32, name="opened%d" % q, offset=FIRST_AT + 2 * KIB * (q % 2))
            nc.scalar.activation(opened[:], sums[q, "gate"][:], TANH, scale=0.5)
            for g in range(2):
                multiply(q, "base", g)
            gated = shared.tile([P, BANK], F32, name="gated%d" % q, offset=FIRST_AT + 2 * KIB * (2 + q % 2))
            nc.vector.scalar_tensor_tensor(gated[:], opened[:], 1.0, sums[q, "more"][:], ADD, MULT)
            y_vals = shared.tile([P, PACK, P], F32, name="y_vals%d" % q, offset=FIRST_AT + 2 * KIB * (4 + q))
            nc.vector.scalar_tensor_tensor(y_vals[:].rearrange("p t m -> p (t m)"), gated[:], 0.5, sums[q, "base"][:], MULT, ADD)
            nc.sync.dma_start(out=out_rows[:, :, cols], in_=y_vals[:])
            y_grouped = shared.tile([P, P, PACK], BF16, name="y_grouped%d" % q, align_bytes=64, offset=GROUPED_AT + KIB * (10 + q))
            interleave(nc.scalar.copy if q < QUARTERS - 1 else nc.vector.tensor_copy, y_grouped[:], y_vals[:])
            nc.vector.quantize_mx(
                out=y_codes[:, cols].bitcast(E4M3), scales=y_plane[:, cols],
                in_=y_grouped[:].rearrange("p m t -> p (m t)"),
            )
            nc.sync.dma_start(out=out_words[:, cols], in_=y_codes[:, cols].bitcast(I32))

        for q in range(QUARTERS):
            for name in names[:2]:
                multiply(q, name, 0)
        for q in range(QUARTERS):
            for name in names[:2]:
                multiply(q, name, 1)
            finish(q)
        for quad in range(P // QUADRANT):
            (nc.sync if quad % 2 == 0 else nc.scalar).dma_start(
                out=out_2[0, 4 * quad : 4 * quad + 4, :].bitcast(I32),
                in_=y_plane[QUADRANT * quad : QUADRANT * quad + 4, :].bitcast(I32),
            )
